import numpy as np
import ml_dtypes


def mxq(x, axis, fmt="e4m3"):
    dtype, down = {"e4m3": (ml_dtypes.float8_e4m3fn, 7), "e5m2": (ml_dtypes.float8_e5m2, 14)}[fmt]
    v = np.moveaxis(np.asarray(x, np.float32).astype(ml_dtypes.bfloat16).astype(np.float64), axis, -1)
    blocks = v.reshape(v.shape[:-1] + (-1, 32))
    amax = np.abs(blocks).max(-1, keepdims=True)
    byte = np.maximum(np.where(amax > 0, np.frexp(amax)[1] - 1 + 127, 0) - down, 1)
    scale = np.exp2(byte - 127.0)
    codes = (blocks / scale).astype(np.float32).astype(dtype).astype(np.float64)
    return np.moveaxis((codes * scale).reshape(v.shape), -1, axis)


WIDE = False


def mx_kscale(k):
    if not WIDE:
        return np.ones(k)
    levels = np.array([10, -10, 5, -5, 0])
    if k % 512:
        return np.exp2(np.random.permutation(np.resize(levels, k // 32))).repeat(32)
    a = np.empty((k // 512, 16))
    for p in range(k // 512):
        a[p, :8] = np.random.permutation(np.resize(levels, 8))
        for g in range(8):
            far = levels[np.abs(levels - a[p, g]) >= 10]
            a[p, g + 8] = far[np.random.randint(len(far))]
    return np.exp2(a.ravel()).repeat(32)


def f64(x):
    return np.asarray(x).astype(np.float64)


def striped(idx):
    return np.tile(idx.reshape(-1, 16).T, (8, 1)).astype(np.uint16)


def unstriped(offs):
    return offs[:16].T.reshape(-1).astype(np.int64)


E2M1 = np.array([0.0, 0.5, 1.0, 1.5, 2.0, 3.0, 4.0, 6.0, -0.0, -0.5, -1.0, -1.5, -2.0, -3.0, -4.0, -6.0])


def pack_weight(w, fmt):
    k, n = w.shape
    w = f64(np.asarray(w, np.float32).astype(ml_dtypes.bfloat16)).reshape(k // 32, 32, n)
    amax = np.abs(w).max(1)
    if fmt == "e4m3":
        byte = np.frexp(amax)[1] - 1 + 127 - 7
    else:
        mant, ex = np.frexp(amax / 6.0)
        byte = np.where(mant > 0.5, ex, ex - 1) + 127
    byte = np.clip(np.where(amax > 0, byte, 1), 1, 254)
    scaled = (w * np.exp2(127.0 - byte)[:, None, :]).reshape(k, n).astype(np.float32)
    by_word = np.ascontiguousarray(scaled.reshape(k // 512, 128, 4, n).transpose(0, 1, 3, 2))
    if fmt == "e4m3":
        words = by_word.astype(ml_dtypes.float8_e4m3fn).view(np.uint8)
    else:
        c = by_word.astype(ml_dtypes.float4_e2m1fn).view(np.uint8) & 0xF
        words = (c[..., 0::2] | (c[..., 1::2] << 4)).reshape(k // 512, 128, 2 * n)
    return np.ascontiguousarray(words), np.ascontiguousarray(byte.astype(np.uint8).reshape(k // 512, 16, n))


def unpack_weight(words, scales, fmt):
    g, _, n = scales.shape
    words = np.ascontiguousarray(words).reshape(g, 128, n, -1)
    if fmt == "e4m3":
        vals = words.view(ml_dtypes.float8_e4m3fn).astype(np.float64)
    else:
        nib = np.empty((g, 128, n, 4), np.uint8)
        nib[..., 0::2] = words & 0xF
        nib[..., 1::2] = words >> 4
        vals = E2M1[nib]
    vals = vals * np.repeat(np.exp2(scales.astype(np.float64) - 127.0), 8, axis=1)[..., None]
    return vals.transpose(0, 1, 3, 2).reshape(g * 512, n)


def gelu(v):
    return 0.5 * v * (1.0 + np.tanh(np.sqrt(2.0 / np.pi) * (v + 0.044715 * v**3)))


K, T, S, H, T2, N = 1024, 2048, 1024, 512, 2048, 512

def setup_inputs():
    n = np.random.standard_normal
    s = mx_kscale(K)[:, None]
    u = mx_kscale(H)[:, None]
    tab_words, tab_scales = pack_weight(n((K, T)) * s, "e4m3")
    wb_words, wb_scales = pack_weight(n((K, H)) / np.sqrt(K) / s, "e2m1")
    return {
        "tab_words": tab_words, "tab_scales": tab_scales,
        "offs": striped(np.random.permutation(T)[:S]),
        "wa": (n((K, H)) / np.sqrt(K) / s * u.T).astype(np.float32),
        "wb_words": wb_words, "wb_scales": wb_scales,
        "wgs": np.exp(0.3 * n((128, S))).astype(np.float32),
        "offs2": striped(np.random.permutation(T2)[:S]),
        "hold": (n((H, T2)) * u).astype(np.float32),
        "wr": (n((H, N)) / np.sqrt(H) / u).astype(np.float32),
    }

def reference(tab_words, tab_scales, offs, wa, wb_words, wb_scales, wgs, offs2, hold, wr):
    v = unpack_weight(tab_words, tab_scales, "e4m3")[:, unstriped(offs)]
    wb = unpack_weight(wb_words, wb_scales, "e2m1")
    a = mxq(f64(wa), 0, "e4m3").T @ v
    b = wb.T @ v
    h = a / (1.0 + np.abs(b))
    page = np.zeros((H, T2))
    page[:, unstriped(offs2)] = np.tile(f64(wgs), (H // 128, 1)) * h
    z = page + f64(hold)
    e = mxq(f64(wr), 0, "e4m3").T @ mxq(z, 0, "e4m3")
    return np.abs(e)

@@ -1,0 +1,305 @@
+from contextlib import ExitStack
+
+import concourse.mybir as mybir
+from concourse.masks import make_identity
+
+K, T, S, H, T2, N = 1024, 2048, 1024, 512, 2048, 512
+FLOPS = 2 * (2 * K * H * S + H * N * T2)
+
+F32 = mybir.dt.float32
+BF16 = mybir.dt.bfloat16
+I32 = mybir.dt.int32
+U32 = mybir.dt.uint32
+U16 = mybir.dt.uint16
+U8 = mybir.dt.uint8
+FP8X4 = mybir.dt.float8_e4m3fn_x4
+FP4X4 = mybir.dt.float4_e2m1fn_x4
+ACT = mybir.ActivationFunctionType
+ALU = mybir.AluOpType
+
+P = 128
+PACK = 4
+PASSES = K // (P * PACK)
+BANK = 512
+HALVES = S // BANK
+CHUNKS = T2 // BANK
+BLOCKS = BANK // P
+QUAD = 32
+RUN = 4
+
+
+def tile_list_damped_trade_exposure_kernel(
+    tc, tab_words, tab_scales, offs, wa, wb_words, wb_scales, wgs, offs2, hold, wr, out
+):
+    nc = tc.nc
+    with ExitStack() as ctx:
+        keep = ctx.enter_context(tc.tile_pool(name="keep", bufs=1))
+        ring = ctx.enter_context(tc.tile_pool(name="ring", bufs=2))
+        psum = ctx.enter_context(tc.psum_pool(name="psum", bufs=1))
+
+        def sb(shape, dtype, name, tag=None):
+            return keep.tile(shape, dtype, name=name, tag=tag or name, align_bytes=64)
+
+        def bank(tag):
+            return psum.tile([P, BANK], F32, name=tag, tag=tag, bufs=4 if tag == "a" else 2)
+
+        def half_cols(h):
+            return slice(h * BANK, (h + 1) * BANK)
+
+        def half_list(lst, h):
+            return lst[:, h * (BANK // 16) : (h + 1) * (BANK // 16)]
+
+        idx = keep.tile([P, S // 16], U16, name="idx")
+        nc.sync.dma_start(idx[:], offs)
+        idx2 = keep.tile([P, S // 16], U16, name="idx2")
+        nc.sync.dma_start(idx2[:], offs2)
+        wb_raw = [sb([P, 2 * H], U8, f"wb_raw{a}") for a in range(PASSES)]
+        for a in range(PASSES):
+            nc.scalar.dma_start(wb_raw[a][:].bitcast(I32), wb_words[a].bitcast(I32))
+
+        warm = sb([P, 2], F32, "warm")
+        nc.gpsimd.memset(warm[:, 0:1], 1.0)
+        nc.scalar.activation(warm[:, 1:2], warm[:, 0:1], ACT.Abs_reciprocal_sqrt)
+
+        def load_scales(src, name):
+            width = src.shape[2]
+            tile = sb([P, PASSES * width], U8, name)
+            nc.vector.memset(tile[:].bitcast(I32), 0)
+            for q in range(4):
+                nc.scalar.dma_start(
+                    tile[QUAD * q : QUAD * q + 4, :].bitcast(I32).rearrange("r (a c) -> r a c", a=PASSES),
+                    src[:, 4 * q : 4 * q + 4, :].bitcast(I32).rearrange("a r c -> r a c"),
+                )
+            return tile
+
+        tab_sc = load_scales(tab_scales, "tab_sc")
+        wb_sc_raw = load_scales(wb_scales, "wb_sc_raw")
+
+        tab_w = [sb([P, T], U32, f"tab_w{a}") for a in range(PASSES)]
+        wa_raw = [sb([P, PACK, H], F32, f"wa_raw{a}") for a in range(PASSES)]
+        for a in range(PASSES):
+            nc.sync.dma_start(tab_w[a][:].bitcast(I32), tab_words[a].rearrange("p t i -> p (t i)").bitcast(I32))
+            rows = wa[a * P * PACK : (a + 1) * P * PACK, :]
+            nc.sync.dma_start(wa_raw[a][:], rows.rearrange("(p j) c -> p j c", j=PACK))
+
+        wgs_rows = wgs.rearrange("(m i c) j -> i m c j", i=PACK, c=RUN)
+
+        def load_weight(i, cols, name):
+            tile = sb([P, cols.stop - cols.start], F32, name)
+            for q in range(4):
+                nc.sync.dma_start(tile[QUAD * q : QUAD * (q + 1), :], wgs_rows[i][:, :, cols])
+            return tile
+
+        hold_rows = hold.rearrange("(m i c) t -> i m c t", i=PACK, c=RUN)
+
+        def load_hold(i):
+            tile = sb([P, T2], F32, f"hold{i}")
+            nc.sync.dma_start(tile[:], hold_rows[i])
+            return tile
+
+        first_weight = [load_weight(0, half_cols(h), f"weight0_{h}") for h in range(HALVES)]
+        weight = [None, load_weight(1, slice(0, S), "weight1")]
+        held = [load_hold(0)]
+        weight.append(load_weight(2, slice(0, S), "weight2"))
+        held.append(load_hold(1))
+        weight.append(load_weight(3, slice(0, S), "weight3"))
+        held.append(load_hold(2))
+        wr_raw = sb([P, PACK, N], F32, "wr_raw")
+        wr_rows = wr.rearrange("(m i c) n -> i m c n", i=PACK, c=RUN)
+        for i in range(PACK):
+            nc.sync.dma_start(wr_raw[:, i, :], wr_rows[i])
+        held.append(load_hold(3))
+
+        page = [sb([P, T2], F32, f"page{i}") for i in range(2)]
+        for i in range(2):
+            nc.vector.memset(page[i][:], 0.0)
+        ident = sb([P, P], F32, "ident")
+        make_identity(nc, ident[:])
+
+        wb_w = [sb([P, 2 * H], U8, f"wb_w{a}") for a in range(PASSES)]
+        for a in range(PASSES):
+            nc.vector.tensor_copy(
+                wb_w[a][:].bitcast(I32).rearrange("p (i m w) -> p i m w", i=PACK, w=2),
+                wb_raw[a][:].bitcast(I32).rearrange("p (m i w) -> p i m w", i=PACK, w=2),
+            )
+
+        v_w = [[sb([P, BANK], U32, f"v_w{a}_{h}") for h in range(HALVES)] for a in range(PASSES)]
+        v_sc = [[sb([P, BANK], U8, f"v_sc{a}_{h}") for h in range(HALVES)] for a in range(PASSES)]
+
+        def gather_words(a, h):
+            nc.vector.tensor_copy(v_w[a][h][:], tab_w[a][:].indirect(half_list(idx, h)))
+
+        def gather_scales(a, h):
+            nc.vector.tensor_copy(v_sc[a][h][:], tab_sc[:, a * T : (a + 1) * T].indirect(half_list(idx, h)))
+
+        for a in range(PASSES):
+            gather_scales(a, 0)
+        gather_words(0, 0)
+        wb_sc = sb([P, PASSES * H], U8, "wb_sc")
+        nc.vector.tensor_copy(
+            wb_sc[:].bitcast(I32).rearrange("p (a i m) -> p a i m", a=PASSES, i=PACK),
+            wb_sc_raw[:].bitcast(I32).rearrange("p (a m i) -> p a i m", a=PASSES, i=PACK),
+        )
+        gather_words(1, 0)
+
+        wa_w = {}
+
+        def prepare_wa(a, lo, hi):
+            n = hi - lo
+            grouped = sb([P, n * P * PACK], BF16, f"wa_g{a}_{lo}")
+            nc.scalar.copy(
+                grouped[:].rearrange("p (i m c j) -> p i m c j", i=n, c=RUN, j=PACK),
+                wa_raw[a][:].rearrange("p j (m i c) -> p i m c j", i=PACK, c=RUN)[:, lo:hi],
+            )
+            codes = sb([P, n * P], U32, f"wa_w{a}_{lo}")
+            scales = sb([P, n * P], U8, f"wa_sc{a}_{lo}")
+            done = 0
+            for width in (4, 2, 1):
+                if n - done >= width:
+                    cols = slice(done * P, (done + width) * P)
+                    nc.vector.quantize_mx(
+                        out=codes[:, cols].bitcast(FP8X4),
+                        scales=scales[:, cols],
+                        in_=grouped[:, cols.start * PACK : cols.stop * PACK],
+                    )
+                    done = done + width
+            for i in range(lo, hi):
+                cols = slice((i - lo) * P, (i - lo + 1) * P)
+                wa_w[a, i] = (codes[:, cols].bitcast(FP8X4), scales[:, cols])
+
+        prepare_wa(0, 0, PACK)
+        prepare_wa(1, 0, 1)
+        for a in range(PASSES):
+            gather_scales(a, 1)
+            gather_words(a, 1)
+
+        damping = [sb([P, S], F32, f"damping{i}") for i in range(PACK)]
+
+        def damp(i, h):
+            acc = bank("x" if h == 0 else "y")
+            for a in range(PASSES):
+                at = (a * PACK + i) * P
+                nc.tensor.matmul_mx(
+                    out=acc[:],
+                    lhsT=wb_w[a][:, 2 * i * P : 2 * (i + 1) * P].bitcast(FP4X4),
+                    lhsT_scale=wb_sc[:, at : at + P],
+                    rhs=v_w[a][h][:].bitcast(FP8X4),
+                    rhs_scale=v_sc[a][h][:],
+                    start=(a == 0),
+                    stop=(a == PASSES - 1),
+                )
+            size = ring.tile([P, BANK], F32, name="size")
+            nc.scalar.activation(size[:], acc[:], ACT.Abs)
+            root = ring.tile([P, BANK], F32, name="root")
+            nc.scalar.activation(root[:], size[:], ACT.Abs_reciprocal_sqrt, bias=1.0)
+            nc.scalar.activation(damping[i][:, half_cols(h)], root[:], ACT.Square)
+
+        def loadings(i, h, dst):
+            acc = bank("a")
+            for a in range(PASSES):
+                codes, scales = wa_w[a, i]
+                nc.tensor.matmul_mx(
+                    out=acc[:],
+                    lhsT=codes,
+                    lhsT_scale=scales,
+                    rhs=v_w[a][h][:].bitcast(FP8X4),
+                    rhs_scale=v_sc[a][h][:],
+                    start=(a == 0),
+                    stop=(a == PASSES - 1),
+                )
+            nc.vector.tensor_tensor(dst, acc[:], damping[i][:, half_cols(h)], ALU.mult)
+
+        for h in range(HALVES):
+            damp(0, h)
+            damped = ring.tile([P, BANK], F32, name="damped_half")
+            loadings(0, h, damped[:])
+            nc.vector.tensor_tensor(page[0][:].indirect(half_list(idx2, h)), damped[:], first_weight[h][:], ALU.mult)
+
+        prepare_wa(1, 1, PACK)
+        page.append(sb([P, T2], F32, "page2", tag="wa_raw1"))
+        nc.gpsimd.memset(page[2][:], 0.0)
+        page.append(sb([P, T2], F32, "page3", tag="weight0_1"))
+        nc.gpsimd.memset(page[3][:], 0.0)
+        for i in range(1, PACK):
+            for h in range(HALVES):
+                damp(i, h)
+
+        turned = [sb([P, BLOCKS, P, 2], BF16, f"turned{c}") for c in range(CHUNKS)]
+        pairs = [sb([P, 2, BANK], F32, f"pairs{c}") for c in range(CHUNKS)]
+
+        def add_turned(i, c):
+            acc = bank("x")
+            for bl in range(BLOCKS):
+                cols = slice(c * BANK + bl * P, c * BANK + (bl + 1) * P)
+                dst = acc[:, bl * P : (bl + 1) * P]
+                nc.tensor.matmul(dst, held[i][:, cols], ident[:], start=True, stop=False, is_transpose=True)
+                nc.tensor.matmul(dst, page[i][:, cols], ident[:], start=False, stop=True, is_transpose=True)
+            nc.scalar.copy(turned[c][:, :, :, i % 2], acc[:].rearrange("t (b p) -> t b p", b=BLOCKS))
+
+        def turn_back(u, c):
+            acc = bank("y")
+            words = turned[c][:].rearrange("t b p e -> t (b p e)").bitcast(F32)
+            for bl in range(BLOCKS):
+                cols = slice(bl * P, (bl + 1) * P)
+                nc.tensor.transpose(acc[:, cols], words[:, cols], ident[:])
+            nc.scalar.copy(pairs[c][:, u, :], acc[:])
+
+        def add_direct(i, c):
+            halves = pairs[c][:, i // 2, :].bitcast(BF16).rearrange("p (t e) -> p t e", e=2)
+            nc.vector.tensor_tensor(halves[:, :, i % 2], page[i][:, half_cols(c)], held[i][:, half_cols(c)], ALU.add)
+
+        def trade(i):
+            damped = ring.tile([P, S], F32, name="damped")
+            for h in range(HALVES):
+                loadings(i, h, damped[:, half_cols(h)])
+            nc.vector.tensor_tensor(page[i][:].indirect(idx2[:]), damped[:], weight[i][:], ALU.mult)
+
+        trade(1)
+        for c in range(CHUNKS):
+            add_turned(0, c)
+        trade(2)
+        for c in range(CHUNKS):
+            add_turned(1, c)
+            turn_back(0, c)
+        wr_g = sb([P, N * PACK], BF16, "wr_g")
+        nc.scalar.copy(
+            wr_g[:].rearrange("p (c i j) -> p c j i", i=4, j=PACK),
+            wr_raw[:].rearrange("p j (c i) -> p c j i", i=4),
+        )
+        wr_w = sb([P, N], U32, "wr_w")
+        wr_sc = sb([P, N], U8, "wr_sc")
+        nc.vector.quantize_mx(out=wr_w[:].bitcast(FP8X4), scales=wr_sc[:], in_=wr_g[:])
+        trade(3)
+        for c in range(CHUNKS):
+            add_turned(2, c)
+            turn_back(1, c)
+
+        out_rows = out.rearrange("(b p) t -> p b t", p=P)
+        stage_tags = ["tab_w0", "tab_w1", "wa_raw0", "hold0"]
+        out_banks = ["a", "a", "a", "a", "x", "x", "y", "y"]
+        for c in range(CHUNKS):
+            add_direct(3, c)
+            z_g = ring.tile([P, BANK, 2], F32, name="z_g", align_bytes=64)
+            nc.vector.tensor_copy(z_g[:], pairs[c][:].rearrange("p u t -> p t u"))
+            z_w = sb([P, BANK], U32, f"z_w{c}")
+            z_sc = sb([P, BANK], U8, f"z_sc{c}")
+            nc.vector.quantize_mx(
+                out=z_w[:].bitcast(FP8X4),
+                scales=z_sc[:],
+                in_=z_g[:].rearrange("p t u -> p (t u)").bitcast(BF16),
+            )
+            result = sb([P, N // P, BANK], F32, f"result{c}", tag=stage_tags[c])
+            for b in range(N // P):
+                acc = bank(out_banks[(c * (N // P) + b) % len(out_banks)])
+                cols = slice(b * P, (b + 1) * P)
+                nc.tensor.matmul_mx(
+                    out=acc[:],
+                    lhsT=wr_w[:, cols].bitcast(FP8X4),
+                    lhsT_scale=wr_sc[:, cols],
+                    rhs=z_w[:].bitcast(FP8X4),
+                    rhs_scale=z_sc[:],
+                    start=True,
+                    stop=True,
+                )
+                nc.scalar.activation(result[:, b, :], acc[:], ACT.Abs)
+                nc.sync.dma_start(out_rows[:, b, half_cols(c)], result[:, b, :])

@@ -26,6 +26,7 @@ CHUNKS = T2 // BANK
 BLOCKS = BANK // P
 QUAD = 32
 RUN = 4
+STRIPS = (128, 128, 256, 512, 512, 512)
 
 
 def tile_list_damped_trade_exposure_kernel(
@@ -51,36 +52,46 @@ def tile_list_damped_trade_exposure_kernel(
 
         idx = keep.tile([P, S // 16], U16, name="idx")
         nc.sync.dma_start(idx[:], offs)
-        idx2 = keep.tile([P, S // 16], U16, name="idx2")
-        nc.sync.dma_start(idx2[:], offs2)
-        wb_raw = [sb([P, 2 * H], U8, f"wb_raw{a}") for a in range(PASSES)]
-        for a in range(PASSES):
-            nc.scalar.dma_start(wb_raw[a][:].bitcast(I32), wb_words[a].bitcast(I32))
-
-        warm = sb([P, 2], F32, "warm")
-        nc.gpsimd.memset(warm[:, 0:1], 1.0)
-        nc.scalar.activation(warm[:, 1:2], warm[:, 0:1], ACT.Abs_reciprocal_sqrt)
 
         def load_scales(src, name):
             width = src.shape[2]
             tile = sb([P, PASSES * width], U8, name)
-            nc.vector.memset(tile[:].bitcast(I32), 0)
+            nc.vector.memset(tile[:, :width].bitcast(I32), 0)
+            nc.gpsimd.memset(tile[:, width:].bitcast(I32), 0)
             for q in range(4):
-                nc.scalar.dma_start(
+                nc.sync.dma_start(
                     tile[QUAD * q : QUAD * q + 4, :].bitcast(I32).rearrange("r (a c) -> r a c", a=PASSES),
                     src[:, 4 * q : 4 * q + 4, :].bitcast(I32).rearrange("a r c -> r a c"),
                 )
             return tile
 
-        tab_sc = load_scales(tab_scales, "tab_sc")
-        wb_sc_raw = load_scales(wb_scales, "wb_sc_raw")
-
         tab_w = [sb([P, T], U32, f"tab_w{a}") for a in range(PASSES)]
         wa_raw = [sb([P, PACK, H], F32, f"wa_raw{a}") for a in range(PASSES)]
-        for a in range(PASSES):
+
+        def load_tab(a):
             nc.sync.dma_start(tab_w[a][:].bitcast(I32), tab_words[a].rearrange("p t i -> p (t i)").bitcast(I32))
+
+        def load_wa(a):
             rows = wa[a * P * PACK : (a + 1) * P * PACK, :]
             nc.sync.dma_start(wa_raw[a][:], rows.rearrange("(p j) c -> p j c", j=PACK))
+
+        tab_sc = load_scales(tab_scales, "tab_sc")
+        idx2 = keep.tile([P, S // 16], U16, name="idx2")
+        nc.sync.dma_start(idx2[:], offs2)
+        wb_raw = sb([P, PASSES * 2 * H], U8, "wb_raw")
+        nc.sync.dma_start(
+            wb_raw[:].bitcast(I32).rearrange("p (a c) -> p a c", a=PASSES),
+            wb_words.bitcast(I32).rearrange("a p c -> p a c"),
+        )
+        load_tab(0)
+        wb_sc_raw = load_scales(wb_scales, "wb_sc_raw")
+        load_wa(0)
+        load_tab(1)
+        load_wa(1)
+
+        warm = sb([P, 2], F32, "warm")
+        nc.gpsimd.memset(warm[:, 0:1], 1.0)
+        nc.scalar.activation(warm[:, 1:2], warm[:, 0:1], ACT.Abs_reciprocal_sqrt)
 
         wgs_rows = wgs.rearrange("(m i c) j -> i m c j", i=PACK, c=RUN)
 
@@ -110,18 +121,11 @@ def tile_list_damped_trade_exposure_kernel(
             nc.sync.dma_start(wr_raw[:, i, :], wr_rows[i])
         held.append(load_hold(3))
 
-        page = [sb([P, T2], F32, f"page{i}") for i in range(2)]
-        for i in range(2):
-            nc.vector.memset(page[i][:], 0.0)
+        page = [sb([P, T2], F32, "page0")]
+        nc.vector.memset(page[0][:], 0.0)
         ident = sb([P, P], F32, "ident")
         make_identity(nc, ident[:])
 
-        wb_w = [sb([P, 2 * H], U8, f"wb_w{a}") for a in range(PASSES)]
-        for a in range(PASSES):
-            nc.vector.tensor_copy(
-                wb_w[a][:].bitcast(I32).rearrange("p (i m w) -> p i m w", i=PACK, w=2),
-                wb_raw[a][:].bitcast(I32).rearrange("p (m i w) -> p i m w", i=PACK, w=2),
-            )
 
         v_w = [[sb([P, BANK], U32, f"v_w{a}_{h}") for h in range(HALVES)] for a in range(PASSES)]
         v_sc = [[sb([P, BANK], U8, f"v_sc{a}_{h}") for h in range(HALVES)] for a in range(PASSES)]
@@ -135,6 +139,11 @@ def tile_list_damped_trade_exposure_kernel(
         for a in range(PASSES):
             gather_scales(a, 0)
         gather_words(0, 0)
+        wb_w = sb([P, PASSES * 2 * H], U8, "wb_w")
+        nc.vector.tensor_copy(
+            wb_w[:].bitcast(I32).rearrange("p (a i m w) -> p a i m w", a=PASSES, i=PACK, w=2),
+            wb_raw[:].bitcast(I32).rearrange("p (a m i w) -> p a i m w", a=PASSES, i=PACK, w=2),
+        )
         wb_sc = sb([P, PASSES * H], U8, "wb_sc")
         nc.vector.tensor_copy(
             wb_sc[:].bitcast(I32).rearrange("p (a i m) -> p a i m", a=PASSES, i=PACK),
@@ -181,7 +190,7 @@ def tile_list_damped_trade_exposure_kernel(
                 at = (a * PACK + i) * P
                 nc.tensor.matmul_mx(
                     out=acc[:],
-                    lhsT=wb_w[a][:, 2 * i * P : 2 * (i + 1) * P].bitcast(FP4X4),
+                    lhsT=wb_w[:, 2 * at : 2 * (at + P)].bitcast(FP4X4),
                     lhsT_scale=wb_sc[:, at : at + P],
                     rhs=v_w[a][h][:].bitcast(FP8X4),
                     rhs_scale=v_sc[a][h][:],
@@ -216,10 +225,9 @@ def tile_list_damped_trade_exposure_kernel(
             nc.vector.tensor_tensor(page[0][:].indirect(half_list(idx2, h)), damped[:], first_weight[h][:], ALU.mult)
 
         prepare_wa(1, 1, PACK)
-        page.append(sb([P, T2], F32, "page2", tag="wa_raw1"))
-        nc.gpsimd.memset(page[2][:], 0.0)
-        page.append(sb([P, T2], F32, "page3", tag="weight0_1"))
-        nc.gpsimd.memset(page[3][:], 0.0)
+        for i, tag in ((1, "weight0_0"), (2, "weight0_1")):
+            page.append(sb([P, T2], F32, f"page{i}", tag=tag))
+            nc.gpsimd.memset(page[i][:], 0.0)
         for i in range(1, PACK):
             for h in range(HALVES):
                 damp(i, h)
@@ -244,10 +252,6 @@ def tile_list_damped_trade_exposure_kernel(
                 nc.tensor.transpose(acc[:, cols], words[:, cols], ident[:])
             nc.scalar.copy(pairs[c][:, u, :], acc[:])
 
-        def add_direct(i, c):
-            halves = pairs[c][:, i // 2, :].bitcast(BF16).rearrange("p (t e) -> p t e", e=2)
-            nc.vector.tensor_tensor(halves[:, :, i % 2], page[i][:, half_cols(c)], held[i][:, half_cols(c)], ALU.add)
-
         def trade(i):
             damped = ring.tile([P, S], F32, name="damped")
             for h in range(HALVES):
@@ -255,6 +259,8 @@ def tile_list_damped_trade_exposure_kernel(
             nc.vector.tensor_tensor(page[i][:].indirect(idx2[:]), damped[:], weight[i][:], ALU.mult)
 
         trade(1)
+        page.append(sb([P, T2], F32, "page3", tag="weight1"))
+        nc.gpsimd.memset(page[3][:], 0.0)
         for c in range(CHUNKS):
             add_turned(0, c)
         trade(2)
@@ -274,32 +280,52 @@ def tile_list_damped_trade_exposure_kernel(
             add_turned(2, c)
             turn_back(1, c)
 
+        last = PACK - 1
         out_rows = out.rearrange("(b p) t -> p b t", p=P)
         stage_tags = ["tab_w0", "tab_w1", "wa_raw0", "hold0"]
         out_banks = ["a", "a", "a", "a", "x", "x", "y", "y"]
-        for c in range(CHUNKS):
-            add_direct(3, c)
-            z_g = ring.tile([P, BANK, 2], F32, name="z_g", align_bytes=64)
-            nc.vector.tensor_copy(z_g[:], pairs[c][:].rearrange("p u t -> p t u"))
-            z_w = sb([P, BANK], U32, f"z_w{c}")
-            z_sc = sb([P, BANK], U8, f"z_sc{c}")
+        results = [sb([P, N // P * BANK], F32, f"result{c}", tag=stage_tags[c]) for c in range(CHUNKS)]
+        banks_used = 0
+        start = 0
+        for width in STRIPS:
+            c, at = divmod(start, BANK)
+            cols = slice(start, start + width)
+            words = pairs[c][:, :, at : at + width]
+            halves = words[:, last // 2, :].bitcast(BF16).rearrange("p (t e) -> p t e", e=2)
+            nc.vector.tensor_tensor(halves[:, :, last % 2], page[last][:, cols], held[last][:, cols], ALU.add)
+            z_g = ring.tile([P, width, 2], F32, name="z_g", align_bytes=64)
+            nc.vector.tensor_copy(z_g[:], words.rearrange("p u t -> p t u"))
+            z_w = sb([P, width], U32, f"z_w{start}")
+            z_sc = sb([P, width], U8, f"z_sc{start}")
             nc.vector.quantize_mx(
                 out=z_w[:].bitcast(FP8X4),
                 scales=z_sc[:],
                 in_=z_g[:].rearrange("p t u -> p (t u)").bitcast(BF16),
             )
-            result = sb([P, N // P, BANK], F32, f"result{c}", tag=stage_tags[c])
-            for b in range(N // P):
-                acc = bank(out_banks[(c * (N // P) + b) % len(out_banks)])
-                cols = slice(b * P, (b + 1) * P)
-                nc.tensor.matmul_mx(
-                    out=acc[:],
-                    lhsT=wr_w[:, cols].bitcast(FP8X4),
-                    lhsT_scale=wr_sc[:, cols],
-                    rhs=z_w[:].bitcast(FP8X4),
-                    rhs_scale=z_sc[:],
-                    start=True,
-                    stop=True,
+            per_bank = BANK // width
+            for first in range(0, N // P, per_bank):
+                acc = bank(out_banks[banks_used % len(out_banks)])
+                for b in range(first, first + per_bank):
+                    rows = slice(b * P, (b + 1) * P)
+                    nc.tensor.matmul_mx(
+                        out=acc[:, (b - first) * width : (b - first + 1) * width],
+                        lhsT=wr_w[:, rows].bitcast(FP8X4),
+                        lhsT_scale=wr_sc[:, rows],
+                        rhs=z_w[:].bitcast(FP8X4),
+                        rhs_scale=z_sc[:],
+                        start=True,
+                        stop=True,
+                    )
+                slot = banks_used % (N // P)
+                result = results[c][:, slot * BANK : (slot + 1) * BANK]
+                banks_used = banks_used + 1
+                if banks_used == CHUNKS * N // P:
+                    negated = ring.tile([P, BANK], F32, name="negated")
+                    nc.vector.tensor_scalar(negated[:], acc[:], -1.0, None, ALU.mult)
+                    nc.vector.tensor_tensor(result, acc[:], negated[:], ALU.max)
+                else:
+                    nc.scalar.activation(result, acc[:], ACT.Abs)
+                nc.sync.dma_start(
+                    out_rows[:, first : first + per_bank, cols], result.rearrange("p (b t) -> p b t", b=per_bank)
                 )
-                nc.scalar.activation(result[:, b, :], acc[:], ACT.Abs)
-                nc.sync.dma_start(out_rows[:, b, half_cols(c)], result[:, b, :])
+            start = start + width

@@ -58,11 +58,9 @@ def tile_list_damped_trade_exposure_kernel(
             tile = sb([P, PASSES * width], U8, name)
             nc.vector.memset(tile[:, :width].bitcast(I32), 0)
             nc.gpsimd.memset(tile[:, width:].bitcast(I32), 0)
-            for q in range(4):
-                nc.sync.dma_start(
-                    tile[QUAD * q : QUAD * q + 4, :].bitcast(I32).rearrange("r (a c) -> r a c", a=PASSES),
-                    src[:, 4 * q : 4 * q + 4, :].bitcast(I32).rearrange("a r c -> r a c"),
-                )
+            rows = src.bitcast(I32).rearrange("a (q r) c -> r q a c", r=4)
+            for r in range(4):
+                nc.sync.dma_start(tile[r:P:QUAD, :].bitcast(I32).rearrange("q (a c) -> q a c", a=PASSES), rows[r])
             return tile
 
         tab_w = [sb([P, T], U32, f"tab_w{a}") for a in range(PASSES)]
@@ -84,8 +82,8 @@ def tile_list_damped_trade_exposure_kernel(
             wb_words.bitcast(I32).rearrange("a p c -> p a c"),
         )
         load_tab(0)
-        wb_sc_raw = load_scales(wb_scales, "wb_sc_raw")
         load_wa(0)
+        wb_sc_raw = load_scales(wb_scales, "wb_sc_raw")
         load_tab(1)
         load_wa(1)
 
@@ -157,8 +155,8 @@ def tile_list_damped_trade_exposure_kernel(
             n = hi - lo
             grouped = sb([P, n * P * PACK], BF16, f"wa_g{a}_{lo}")
             nc.scalar.copy(
-                grouped[:].rearrange("p (i m c j) -> p i m c j", i=n, c=RUN, j=PACK),
-                wa_raw[a][:].rearrange("p j (m i c) -> p i m c j", i=PACK, c=RUN)[:, lo:hi],
+                grouped[:].rearrange("p (i m c j) -> p i m j c", i=n, c=RUN, j=PACK),
+                wa_raw[a][:].rearrange("p j (m i c) -> p i m j c", i=PACK, c=RUN)[:, lo:hi],
             )
             codes = sb([P, n * P], U32, f"wa_w{a}_{lo}")
             scales = sb([P, n * P], U8, f"wa_sc{a}_{lo}")

@@ -26,6 +26,7 @@ CHUNKS = T2 // BANK
 BLOCKS = BANK // P
 QUAD = 32
 RUN = 4
+GROUP = PACK * RUN
 STRIPS = (128, 128, 256, 512, 512, 512)
 
 
@@ -42,7 +43,7 @@ def tile_list_damped_trade_exposure_kernel(
             return keep.tile(shape, dtype, name=name, tag=tag or name, align_bytes=64)
 
         def bank(tag):
-            return psum.tile([P, BANK], F32, name=tag, tag=tag, bufs=4 if tag == "a" else 2)
+            return psum.tile([P, BANK], F32, name=tag, tag=tag, bufs=4 if tag == "s" else 2)
 
         def half_cols(h):
             return slice(h * BANK, (h + 1) * BANK)
@@ -63,246 +64,335 @@ def tile_list_damped_trade_exposure_kernel(
                 nc.sync.dma_start(tile[r:P:QUAD, :].bitcast(I32).rearrange("q (a c) -> q a c", a=PASSES), rows[r])
             return tile
 
-        tab_w = [sb([P, T], U32, f"tab_w{a}") for a in range(PASSES)]
-        wa_raw = [sb([P, PACK, H], F32, f"wa_raw{a}") for a in range(PASSES)]
-
         def load_tab(a):
-            nc.sync.dma_start(tab_w[a][:].bitcast(I32), tab_words[a].rearrange("p t i -> p (t i)").bitcast(I32))
+            tile = sb([P, T], U32, f"tab_w{a}")
+            nc.sync.dma_start(tile[:].bitcast(I32), tab_words[a].rearrange("p t i -> p (t i)").bitcast(I32))
+            return tile
 
-        def load_wa(a):
-            rows = wa[a * P * PACK : (a + 1) * P * PACK, :]
-            nc.sync.dma_start(wa_raw[a][:], rows.rearrange("(p j) c -> p j c", j=PACK))
+        def load_wa(a, s):
+            tile = sb([P, PACK, H // 2], F32, f"wa_raw{a}_{s}")
+            rows = wa[a * P * PACK : (a + 1) * P * PACK, s * H // 2 : (s + 1) * H // 2]
+            nc.sync.dma_start(tile[:], rows.rearrange("(p j) c -> p j c", j=PACK))
+            return tile
 
+        def load_pair_weight(h):
+            tile = sb([P, BANK], F32, f"pair_weight{h}")
+            rows = wgs.rearrange("(m x) j -> m x j", x=GROUP)[:, : 2 * RUN, half_cols(h)]
+            for rep in range(2):
+                nc.sync.dma_start(tile[rep * P // 2 : (rep + 1) * P // 2, :], rows)
+            return tile
+
+        def load_weight(i):
+            tile = sb([P, S], F32, f"weight{i}")
+            rows = wgs.rearrange("(m i c) j -> i m c j", i=PACK, c=RUN)[i]
+            for q in range(4):
+                nc.sync.dma_start(tile[QUAD * q : QUAD * (q + 1), :], rows)
+            return tile
+
+        def load_hold(i):
+            tile = sb([P, T2], F32, f"hold{i}")
+            if i < 2:
+                rows = hold.rearrange("(s m x) t -> s m x t", s=2, x=GROUP)[i][:, : 2 * RUN, :]
+            else:
+                rows = hold.rearrange("(m i c) t -> i m c t", i=PACK, c=RUN)[i]
+            nc.sync.dma_start(tile[:], rows)
+            return tile
+
+        tab_w = [load_tab(0)]
         tab_sc = load_scales(tab_scales, "tab_sc")
-        idx2 = keep.tile([P, S // 16], U16, name="idx2")
-        nc.sync.dma_start(idx2[:], offs2)
+        wa_raw = {(0, 0): load_wa(0, 0)}
+        tab_w.append(load_tab(1))
         wb_raw = sb([P, PASSES * 2 * H], U8, "wb_raw")
         nc.sync.dma_start(
             wb_raw[:].bitcast(I32).rearrange("p (a c) -> p a c", a=PASSES),
             wb_words.bitcast(I32).rearrange("a p c -> p a c"),
         )
-        load_tab(0)
-        load_wa(0)
         wb_sc_raw = load_scales(wb_scales, "wb_sc_raw")
-        load_tab(1)
-        load_wa(1)
-
-        warm = sb([P, 2], F32, "warm")
-        nc.gpsimd.memset(warm[:, 0:1], 1.0)
-        nc.scalar.activation(warm[:, 1:2], warm[:, 0:1], ACT.Abs_reciprocal_sqrt)
-
-        wgs_rows = wgs.rearrange("(m i c) j -> i m c j", i=PACK, c=RUN)
-
-        def load_weight(i, cols, name):
-            tile = sb([P, cols.stop - cols.start], F32, name)
-            for q in range(4):
-                nc.sync.dma_start(tile[QUAD * q : QUAD * (q + 1), :], wgs_rows[i][:, :, cols])
-            return tile
-
-        hold_rows = hold.rearrange("(m i c) t -> i m c t", i=PACK, c=RUN)
-
-        def load_hold(i):
-            tile = sb([P, T2], F32, f"hold{i}")
-            nc.sync.dma_start(tile[:], hold_rows[i])
-            return tile
-
-        first_weight = [load_weight(0, half_cols(h), f"weight0_{h}") for h in range(HALVES)]
-        weight = [None, load_weight(1, slice(0, S), "weight1")]
+        wa_raw[1, 0] = load_wa(1, 0)
+        idx2 = keep.tile([P, S // 16], U16, name="idx2")
+        nc.sync.dma_start(idx2[:], offs2)
+        pair_weight = [load_pair_weight(h) for h in range(HALVES)]
+        for a in range(PASSES):
+            wa_raw[a, 1] = load_wa(a, 1)
         held = [load_hold(0)]
-        weight.append(load_weight(2, slice(0, S), "weight2"))
+        weight = {2: load_weight(2)}
         held.append(load_hold(1))
-        weight.append(load_weight(3, slice(0, S), "weight3"))
-        held.append(load_hold(2))
         wr_raw = sb([P, PACK, N], F32, "wr_raw")
         wr_rows = wr.rearrange("(m i c) n -> i m c n", i=PACK, c=RUN)
         for i in range(PACK):
             nc.sync.dma_start(wr_raw[:, i, :], wr_rows[i])
+        weight[3] = load_weight(3)
+        held.append(load_hold(2))
         held.append(load_hold(3))
 
-        page = [sb([P, T2], F32, "page0")]
-        nc.vector.memset(page[0][:], 0.0)
+        warm = sb([P, 2], F32, "warm")
+        nc.gpsimd.memset(warm[:, 0:1], 1.0)
+        nc.scalar.activation(warm[:, 1:2], warm[:, 0:1], ACT.Abs_reciprocal_sqrt)
         ident = sb([P, P], F32, "ident")
         make_identity(nc, ident[:])
 
+        page = [sb([P, T2], F32, f"page{n}") for n in range(2)]
+        for tile in page:
+            nc.vector.memset(tile[:].bitcast(I32), 0)
 
-        v_w = [[sb([P, BANK], U32, f"v_w{a}_{h}") for h in range(HALVES)] for a in range(PASSES)]
-        v_sc = [[sb([P, BANK], U8, f"v_sc{a}_{h}") for h in range(HALVES)] for a in range(PASSES)]
+        v_w, v_sc = {}, {}
 
-        def gather_words(a, h):
-            nc.vector.tensor_copy(v_w[a][h][:], tab_w[a][:].indirect(half_list(idx, h)))
+        def gather_words(a, h, tag=None):
+            v_w[a, h] = sb([P, BANK], U32, f"v_w{a}_{h}", tag)
+            nc.vector.tensor_copy(v_w[a, h][:], tab_w[a][:].indirect(half_list(idx, h)))
 
-        def gather_scales(a, h):
-            nc.vector.tensor_copy(v_sc[a][h][:], tab_sc[:, a * T : (a + 1) * T].indirect(half_list(idx, h)))
+        def gather_scales(h, tag=None):
+            tile = sb([P, PASSES * BANK], U8, f"v_sc{h}", tag)
+            for a in range(PASSES):
+                v_sc[a, h] = tile[:, a * BANK : (a + 1) * BANK]
+                nc.vector.tensor_copy(v_sc[a, h], tab_sc[:, a * T : (a + 1) * T].indirect(half_list(idx, h)))
 
-        for a in range(PASSES):
-            gather_scales(a, 0)
+        def deal(raw, name, words):
+            tile = sb([P, raw.shape[1]], U8, name)
+            src = raw[:].bitcast(U32).rearrange("p (a m w) -> p a m w", a=PASSES, w=PACK * words)
+            dst = tile[:].bitcast(U32).rearrange("p (a e x) -> p a e x", a=PASSES, e=2)
+            nc.scalar.copy(dst[:, :, 0, :].rearrange("p a (m w) -> p a m w", w=2 * words), src[:, :, :, : 2 * words])
+            nc.scalar.copy(
+                dst[:, :, 1, :].rearrange("p a (i m w) -> p a i m w", i=2, w=words),
+                src[:, :, :, 2 * words :].rearrange("p a m (i w) -> p a i m w", i=2),
+            )
+            return tile
+
         gather_words(0, 0)
-        wb_w = sb([P, PASSES * 2 * H], U8, "wb_w")
-        nc.vector.tensor_copy(
-            wb_w[:].bitcast(I32).rearrange("p (a i m w) -> p a i m w", a=PASSES, i=PACK, w=2),
-            wb_raw[:].bitcast(I32).rearrange("p (a m i w) -> p a i m w", a=PASSES, i=PACK, w=2),
-        )
-        wb_sc = sb([P, PASSES * H], U8, "wb_sc")
-        nc.vector.tensor_copy(
-            wb_sc[:].bitcast(I32).rearrange("p (a i m) -> p a i m", a=PASSES, i=PACK),
-            wb_sc_raw[:].bitcast(I32).rearrange("p (a m i) -> p a i m", a=PASSES, i=PACK),
-        )
+        gather_scales(0)
+        gather_words(0, 1)
         gather_words(1, 0)
 
-        wa_w = {}
-
-        def prepare_wa(a, lo, hi):
-            n = hi - lo
-            grouped = sb([P, n * P * PACK], BF16, f"wa_g{a}_{lo}")
+        def round_pair_slice(grouped, a, s):
             nc.scalar.copy(
-                grouped[:].rearrange("p (i m c j) -> p i m j c", i=n, c=RUN, j=PACK),
-                wa_raw[a][:].rearrange("p j (m i c) -> p i m j c", i=PACK, c=RUN)[:, lo:hi],
+                grouped[:, half_cols(a)].rearrange("p (m h c j) -> p m h j c", h=2, c=RUN, j=PACK),
+                wa_raw[a, s][:].rearrange("p j (m h c) -> p m h j c", h=PACK, c=RUN)[:, :, :2],
             )
-            codes = sb([P, n * P], U32, f"wa_w{a}_{lo}")
-            scales = sb([P, n * P], U8, f"wa_sc{a}_{lo}")
-            done = 0
-            for width in (4, 2, 1):
-                if n - done >= width:
-                    cols = slice(done * P, (done + width) * P)
-                    nc.vector.quantize_mx(
-                        out=codes[:, cols].bitcast(FP8X4),
-                        scales=scales[:, cols],
-                        in_=grouped[:, cols.start * PACK : cols.stop * PACK],
+
+        def round_on_gpsimd(dst, src):
+            nc.gpsimd.tensor_scalar(dst, src, 1.0, 0.0, ALU.mult, ALU.add)
+
+        def round_single_slice(i, tag, copy, walk):
+            grouped = sb([P, PASSES * BANK], BF16, f"wa_g{i}", tag)
+            for a in range(PASSES):
+                for s in range(2):
+                    at = a * BANK + s * BANK // 2
+                    copy(
+                        grouped[:, at : at + BANK // 2].rearrange("p (m c j) -> p " + walk, c=RUN, j=PACK),
+                        wa_raw[a, s][:].rearrange("p j (m h c) -> p h " + walk, h=PACK, c=RUN)[:, i],
                     )
-                    done = done + width
-            for i in range(lo, hi):
-                cols = slice((i - lo) * P, (i - lo + 1) * P)
-                wa_w[a, i] = (codes[:, cols].bitcast(FP8X4), scales[:, cols])
+            return grouped
 
-        prepare_wa(0, 0, PACK)
-        prepare_wa(1, 0, 1)
-        for a in range(PASSES):
-            gather_scales(a, 1)
-            gather_words(a, 1)
+        wa_w, wa_sc = {}, {}
 
-        damping = [sb([P, S], F32, f"damping{i}") for i in range(PACK)]
+        def quantise_wa(i, grouped):
+            wa_w[i] = sb([P, PASSES * P], U32, f"wa_w{i}")
+            wa_sc[i] = sb([P, PASSES * P], U8, f"wa_sc{i}")
+            nc.vector.quantize_mx(out=wa_w[i][:].bitcast(FP8X4), scales=wa_sc[i][:], in_=grouped[:])
 
-        def damp(i, h):
-            acc = bank("x" if h == 0 else "y")
+        def product(tag, codes, scales, h):
+            acc = bank(tag)
             for a in range(PASSES):
-                at = (a * PACK + i) * P
                 nc.tensor.matmul_mx(
                     out=acc[:],
-                    lhsT=wb_w[:, 2 * at : 2 * (at + P)].bitcast(FP4X4),
-                    lhsT_scale=wb_sc[:, at : at + P],
-                    rhs=v_w[a][h][:].bitcast(FP8X4),
-                    rhs_scale=v_sc[a][h][:],
+                    lhsT=codes(a),
+                    lhsT_scale=scales(a),
+                    rhs=v_w[a, h][:].bitcast(FP8X4),
+                    rhs_scale=v_sc[a, h],
                     start=(a == 0),
                     stop=(a == PASSES - 1),
                 )
-            size = ring.tile([P, BANK], F32, name="size")
+            return acc
+
+        def stress(i, h, tag):
+            return product(
+                tag,
+                lambda a: wb_w[:, 2 * (a * PACK + i) * P : 2 * (a * PACK + i + 1) * P].bitcast(FP4X4),
+                lambda a: wb_sc[:, (a * PACK + i) * P : (a * PACK + i + 1) * P],
+                h,
+            )
+
+        def loadings(i, h, tag):
+            return product(
+                tag,
+                lambda a: wa_w[i][:, a * P : (a + 1) * P].bitcast(FP8X4),
+                lambda a: wa_sc[i][:, a * P : (a + 1) * P],
+                h,
+            )
+
+        def size_of(i, h, bank_tag, tag=None):
+            acc = stress(i, h, bank_tag)
+            size = sb([P, BANK], F32, f"size{i}_{h}", tag)
             nc.scalar.activation(size[:], acc[:], ACT.Abs)
-            root = ring.tile([P, BANK], F32, name="root")
+            return size
+
+        def root_of(i, h, size):
+            root = sb([P, BANK], F32, f"root{i}_{h}")
             nc.scalar.activation(root[:], size[:], ACT.Abs_reciprocal_sqrt, bias=1.0)
-            nc.scalar.activation(damping[i][:, half_cols(h)], root[:], ACT.Square)
+            return root
 
-        def loadings(i, h, dst):
-            acc = bank("a")
-            for a in range(PASSES):
-                codes, scales = wa_w[a, i]
-                nc.tensor.matmul_mx(
-                    out=acc[:],
-                    lhsT=codes,
-                    lhsT_scale=scales,
-                    rhs=v_w[a][h][:].bitcast(FP8X4),
-                    rhs_scale=v_sc[a][h][:],
-                    start=(a == 0),
-                    stop=(a == PASSES - 1),
+        def factor_of(i, h, root):
+            factor = sb([P, BANK], F32, f"factor{i}_{h}")
+            nc.scalar.activation(factor[:], root[:], ACT.Square)
+            return factor
+
+        def weigh(engine, i, h, factor, tag=None):
+            weighed = sb([P, BANK], F32, f"weighed{i}_{h}", tag)
+            rows = pair_weight[h][:] if i < 2 else weight[i][:, half_cols(h)]
+            engine.tensor_tensor(weighed[:], factor[:], rows, ALU.mult)
+            return weighed
+
+        def trade_half(i, h, weighed, tag=None):
+            acc = loadings(i, h, "a")
+            trades = sb([P, BANK], F32, f"trades{i}_{h}", tag)
+            nc.vector.tensor_tensor(trades[:], acc[:], weighed[:], ALU.mult)
+            nc.vector.tensor_copy(page[i][:].indirect(half_list(idx2, h)), trades[:])
+
+        grouped0 = sb([P, PASSES * BANK], BF16, "wa_g0")
+        round_pair_slice(grouped0, 0, 0)
+        wb_w = deal(wb_raw, "wb_w", 2)
+        wb_sc = deal(wb_sc_raw, "wb_sc", 1)
+        round_pair_slice(grouped0, 1, 0)
+        factor00 = factor_of(0, 0, root_of(0, 0, size_of(0, 0, "b")))
+        gather_words(1, 1)
+        gather_scales(1, "wb_sc_raw")
+        quantise_wa(0, grouped0)
+        weighed00 = weigh(nc.vector, 0, 0, factor00)
+        trade_half(0, 0, weighed00)
+
+        factor10 = factor_of(1, 0, root_of(1, 0, size_of(1, 0, "b", "root0_0")))
+        weighed10 = weigh(nc.gpsimd, 1, 0, factor10, "factor0_0")
+        grouped2 = round_single_slice(2, "weighed0_0", round_on_gpsimd, "m c j")
+        factor01 = factor_of(0, 1, root_of(0, 1, size_of(0, 1, "b", "root1_0")))
+        weighed01 = weigh(nc.gpsimd, 0, 1, factor01)
+        grouped1 = sb([P, PASSES * BANK], BF16, "wa_g1", "root1_0")
+        for a in range(PASSES):
+            round_pair_slice(grouped1, a, 1)
+        quantise_wa(1, grouped1)
+        trade_half(0, 1, weighed01, "root1_0")
+
+        factor11 = factor_of(1, 1, root_of(1, 1, size_of(1, 1, "b", "root0_1")))
+        weighed11 = weigh(nc.gpsimd, 1, 1, factor11)
+        quantise_wa(2, grouped2)
+        trade_half(1, 0, weighed10, "weighed0_0")
+        factor20 = factor_of(2, 0, root_of(2, 0, size_of(2, 0, "s", "root0_1")))
+        size21 = size_of(2, 1, "s", "root1_1")
+        quantise_wa(3, round_single_slice(3, "factor0_0", nc.scalar.copy, "m j c"))
+        trade_half(1, 1, weighed11, "factor0_0")
+
+        wr_w = sb([P, N], U32, "wr_w")
+        wr_sc = sb([P, N], U8, "wr_sc")
+
+        def prepare_wr(e, tag):
+            grouped = sb([P, N // 2 * PACK], BF16, f"wr_g{e}", tag)
+            for b in range(2):
+                at = (2 * e + b) * P
+                round_on_gpsimd(
+                    grouped[:, half_cols(b)].rearrange("p (n j) -> p n j", j=PACK),
+                    wr_raw[:, :, at : at + P].rearrange("p j n -> p n j"),
                 )
-            nc.vector.tensor_tensor(dst, acc[:], damping[i][:, half_cols(h)], ALU.mult)
+            cols = slice(e * N // 2, (e + 1) * N // 2)
+            nc.vector.quantize_mx(out=wr_w[:, cols].bitcast(FP8X4), scales=wr_sc[:, cols], in_=grouped[:])
 
-        for h in range(HALVES):
-            damp(0, h)
-            damped = ring.tile([P, BANK], F32, name="damped_half")
-            loadings(0, h, damped[:])
-            nc.vector.tensor_tensor(page[0][:].indirect(half_list(idx2, h)), damped[:], first_weight[h][:], ALU.mult)
+        def trade_lifted(i, h, factor, bank_tag, trades):
+            weighed = weigh(nc.gpsimd, i, h, factor)
+            acc = loadings(i, h, bank_tag)
+            lifted = sb([P, BANK], F32, f"lifted{i}_{h}")
+            nc.scalar.copy(lifted[:], acc[:])
+            nc.gpsimd.tensor_tensor(trades[:, half_cols(h)], lifted[:], weighed[:], ALU.mult)
 
-        prepare_wa(1, 1, PACK)
-        for i, tag in ((1, "weight0_0"), (2, "weight0_1")):
-            page.append(sb([P, T2], F32, f"page{i}", tag=tag))
-            nc.gpsimd.memset(page[i][:], 0.0)
-        for i in range(1, PACK):
-            for h in range(HALVES):
-                damp(i, h)
+        def scatter(i, trades):
+            nc.vector.tensor_copy(page[i % 2][:].indirect(idx2[:]), trades[:])
 
-        turned = [sb([P, BLOCKS, P, 2], BF16, f"turned{c}") for c in range(CHUNKS)]
-        pairs = [sb([P, 2, BANK], F32, f"pairs{c}") for c in range(CHUNKS)]
+        trades2 = sb([P, S], F32, "trades2")
+        trade_lifted(2, 0, factor20, "b", trades2)
+        trade_lifted(2, 1, factor_of(2, 1, root_of(2, 1, size21)), "b", trades2)
+        sizes3 = [size_of(3, h, "b") for h in range(HALVES)]
+        roots3 = [root_of(3, h, sizes3[h]) for h in range(HALVES)]
+        factors3 = [factor_of(3, h, roots3[h]) for h in range(HALVES)]
+
+        turned_tags = ["root2_1", "root2_0", "root1_1", "root0_1"]
+        turned = [sb([P, BLOCKS, 2, P], BF16, f"turned{c}", turned_tags[c]) for c in range(CHUNKS)]
+        pairs = [sb([P, 2, BANK], F32, f"pairs{c}", f"wa_raw{c // 2}_{c % 2}") for c in range(CHUNKS)]
 
         def add_turned(i, c):
-            acc = bank("x")
+            acc = bank("s")
             for bl in range(BLOCKS):
                 cols = slice(c * BANK + bl * P, c * BANK + (bl + 1) * P)
                 dst = acc[:, bl * P : (bl + 1) * P]
                 nc.tensor.matmul(dst, held[i][:, cols], ident[:], start=True, stop=False, is_transpose=True)
-                nc.tensor.matmul(dst, page[i][:, cols], ident[:], start=False, stop=True, is_transpose=True)
-            nc.scalar.copy(turned[c][:, :, :, i % 2], acc[:].rearrange("t (b p) -> t b p", b=BLOCKS))
+                nc.tensor.matmul(dst, page[i % 2][:, cols], ident[:], start=False, stop=True, is_transpose=True)
+            nc.scalar.copy(
+                turned[c][:, :, i, :].rearrange("t b (m c e) -> t b m c e", c=RUN, e=2),
+                acc[:].rearrange("t (b m e c) -> t b m c e", b=BLOCKS, e=2, c=RUN),
+            )
 
-        def turn_back(u, c):
-            acc = bank("y")
-            words = turned[c][:].rearrange("t b p e -> t (b p e)").bitcast(F32)
+        def turn_back(c):
+            acc = bank("a")
+            words = turned[c][:].rearrange("t b s x -> t (b s x)").bitcast(F32)
             for bl in range(BLOCKS):
                 cols = slice(bl * P, (bl + 1) * P)
                 nc.tensor.transpose(acc[:, cols], words[:, cols], ident[:])
-            nc.scalar.copy(pairs[c][:, u, :], acc[:])
+            nc.scalar.copy(pairs[c][:, 0, :], acc[:])
 
-        def trade(i):
-            damped = ring.tile([P, S], F32, name="damped")
-            for h in range(HALVES):
-                loadings(i, h, damped[:, half_cols(h)])
-            nc.vector.tensor_tensor(page[i][:].indirect(idx2[:]), damped[:], weight[i][:], ALU.mult)
-
-        trade(1)
-        page.append(sb([P, T2], F32, "page3", tag="weight1"))
-        nc.gpsimd.memset(page[3][:], 0.0)
-        for c in range(CHUNKS):
-            add_turned(0, c)
-        trade(2)
+        trades3 = sb([P, S], F32, "trades3")
+        for h in range(HALVES):
+            add_turned(0, 2 * h)
+            add_turned(0, 2 * h + 1)
+            trade_lifted(3, h, factors3[h], "a", trades3)
+        scatter(2, trades2)
+        prepare_wr(0, "lifted2_1")
         for c in range(CHUNKS):
             add_turned(1, c)
-            turn_back(0, c)
-        wr_g = sb([P, N * PACK], BF16, "wr_g")
-        nc.scalar.copy(
-            wr_g[:].rearrange("p (c i j) -> p c j i", i=4, j=PACK),
-            wr_raw[:].rearrange("p j (c i) -> p c j i", i=4),
-        )
-        wr_w = sb([P, N], U32, "wr_w")
-        wr_sc = sb([P, N], U8, "wr_sc")
-        nc.vector.quantize_mx(out=wr_w[:].bitcast(FP8X4), scales=wr_sc[:], in_=wr_g[:])
-        trade(3)
+        scatter(3, trades3)
+        prepare_wr(1, "lifted3_1")
         for c in range(CHUNKS):
-            add_turned(2, c)
-            turn_back(1, c)
+            turn_back(c)
+
+        total = sb([P, T2], F32, "total", "weighed3_1")
+        for c in range(CHUNKS):
+            cols = half_cols(c)
+            nc.gpsimd.tensor_tensor(total[:, cols], held[2][:, cols], page[0][:, cols], ALU.add)
+            nc.scalar.copy(
+                pairs[c][:, 1, :].bitcast(BF16).rearrange("p (t e) -> p t e", e=2),
+                total[:, cols].unsqueeze(2).to_broadcast([P, BANK, 2]),
+            )
 
         last = PACK - 1
         out_rows = out.rearrange("(b p) t -> p b t", p=P)
-        stage_tags = ["tab_w0", "tab_w1", "wa_raw0", "hold0"]
-        out_banks = ["a", "a", "a", "a", "x", "x", "y", "y"]
+        stage_tags = ["tab_w0", "tab_w1", "hold0", "hold1"]
+        out_banks = ["b", "b", "s", "s", "s", "s", "a", "a"]
         results = [sb([P, N // P * BANK], F32, f"result{c}", tag=stage_tags[c]) for c in range(CHUNKS)]
-        banks_used = 0
-        start = 0
-        for width in STRIPS:
-            c, at = divmod(start, BANK)
-            cols = slice(start, start + width)
-            words = pairs[c][:, :, at : at + width]
-            halves = words[:, last // 2, :].bitcast(BF16).rearrange("p (t e) -> p t e", e=2)
-            nc.vector.tensor_tensor(halves[:, :, last % 2], page[last][:, cols], held[last][:, cols], ALU.add)
-            z_g = ring.tile([P, width, 2], F32, name="z_g", align_bytes=64)
-            nc.vector.tensor_copy(z_g[:], words.rearrange("p u t -> p t u"))
-            z_w = sb([P, width], U32, f"z_w{start}")
-            z_sc = sb([P, width], U8, f"z_sc{start}")
+        starts = [sum(STRIPS[:k]) for k in range(len(STRIPS))]
+        woven = {}
+
+        def strip_words(k):
+            c, at = divmod(starts[k], BANK)
+            return pairs[c][:, :, at : at + STRIPS[k]]
+
+        def add_last(k):
+            cols = slice(starts[k], starts[k] + STRIPS[k])
+            halves = strip_words(k)[:, last // 2, :].bitcast(BF16).rearrange("p (t e) -> p t e", e=2)
+            nc.vector.tensor_tensor(halves[:, :, last % 2], page[last % 2][:, cols], held[last][:, cols], ALU.add)
+
+        def weave(k):
+            woven[k] = ring.tile([P, STRIPS[k], 2], F32, name="woven", align_bytes=64)
+            nc.vector.tensor_copy(woven[k][:], strip_words(k).rearrange("p u t -> p t u"))
+
+        def expose(k):
+            width = STRIPS[k]
+            cols = slice(starts[k], starts[k] + width)
+            z_w = sb([P, width], U32, f"z_w{k}")
+            z_sc = sb([P, width], U8, f"z_sc{k}")
             nc.vector.quantize_mx(
                 out=z_w[:].bitcast(FP8X4),
                 scales=z_sc[:],
-                in_=z_g[:].rearrange("p t u -> p (t u)").bitcast(BF16),
+                in_=woven[k][:].rearrange("p t u -> p (t u)").bitcast(BF16),
             )
             per_bank = BANK // width
             for first in range(0, N // P, per_bank):
-                acc = bank(out_banks[banks_used % len(out_banks)])
+                used = (starts[k] * (N // P) + first * width) // BANK
+                acc = bank(out_banks[used % len(out_banks)])
                 for b in range(first, first + per_bank):
                     rows = slice(b * P, (b + 1) * P)
                     nc.tensor.matmul_mx(
@@ -314,11 +404,9 @@ def tile_list_damped_trade_exposure_kernel(
                         start=True,
                         stop=True,
                     )
-                slot = banks_used % (N // P)
-                result = results[c][:, slot * BANK : (slot + 1) * BANK]
-                banks_used = banks_used + 1
-                if banks_used == CHUNKS * N // P:
-                    negated = ring.tile([P, BANK], F32, name="negated")
+                result = results[used // (N // P)][:, half_cols(used % (N // P))]
+                if used == CHUNKS * N // P - 1:
+                    negated = sb([P, BANK], F32, "negated")
                     nc.vector.tensor_scalar(negated[:], acc[:], -1.0, None, ALU.mult)
                     nc.vector.tensor_tensor(result, acc[:], negated[:], ALU.max)
                 else:
@@ -326,4 +414,14 @@ def tile_list_damped_trade_exposure_kernel(
                 nc.sync.dma_start(
                     out_rows[:, first : first + per_bank, cols], result.rearrange("p (b t) -> p b t", b=per_bank)
                 )
-            start = start + width
+
+        add_last(0)
+        add_last(1)
+        weave(0)
+        weave(1)
+        expose(0)
+        for k in range(2, len(STRIPS)):
+            add_last(k)
+            expose(k - 1)
+            weave(k)
+        expose(len(STRIPS) - 1)

@@ -111,9 +111,10 @@ def tile_list_damped_trade_exposure_kernel(
         wa_raw[1, 0] = load_wa(1, 0)
         idx2 = keep.tile([P, S // 16], U16, name="idx2")
         nc.sync.dma_start(idx2[:], offs2)
-        pair_weight = [load_pair_weight(h) for h in range(HALVES)]
+        pair_weight = [load_pair_weight(0)]
         for a in range(PASSES):
             wa_raw[a, 1] = load_wa(a, 1)
+        pair_weight.append(load_pair_weight(1))
         held = [load_hold(0)]
         weight = {2: load_weight(2)}
         held.append(load_hold(1))
@@ -169,17 +170,14 @@ def tile_list_damped_trade_exposure_kernel(
                 wa_raw[a, s][:].rearrange("p j (m h c) -> p m h j c", h=PACK, c=RUN)[:, :, :2],
             )
 
-        def round_on_gpsimd(dst, src):
-            nc.gpsimd.tensor_scalar(dst, src, 1.0, 0.0, ALU.mult, ALU.add)
-
-        def round_single_slice(i, tag, copy, walk):
+        def round_single_slice(i, tag):
             grouped = sb([P, PASSES * BANK], BF16, f"wa_g{i}", tag)
             for a in range(PASSES):
                 for s in range(2):
                     at = a * BANK + s * BANK // 2
-                    copy(
-                        grouped[:, at : at + BANK // 2].rearrange("p (m c j) -> p " + walk, c=RUN, j=PACK),
-                        wa_raw[a, s][:].rearrange("p j (m h c) -> p h " + walk, h=PACK, c=RUN)[:, i],
+                    nc.scalar.copy(
+                        grouped[:, at : at + BANK // 2].rearrange("p (m c j) -> p m j c", c=RUN, j=PACK),
+                        wa_raw[a, s][:].rearrange("p j (m h c) -> p h m j c", h=PACK, c=RUN)[:, i],
                     )
             return grouped
 
@@ -236,17 +234,34 @@ def tile_list_damped_trade_exposure_kernel(
             nc.scalar.activation(factor[:], root[:], ACT.Square)
             return factor
 
-        def weigh(engine, i, h, factor, tag=None):
-            weighed = sb([P, BANK], F32, f"weighed{i}_{h}", tag)
+        def weigh(i, h, factor):
+            weighed = sb([P, BANK], F32, f"weighed{i}_{h}")
             rows = pair_weight[h][:] if i < 2 else weight[i][:, half_cols(h)]
-            engine.tensor_tensor(weighed[:], factor[:], rows, ALU.mult)
+            nc.vector.tensor_tensor(weighed[:], factor[:], rows, ALU.mult)
             return weighed
 
-        def trade_half(i, h, weighed, tag=None):
+        def trade_half(i, h, factor, tag=None):
+            weighed = weigh(i, h, factor)
             acc = loadings(i, h, "a")
             trades = sb([P, BANK], F32, f"trades{i}_{h}", tag)
             nc.vector.tensor_tensor(trades[:], acc[:], weighed[:], ALU.mult)
             nc.vector.tensor_copy(page[i][:].indirect(half_list(idx2, h)), trades[:])
+
+        def factors_of(i, bank_tag, tags):
+            sizes = [size_of(i, h, bank_tag, tags[h]) for h in range(HALVES)]
+            roots = [root_of(i, h, sizes[h]) for h in range(HALVES)]
+            return [factor_of(i, h, roots[h]) for h in range(HALVES)]
+
+        def trades_of(i, factors):
+            weighed = [weigh(i, h, factors[h]) for h in range(HALVES)]
+            trades = sb([P, S], F32, f"trades{i}")
+            for h in range(HALVES):
+                acc = loadings(i, h, "a")
+                nc.vector.tensor_tensor(trades[:, half_cols(h)], acc[:], weighed[h][:], ALU.mult)
+            return trades
+
+        def scatter(i, trades):
+            nc.vector.tensor_copy(page[i % 2][:].indirect(idx2[:]), trades[:])
 
         grouped0 = sb([P, PASSES * BANK], BF16, "wa_g0")
         round_pair_slice(grouped0, 0, 0)
@@ -257,61 +272,25 @@ def tile_list_damped_trade_exposure_kernel(
         gather_words(1, 1)
         gather_scales(1, "wb_sc_raw")
         quantise_wa(0, grouped0)
-        weighed00 = weigh(nc.vector, 0, 0, factor00)
-        trade_half(0, 0, weighed00)
+        trade_half(0, 0, factor00)
 
-        factor10 = factor_of(1, 0, root_of(1, 0, size_of(1, 0, "b", "root0_0")))
-        weighed10 = weigh(nc.gpsimd, 1, 0, factor10, "factor0_0")
-        grouped2 = round_single_slice(2, "weighed0_0", round_on_gpsimd, "m c j")
-        factor01 = factor_of(0, 1, root_of(0, 1, size_of(0, 1, "b", "root1_0")))
-        weighed01 = weigh(nc.gpsimd, 0, 1, factor01)
-        grouped1 = sb([P, PASSES * BANK], BF16, "wa_g1", "root1_0")
+        grouped1 = sb([P, PASSES * BANK], BF16, "wa_g1", "root0_0")
         for a in range(PASSES):
             round_pair_slice(grouped1, a, 1)
+        factor01 = factor_of(0, 1, root_of(0, 1, size_of(0, 1, "b", "factor0_0")))
         quantise_wa(1, grouped1)
-        trade_half(0, 1, weighed01, "root1_0")
+        trade_half(0, 1, factor01, "root0_0")
 
-        factor11 = factor_of(1, 1, root_of(1, 1, size_of(1, 1, "b", "root0_1")))
-        weighed11 = weigh(nc.gpsimd, 1, 1, factor11)
-        quantise_wa(2, grouped2)
-        trade_half(1, 0, weighed10, "weighed0_0")
-        factor20 = factor_of(2, 0, root_of(2, 0, size_of(2, 0, "s", "root0_1")))
-        size21 = size_of(2, 1, "s", "root1_1")
-        quantise_wa(3, round_single_slice(3, "factor0_0", nc.scalar.copy, "m j c"))
-        trade_half(1, 1, weighed11, "factor0_0")
+        factor10 = factor_of(1, 0, root_of(1, 0, size_of(1, 0, "b", "root0_1")))
+        trade_half(1, 0, factor10)
+        factor11 = factor_of(1, 1, root_of(1, 1, size_of(1, 1, "b", "root1_0")))
+        quantise_wa(2, round_single_slice(2, "root1_1"))
+        trade_half(1, 1, factor11, "root1_1")
 
-        wr_w = sb([P, N], U32, "wr_w")
-        wr_sc = sb([P, N], U8, "wr_sc")
+        trades2 = trades_of(2, factors_of(2, "b", ["root1_0", "factor1_0"]))
+        quantise_wa(3, round_single_slice(3, "root2_1"))
 
-        def prepare_wr(e, tag):
-            grouped = sb([P, N // 2 * PACK], BF16, f"wr_g{e}", tag)
-            for b in range(2):
-                at = (2 * e + b) * P
-                round_on_gpsimd(
-                    grouped[:, half_cols(b)].rearrange("p (n j) -> p n j", j=PACK),
-                    wr_raw[:, :, at : at + P].rearrange("p j n -> p n j"),
-                )
-            cols = slice(e * N // 2, (e + 1) * N // 2)
-            nc.vector.quantize_mx(out=wr_w[:, cols].bitcast(FP8X4), scales=wr_sc[:, cols], in_=grouped[:])
-
-        def trade_lifted(i, h, factor, bank_tag, trades):
-            weighed = weigh(nc.gpsimd, i, h, factor)
-            acc = loadings(i, h, bank_tag)
-            lifted = sb([P, BANK], F32, f"lifted{i}_{h}")
-            nc.scalar.copy(lifted[:], acc[:])
-            nc.gpsimd.tensor_tensor(trades[:, half_cols(h)], lifted[:], weighed[:], ALU.mult)
-
-        def scatter(i, trades):
-            nc.vector.tensor_copy(page[i % 2][:].indirect(idx2[:]), trades[:])
-
-        trades2 = sb([P, S], F32, "trades2")
-        trade_lifted(2, 0, factor20, "b", trades2)
-        trade_lifted(2, 1, factor_of(2, 1, root_of(2, 1, size21)), "b", trades2)
-        sizes3 = [size_of(3, h, "b") for h in range(HALVES)]
-        roots3 = [root_of(3, h, sizes3[h]) for h in range(HALVES)]
-        factors3 = [factor_of(3, h, roots3[h]) for h in range(HALVES)]
-
-        turned_tags = ["root2_1", "root2_0", "root1_1", "root0_1"]
+        turned_tags = ["factor2_0", "factor2_1", "weighed2_0", "weighed2_1"]
         turned = [sb([P, BLOCKS, 2, P], BF16, f"turned{c}", turned_tags[c]) for c in range(CHUNKS)]
         pairs = [sb([P, 2, BANK], F32, f"pairs{c}", f"wa_raw{c // 2}_{c % 2}") for c in range(CHUNKS)]
 
@@ -328,40 +307,35 @@ def tile_list_damped_trade_exposure_kernel(
             )
 
         def turn_back(c):
-            acc = bank("a")
+            acc = bank("b")
             words = turned[c][:].rearrange("t b s x -> t (b s x)").bitcast(F32)
             for bl in range(BLOCKS):
                 cols = slice(bl * P, (bl + 1) * P)
                 nc.tensor.transpose(acc[:, cols], words[:, cols], ident[:])
             nc.scalar.copy(pairs[c][:, 0, :], acc[:])
 
-        trades3 = sb([P, S], F32, "trades3")
-        for h in range(HALVES):
-            add_turned(0, 2 * h)
-            add_turned(0, 2 * h + 1)
-            trade_lifted(3, h, factors3[h], "a", trades3)
+        for c in range(CHUNKS):
+            add_turned(0, c)
         scatter(2, trades2)
-        prepare_wr(0, "lifted2_1")
+        trades3 = trades_of(3, factors_of(3, "b", ["root2_1", "root1_1"]))
         for c in range(CHUNKS):
             add_turned(1, c)
         scatter(3, trades3)
-        prepare_wr(1, "lifted3_1")
+        wr_g = sb([P, N * PACK], BF16, "wr_g", "root3_0")
+        for b in range(N // P):
+            nc.scalar.copy(
+                wr_g[:, half_cols(b)].rearrange("p (n i j) -> p n j i", i=4, j=PACK),
+                wr_raw[:, :, b * P : (b + 1) * P].rearrange("p j (n i) -> p n j i", i=4),
+            )
+        wr_w = sb([P, N], U32, "wr_w")
+        wr_sc = sb([P, N], U8, "wr_sc")
+        nc.vector.quantize_mx(out=wr_w[:].bitcast(FP8X4), scales=wr_sc[:], in_=wr_g[:])
         for c in range(CHUNKS):
             turn_back(c)
 
-        total = sb([P, T2], F32, "total", "weighed3_1")
-        for c in range(CHUNKS):
-            cols = half_cols(c)
-            nc.gpsimd.tensor_tensor(total[:, cols], held[2][:, cols], page[0][:, cols], ALU.add)
-            nc.scalar.copy(
-                pairs[c][:, 1, :].bitcast(BF16).rearrange("p (t e) -> p t e", e=2),
-                total[:, cols].unsqueeze(2).to_broadcast([P, BANK, 2]),
-            )
-
-        last = PACK - 1
         out_rows = out.rearrange("(b p) t -> p b t", p=P)
         stage_tags = ["tab_w0", "tab_w1", "hold0", "hold1"]
-        out_banks = ["b", "b", "s", "s", "s", "s", "a", "a"]
+        out_banks = ["a", "a", "s", "s", "s", "s", "b", "b"]
         results = [sb([P, N // P * BANK], F32, f"result{c}", tag=stage_tags[c]) for c in range(CHUNKS)]
         starts = [sum(STRIPS[:k]) for k in range(len(STRIPS))]
         woven = {}
@@ -372,8 +346,9 @@ def tile_list_damped_trade_exposure_kernel(
 
         def add_last(k):
             cols = slice(starts[k], starts[k] + STRIPS[k])
-            halves = strip_words(k)[:, last // 2, :].bitcast(BF16).rearrange("p (t e) -> p t e", e=2)
-            nc.vector.tensor_tensor(halves[:, :, last % 2], page[last % 2][:, cols], held[last][:, cols], ALU.add)
+            halves = strip_words(k)[:, 1, :].bitcast(BF16).rearrange("p (t e) -> p t e", e=2)
+            for e in range(2):
+                nc.vector.tensor_tensor(halves[:, :, e], page[e][:, cols], held[2 + e][:, cols], ALU.add)
 
         def weave(k):
             woven[k] = ring.tile([P, STRIPS[k], 2], F32, name="woven", align_bytes=64)

@@ -27,7 +27,7 @@ BLOCKS = BANK // P
 QUAD = 32
 RUN = 4
 GROUP = PACK * RUN
-STRIPS = (128, 128, 256, 512, 512, 512)
+STRIPS = (128, 128, 256, 256, 256, 512, 256, 256)
 
 
 def tile_list_damped_trade_exposure_kernel(
@@ -76,11 +76,9 @@ def tile_list_damped_trade_exposure_kernel(
             return tile
 
         def load_pair_weight(h):
-            tile = sb([P, BANK], F32, f"pair_weight{h}")
             rows = wgs.rearrange("(m x) j -> m x j", x=GROUP)[:, : 2 * RUN, half_cols(h)]
             for rep in range(2):
-                nc.sync.dma_start(tile[rep * P // 2 : (rep + 1) * P // 2, :], rows)
-            return tile
+                nc.sync.dma_start(pair_weight[rep * P // 2 : (rep + 1) * P // 2, half_cols(h)], rows)
 
         def load_weight(i):
             tile = sb([P, S], F32, f"weight{i}")
@@ -99,22 +97,22 @@ def tile_list_damped_trade_exposure_kernel(
             return tile
 
         tab_w = [load_tab(0)]
-        tab_sc = load_scales(tab_scales, "tab_sc")
-        wa_raw = {(0, 0): load_wa(0, 0)}
-        tab_w.append(load_tab(1))
         wb_raw = sb([P, PASSES * 2 * H], U8, "wb_raw")
         nc.sync.dma_start(
             wb_raw[:].bitcast(I32).rearrange("p (a c) -> p a c", a=PASSES),
             wb_words.bitcast(I32).rearrange("a p c -> p a c"),
         )
+        tab_sc = load_scales(tab_scales, "tab_sc")
+        tab_w.append(load_tab(1))
         wb_sc_raw = load_scales(wb_scales, "wb_sc_raw")
-        wa_raw[1, 0] = load_wa(1, 0)
+        wa_raw = {(a, 0): load_wa(a, 0) for a in range(PASSES)}
         idx2 = keep.tile([P, S // 16], U16, name="idx2")
         nc.sync.dma_start(idx2[:], offs2)
-        pair_weight = [load_pair_weight(0)]
+        pair_weight = sb([P, S], F32, "pair_weight")
+        load_pair_weight(0)
         for a in range(PASSES):
             wa_raw[a, 1] = load_wa(a, 1)
-        pair_weight.append(load_pair_weight(1))
+        load_pair_weight(1)
         held = [load_hold(0)]
         weight = {2: load_weight(2)}
         held.append(load_hold(1))
@@ -132,9 +130,8 @@ def tile_list_damped_trade_exposure_kernel(
         ident = sb([P, P], F32, "ident")
         make_identity(nc, ident[:])
 
-        page = [sb([P, T2], F32, f"page{n}") for n in range(2)]
-        for tile in page:
-            nc.vector.memset(tile[:].bitcast(I32), 0)
+        page = [sb([P, T2], F32, "page0")]
+        nc.vector.memset(page[0][:], 0.0)
 
         v_w, v_sc = {}, {}
 
@@ -142,51 +139,44 @@ def tile_list_damped_trade_exposure_kernel(
             v_w[a, h] = sb([P, BANK], U32, f"v_w{a}_{h}", tag)
             nc.vector.tensor_copy(v_w[a, h][:], tab_w[a][:].indirect(half_list(idx, h)))
 
-        def gather_scales(h, tag=None):
-            tile = sb([P, PASSES * BANK], U8, f"v_sc{h}", tag)
-            for a in range(PASSES):
-                v_sc[a, h] = tile[:, a * BANK : (a + 1) * BANK]
-                nc.vector.tensor_copy(v_sc[a, h], tab_sc[:, a * T : (a + 1) * T].indirect(half_list(idx, h)))
+        def gather_scales(a, h, tag=None):
+            v_sc[a, h] = sb([P, BANK], U8, f"v_sc{a}_{h}", tag)
+            nc.vector.tensor_copy(v_sc[a, h][:], tab_sc[:, a * T : (a + 1) * T].indirect(half_list(idx, h)))
 
-        def deal(raw, name, words):
-            tile = sb([P, raw.shape[1]], U8, name)
-            src = raw[:].bitcast(U32).rearrange("p (a m w) -> p a m w", a=PASSES, w=PACK * words)
-            dst = tile[:].bitcast(U32).rearrange("p (a e x) -> p a e x", a=PASSES, e=2)
-            nc.scalar.copy(dst[:, :, 0, :].rearrange("p a (m w) -> p a m w", w=2 * words), src[:, :, :, : 2 * words])
-            nc.scalar.copy(
-                dst[:, :, 1, :].rearrange("p a (i m w) -> p a i m w", i=2, w=words),
-                src[:, :, :, 2 * words :].rearrange("p a m (i w) -> p a i m w", i=2),
-            )
+        def deal(part, tag=None):
+            tile = sb([P, PASSES * 3 * H // 2], U8, f"wb_part{part}", tag)
+            for raw, dst, words in ((wb_raw, tile[:, : PASSES * H], 2), (wb_sc_raw, tile[:, PASSES * H :], 1)):
+                src = raw[:].bitcast(U32).rearrange("p (a m e i w) -> p e a i m w", a=PASSES, e=2, i=1 + part, w=2 * words // (1 + part))
+                nc.scalar.copy(dst.bitcast(U32).rearrange("p (a i m w) -> p a i m w", a=PASSES, i=1 + part, m=QUAD), src[:, part])
             return tile
 
         gather_words(0, 0)
-        gather_scales(0)
-        gather_words(0, 1)
+        for a in range(PASSES):
+            gather_scales(a, 0)
         gather_words(1, 0)
 
-        def round_pair_slice(grouped, a, s):
-            nc.scalar.copy(
-                grouped[:, half_cols(a)].rearrange("p (m h c j) -> p m h j c", h=2, c=RUN, j=PACK),
+        def round_pair_slice(copy, grouped, a, s):
+            copy(
+                grouped.rearrange("p (m h c j) -> p m h j c", h=2, c=RUN, j=PACK),
                 wa_raw[a, s][:].rearrange("p j (m h c) -> p m h j c", h=PACK, c=RUN)[:, :, :2],
             )
 
-        def round_single_slice(i, tag):
-            grouped = sb([P, PASSES * BANK], BF16, f"wa_g{i}", tag)
-            for a in range(PASSES):
-                for s in range(2):
-                    at = a * BANK + s * BANK // 2
-                    nc.scalar.copy(
-                        grouped[:, at : at + BANK // 2].rearrange("p (m c j) -> p m j c", c=RUN, j=PACK),
-                        wa_raw[a, s][:].rearrange("p j (m h c) -> p h m j c", h=PACK, c=RUN)[:, i],
-                    )
-            return grouped
+        grouped_late = sb([P, PASSES, 2, 2, BANK // 2], BF16, "wa_g_late")
 
-        wa_w, wa_sc = {}, {}
+        def round_late_slices(a, s):
+            nc.scalar.copy(
+                grouped_late[:, a, :, s, :].rearrange("p i (m c j) -> p i m j c", c=RUN, j=PACK),
+                wa_raw[a, s][:].rearrange("p j (m h c) -> p h m j c", h=PACK, c=RUN)[:, 2:],
+            )
 
-        def quantise_wa(i, grouped):
-            wa_w[i] = sb([P, PASSES * P], U32, f"wa_w{i}")
-            wa_sc[i] = sb([P, PASSES * P], U8, f"wa_sc{i}")
-            nc.vector.quantize_mx(out=wa_w[i][:].bitcast(FP8X4), scales=wa_sc[i][:], in_=grouped[:])
+        wa_w = {0: sb([P, PASSES * P], U32, "wa_w0")}
+        wa_sc = {0: sb([P, PASSES * P], U8, "wa_sc0")}
+
+        def quantise_wa(g, grouped, cols=slice(None), tag=None):
+            if g not in wa_w:
+                wa_w[g] = sb([P, grouped.shape[1] // PACK], U32, f"wa_w{g}", tag)
+                wa_sc[g] = sb([P, grouped.shape[1] // PACK], U8, f"wa_sc{g}")
+            nc.vector.quantize_mx(out=wa_w[g][:, cols].bitcast(FP8X4), scales=wa_sc[g][:, cols], in_=grouped)
 
         def product(tag, codes, scales, h):
             acc = bank(tag)
@@ -196,25 +186,28 @@ def tile_list_damped_trade_exposure_kernel(
                     lhsT=codes(a),
                     lhsT_scale=scales(a),
                     rhs=v_w[a, h][:].bitcast(FP8X4),
-                    rhs_scale=v_sc[a, h],
+                    rhs_scale=v_sc[a, h][:],
                     start=(a == 0),
                     stop=(a == PASSES - 1),
                 )
             return acc
 
         def stress(i, h, tag):
+            words, scales = wb_part[i // 2][:, : PASSES * H], wb_part[i // 2][:, PASSES * H :]
             return product(
                 tag,
-                lambda a: wb_w[:, 2 * (a * PACK + i) * P : 2 * (a * PACK + i + 1) * P].bitcast(FP4X4),
-                lambda a: wb_sc[:, (a * PACK + i) * P : (a * PACK + i + 1) * P],
+                lambda a: words[:, 2 * (2 * a + i % 2) * P : 2 * (2 * a + i % 2 + 1) * P].bitcast(FP4X4),
+                lambda a: scales[:, (2 * a + i % 2) * P : (2 * a + i % 2 + 1) * P],
                 h,
             )
 
         def loadings(i, h, tag):
+            g = min(i, 2)
+            at = [a * P if i < 2 else (2 * a + i - 2) * P for a in range(PASSES)]
             return product(
                 tag,
-                lambda a: wa_w[i][:, a * P : (a + 1) * P].bitcast(FP8X4),
-                lambda a: wa_sc[i][:, a * P : (a + 1) * P],
+                lambda a: wa_w[g][:, at[a] : at[a] + P].bitcast(FP8X4),
+                lambda a: wa_sc[g][:, at[a] : at[a] + P],
                 h,
             )
 
@@ -234,104 +227,142 @@ def tile_list_damped_trade_exposure_kernel(
             nc.scalar.activation(factor[:], root[:], ACT.Square)
             return factor
 
-        def weigh(i, h, factor):
-            weighed = sb([P, BANK], F32, f"weighed{i}_{h}")
-            rows = pair_weight[h][:] if i < 2 else weight[i][:, half_cols(h)]
-            nc.vector.tensor_tensor(weighed[:], factor[:], rows, ALU.mult)
-            return weighed
+        def damped_half(i, h, factor):
+            damped = sb([P, BANK], F32, f"damped{i}_{h}")
+            nc.vector.tensor_tensor(damped[:], loadings(i, h, "a")[:], factor[:], ALU.mult)
+            return damped
 
-        def trade_half(i, h, factor, tag=None):
-            weighed = weigh(i, h, factor)
-            acc = loadings(i, h, "a")
-            trades = sb([P, BANK], F32, f"trades{i}_{h}", tag)
-            nc.vector.tensor_tensor(trades[:], acc[:], weighed[:], ALU.mult)
-            nc.vector.tensor_copy(page[i][:].indirect(half_list(idx2, h)), trades[:])
+        def scatter_half(i, h, damped):
+            nc.vector.tensor_tensor(page[i][:].indirect(half_list(idx2, h)), damped[:], pair_weight[:, half_cols(h)], ALU.mult)
 
         def factors_of(i, bank_tag, tags):
             sizes = [size_of(i, h, bank_tag, tags[h]) for h in range(HALVES)]
             roots = [root_of(i, h, sizes[h]) for h in range(HALVES)]
             return [factor_of(i, h, roots[h]) for h in range(HALVES)]
 
-        def trades_of(i, factors):
-            weighed = [weigh(i, h, factors[h]) for h in range(HALVES)]
-            trades = sb([P, S], F32, f"trades{i}")
+        def damped_of(i, factors, bank_tag, tag=None):
+            damped = sb([P, S], F32, f"damped{i}", tag)
             for h in range(HALVES):
-                acc = loadings(i, h, "a")
-                nc.vector.tensor_tensor(trades[:, half_cols(h)], acc[:], weighed[h][:], ALU.mult)
-            return trades
+                nc.vector.tensor_tensor(damped[:, half_cols(h)], loadings(i, h, bank_tag)[:], factors[h][:], ALU.mult)
+            return damped
 
-        def scatter(i, trades):
-            nc.vector.tensor_copy(page[i % 2][:].indirect(idx2[:]), trades[:])
+        def scatter(i, damped):
+            rows = pair_weight if i < 2 else weight[i]
+            nc.vector.tensor_tensor(page[i % 2][:].indirect(idx2[:]), damped[:], rows[:], ALU.mult)
 
-        grouped0 = sb([P, PASSES * BANK], BF16, "wa_g0")
-        round_pair_slice(grouped0, 0, 0)
-        wb_w = deal(wb_raw, "wb_w", 2)
-        wb_sc = deal(wb_sc_raw, "wb_sc", 1)
-        round_pair_slice(grouped0, 1, 0)
-        factor00 = factor_of(0, 0, root_of(0, 0, size_of(0, 0, "b")))
+        grouped0 = [sb([P, BANK], BF16, f"wa_g0_{a}") for a in range(PASSES)]
+        round_pair_slice(nc.scalar.copy, grouped0[0][:], 0, 0)
+        round_late_slices(0, 0)
+        wb_part = [deal(0)]
+        size00 = size_of(0, 0, "b", "wa_raw0_0")
+        roots00 = [sb([P, BANK // 2], F32, f"root0_0{name}") for name in ("", "b")]
+        factor00 = sb([P, BANK], F32, "factor0_0")
+        quarters = [slice(e * BANK // 2, (e + 1) * BANK // 2) for e in range(2)]
+        for e in range(2):
+            nc.scalar.activation(roots00[e][:], size00[:, quarters[e]], ACT.Abs_reciprocal_sqrt, bias=1.0)
+        for e in range(2):
+            nc.scalar.activation(factor00[:, quarters[e]], roots00[e][:], ACT.Square)
+        gather_scales(0, 1)
+        quantise_wa(0, grouped0[0][:], slice(0, P))
         gather_words(1, 1)
-        gather_scales(1, "wb_sc_raw")
-        quantise_wa(0, grouped0)
-        trade_half(0, 0, factor00)
+        round_pair_slice(nc.vector.tensor_copy, grouped0[1][:], 1, 0)
+        gather_words(0, 1, "wa_g0_0")
+        quantise_wa(0, grouped0[1][:], slice(P, 2 * P))
+        gather_scales(1, 1, "wa_g0_1")
+        scatter_half(0, 0, damped_half(0, 0, factor00))
+        page.append(sb([P, T2], F32, "page1", "factor0_0"))
+        nc.gpsimd.memset(page[1][:], 0.0)
 
+        factor10 = factor_of(1, 0, root_of(1, 0, size_of(1, 0, "b", "root0_0b")))
+        round_late_slices(1, 0)
         grouped1 = sb([P, PASSES * BANK], BF16, "wa_g1", "root0_0")
         for a in range(PASSES):
-            round_pair_slice(grouped1, a, 1)
-        factor01 = factor_of(0, 1, root_of(0, 1, size_of(0, 1, "b", "factor0_0")))
-        quantise_wa(1, grouped1)
-        trade_half(0, 1, factor01, "root0_0")
+            round_pair_slice(nc.scalar.copy, grouped1[:, half_cols(a)], a, 1)
+        factor01 = factor_of(0, 1, root_of(0, 1, size_of(0, 1, "b", "root1_0")))
+        damped01 = damped_half(0, 1, factor01)
+        quantise_wa(1, grouped1[:], tag="damped0_0")
+        scatter_half(0, 1, damped01)
 
-        factor10 = factor_of(1, 0, root_of(1, 0, size_of(1, 0, "b", "root0_1")))
-        trade_half(1, 0, factor10)
-        factor11 = factor_of(1, 1, root_of(1, 1, size_of(1, 1, "b", "root1_0")))
-        quantise_wa(2, round_single_slice(2, "root1_1"))
-        trade_half(1, 1, factor11, "root1_1")
+        wb_part.append(deal(1, "root0_0b"))
+        for a in range(PASSES):
+            round_late_slices(a, 1)
+        factor11 = factor_of(1, 1, root_of(1, 1, size_of(1, 1, "b", "root0_1")))
+        damped1 = damped_of(1, [factor10, factor11], "a", "root1_1")
+        quantise_wa(2, grouped_late[:].rearrange("p a i s x -> p (a i s x)"), tag="factor1_0")
+        scatter(1, damped1)
 
-        trades2 = trades_of(2, factors_of(2, "b", ["root1_0", "factor1_0"]))
-        quantise_wa(3, round_single_slice(3, "root2_1"))
-
-        turned_tags = ["factor2_0", "factor2_1", "weighed2_0", "weighed2_1"]
-        turned = [sb([P, BLOCKS, 2, P], BF16, f"turned{c}", turned_tags[c]) for c in range(CHUNKS)]
-        pairs = [sb([P, 2, BANK], F32, f"pairs{c}", f"wa_raw{c // 2}_{c % 2}") for c in range(CHUNKS)]
-
-        def add_turned(i, c):
-            acc = bank("s")
-            for bl in range(BLOCKS):
-                cols = slice(c * BANK + bl * P, c * BANK + (bl + 1) * P)
-                dst = acc[:, bl * P : (bl + 1) * P]
-                nc.tensor.matmul(dst, held[i][:, cols], ident[:], start=True, stop=False, is_transpose=True)
-                nc.tensor.matmul(dst, page[i % 2][:, cols], ident[:], start=False, stop=True, is_transpose=True)
-            nc.scalar.copy(
-                turned[c][:, :, i, :].rearrange("t b (m c e) -> t b m c e", c=RUN, e=2),
-                acc[:].rearrange("t (b m e c) -> t b m c e", b=BLOCKS, e=2, c=RUN),
-            )
-
-        def turn_back(c):
-            acc = bank("b")
-            words = turned[c][:].rearrange("t b s x -> t (b s x)").bitcast(F32)
-            for bl in range(BLOCKS):
-                cols = slice(bl * P, (bl + 1) * P)
-                nc.tensor.transpose(acc[:, cols], words[:, cols], ident[:])
-            nc.scalar.copy(pairs[c][:, 0, :], acc[:])
-
-        for c in range(CHUNKS):
-            add_turned(0, c)
-        scatter(2, trades2)
-        trades3 = trades_of(3, factors_of(3, "b", ["root2_1", "root1_1"]))
-        for c in range(CHUNKS):
-            add_turned(1, c)
-        scatter(3, trades3)
-        wr_g = sb([P, N * PACK], BF16, "wr_g", "root3_0")
+        factors2 = factors_of(2, "s", ["root0_1", "factor0_1"])
+        wr_g = sb([P, N * PACK], BF16, "wr_g", "root2_1")
         for b in range(N // P):
             nc.scalar.copy(
                 wr_g[:, half_cols(b)].rearrange("p (n i j) -> p n j i", i=4, j=PACK),
                 wr_raw[:, :, b * P : (b + 1) * P].rearrange("p j (n i) -> p n j i", i=4),
             )
-        wr_w = sb([P, N], U32, "wr_w")
+        damped2 = damped_of(2, factors2, "b")
+
+        factors3 = factors_of(3, "s", ["root0_1", "factor0_1"])
+        turned_tags = ["root2_0", "root3_0", "root0_1", "factor0_1"]
+        turned = [sb([P, BLOCKS, 2, P], BF16, f"turned{c}", turned_tags[c]) for c in range(CHUNKS)]
+        pairs = [sb([P, 2, BANK], F32, f"pairs{c}", f"wa_raw{c // 2}_{c % 2}") for c in range(CHUNKS)]
+
+        def turn_into(acc, src, c, identity, opens):
+            for bl in range(BLOCKS):
+                cols = slice(c * BANK + bl * P, c * BANK + (bl + 1) * P)
+                nc.tensor.matmul(
+                    acc[:, bl * P : (bl + 1) * P],
+                    src[:, cols],
+                    identity[:],
+                    start=opens and bl == 0,
+                    stop=not opens and bl == BLOCKS - 1,
+                    is_transpose=True,
+                )
+
+        def open_sum(i, c):
+            acc = bank("s")
+            turn_into(acc, held[i], c, ident, True)
+            return acc
+
+        def add_turned(i, c, acc, identity):
+            turn_into(acc, page[i % 2], c, identity, False)
+            if i < 2:
+                nc.scalar.copy(
+                    turned[c][:, :, i, :].rearrange("t b (m c e) -> t b m c e", c=RUN, e=2),
+                    acc[:].rearrange("t (b m e c) -> t b m c e", b=BLOCKS, e=2, c=RUN),
+                )
+            else:
+                nc.scalar.copy(
+                    turned[c][:].rearrange("t b s (x e) -> t b s x e", e=2)[:, :, :, :, 0],
+                    acc[:].rearrange("t (b s x) -> t b s x", b=BLOCKS, s=2),
+                )
+
+        def turn_back(u, c):
+            acc = bank("b")
+            words = turned[c][:].rearrange("t b s x -> t (b s x)").bitcast(F32)
+            for bl in range(BLOCKS):
+                cols = slice(bl * P, (bl + 1) * P)
+                nc.tensor.transpose(acc[:, cols], words[:, cols], ident[:])
+            nc.scalar.copy(pairs[c][:, u, :], acc[:])
+
+        for c in range(CHUNKS):
+            add_turned(0, c, open_sum(0, c), ident)
+        scatter(2, damped2)
+        damped3 = damped_of(3, factors3, "a", "root3_1")
+        wr_w = sb([P, N], U32, "wr_w", "factor3_0")
         wr_sc = sb([P, N], U8, "wr_sc")
         nc.vector.quantize_mx(out=wr_w[:].bitcast(FP8X4), scales=wr_sc[:], in_=wr_g[:])
         for c in range(CHUNKS):
-            turn_back(c)
+            add_turned(1, c, open_sum(1, c), ident)
+        scatter(3, damped3)
+        sums2 = []
+        for c in range(CHUNKS):
+            sums2.append(open_sum(2, c))
+            turn_back(0, c)
+        late_ident = sb([P, P], F32, "late_ident", "hold2")
+        nc.scalar.copy(late_ident[:], ident[:])
+        for c in range(CHUNKS):
+            add_turned(2, c, sums2[c], late_ident)
+        for c in range(CHUNKS):
+            turn_back(1, c)
 
         out_rows = out.rearrange("(b p) t -> p b t", p=P)
         stage_tags = ["tab_w0", "tab_w1", "hold0", "hold1"]
@@ -339,6 +370,8 @@ def tile_list_damped_trade_exposure_kernel(
         results = [sb([P, N // P * BANK], F32, f"result{c}", tag=stage_tags[c]) for c in range(CHUNKS)]
         starts = [sum(STRIPS[:k]) for k in range(len(STRIPS))]
         woven = {}
+        stored = []
+        left_to_vector = []
 
         def strip_words(k):
             c, at = divmod(starts[k], BANK)
@@ -347,8 +380,7 @@ def tile_list_damped_trade_exposure_kernel(
         def add_last(k):
             cols = slice(starts[k], starts[k] + STRIPS[k])
             halves = strip_words(k)[:, 1, :].bitcast(BF16).rearrange("p (t e) -> p t e", e=2)
-            for e in range(2):
-                nc.vector.tensor_tensor(halves[:, :, e], page[e][:, cols], held[2 + e][:, cols], ALU.add)
+            nc.vector.tensor_tensor(halves[:, :, 1], page[1][:, cols], held[3][:, cols], ALU.add)
 
         def weave(k):
             woven[k] = ring.tile([P, STRIPS[k], 2], F32, name="woven", align_bytes=64)
@@ -364,10 +396,9 @@ def tile_list_damped_trade_exposure_kernel(
                 scales=z_sc[:],
                 in_=woven[k][:].rearrange("p t u -> p (t u)").bitcast(BF16),
             )
-            per_bank = BANK // width
+            per_bank = min(BANK // width, 2 if k == 0 else N // P)
             for first in range(0, N // P, per_bank):
-                used = (starts[k] * (N // P) + first * width) // BANK
-                acc = bank(out_banks[used % len(out_banks)])
+                acc = bank(out_banks[len(stored) % len(out_banks)])
                 for b in range(first, first + per_bank):
                     rows = slice(b * P, (b + 1) * P)
                     nc.tensor.matmul_mx(
@@ -379,16 +410,16 @@ def tile_list_damped_trade_exposure_kernel(
                         start=True,
                         stop=True,
                     )
-                result = results[used // (N // P)][:, half_cols(used % (N // P))]
-                if used == CHUNKS * N // P - 1:
-                    negated = sb([P, BANK], F32, "negated")
-                    nc.vector.tensor_scalar(negated[:], acc[:], -1.0, None, ALU.mult)
-                    nc.vector.tensor_tensor(result, acc[:], negated[:], ALU.max)
+                c, at = divmod(starts[k] * (N // P) + first * width, N // P * BANK)
+                sums = acc[:, : per_bank * width]
+                result = results[c][:, at : at + per_bank * width]
+                dst = out_rows[:, first : first + per_bank, cols]
+                if k >= len(STRIPS) - 2 and first + per_bank == N // P:
+                    left_to_vector.append((dst, result, sums))
                 else:
-                    nc.scalar.activation(result, acc[:], ACT.Abs)
-                nc.sync.dma_start(
-                    out_rows[:, first : first + per_bank, cols], result.rearrange("p (b t) -> p b t", b=per_bank)
-                )
+                    nc.scalar.activation(result, sums, ACT.Abs)
+                    nc.sync.dma_start(dst, result.rearrange("p (b t) -> p b t", b=per_bank))
+                stored.append(result)
 
         add_last(0)
         add_last(1)
@@ -400,3 +431,9 @@ def tile_list_damped_trade_exposure_kernel(
             expose(k - 1)
             weave(k)
         expose(len(STRIPS) - 1)
+        negated = [sb([P, BANK], F32, f"negated{n}") for n in range(len(left_to_vector))]
+        for (dst, result, sums), minus in zip(left_to_vector, negated):
+            nc.vector.tensor_scalar(minus[:], sums, -1.0, None, ALU.mult)
+        for (dst, result, sums), minus in zip(left_to_vector, negated):
+            nc.vector.tensor_tensor(result, sums, minus[:], ALU.max)
+            nc.sync.dma_start(dst, result.rearrange("p (b t) -> p b t", b=dst.shape[1]))

@@ -27,7 +27,7 @@ BLOCKS = BANK // P
 QUAD = 32
 RUN = 4
 GROUP = PACK * RUN
-STRIPS = (128, 128, 256, 256, 256, 512, 256, 256)
+STRIPS = (128, 128, 256, 512, 512, 512)
 
 
 def tile_list_damped_trade_exposure_kernel(
@@ -414,7 +414,7 @@ def tile_list_damped_trade_exposure_kernel(
                 sums = acc[:, : per_bank * width]
                 result = results[c][:, at : at + per_bank * width]
                 dst = out_rows[:, first : first + per_bank, cols]
-                if k >= len(STRIPS) - 2 and first + per_bank == N // P:
+                if k == len(STRIPS) - 1 and first + per_bank == N // P:
                     left_to_vector.append((dst, result, sums))
                 else:
                     nc.scalar.activation(result, sums, ACT.Abs)

@@ -115,13 +115,12 @@ def tile_list_damped_trade_exposure_kernel(
         load_pair_weight(1)
         held = [load_hold(0)]
         weight = {2: load_weight(2)}
-        held.append(load_hold(1))
         wr_raw = sb([P, PACK, N], F32, "wr_raw")
         wr_rows = wr.rearrange("(m i c) n -> i m c n", i=PACK, c=RUN)
         for i in range(PACK):
             nc.sync.dma_start(wr_raw[:, i, :], wr_rows[i])
+        held.extend(load_hold(i) for i in (1, 2))
         weight[3] = load_weight(3)
-        held.append(load_hold(2))
         held.append(load_hold(3))
 
         warm = sb([P, 2], F32, "warm")
@@ -172,10 +171,7 @@ def tile_list_damped_trade_exposure_kernel(
         wa_w = {0: sb([P, PASSES * P], U32, "wa_w0")}
         wa_sc = {0: sb([P, PASSES * P], U8, "wa_sc0")}
 
-        def quantise_wa(g, grouped, cols=slice(None), tag=None):
-            if g not in wa_w:
-                wa_w[g] = sb([P, grouped.shape[1] // PACK], U32, f"wa_w{g}", tag)
-                wa_sc[g] = sb([P, grouped.shape[1] // PACK], U8, f"wa_sc{g}")
+        def quantise_wa(g, grouped, cols):
             nc.vector.quantize_mx(out=wa_w[g][:, cols].bitcast(FP8X4), scales=wa_sc[g][:, cols], in_=grouped)
 
         def product(tag, codes, scales, h):
@@ -227,8 +223,18 @@ def tile_list_damped_trade_exposure_kernel(
             nc.scalar.activation(factor[:], root[:], ACT.Square)
             return factor
 
-        def damped_half(i, h, factor):
-            damped = sb([P, BANK], F32, f"damped{i}_{h}")
+        def factor_in_pieces(i, h, size):
+            pieces = [slice(e * BANK // 2, (e + 1) * BANK // 2) for e in range(2)]
+            roots = [sb([P, BANK // 2], F32, f"root{i}_{h}{name}") for name in "ab"]
+            factor = sb([P, BANK], F32, f"factor{i}_{h}")
+            for root, cols in zip(roots, pieces):
+                nc.scalar.activation(root[:], size[:, cols], ACT.Abs_reciprocal_sqrt, bias=1.0)
+            for root, cols in zip(roots, pieces):
+                nc.scalar.activation(factor[:, cols], root[:], ACT.Square)
+            return factor
+
+        def damped_half(i, h, factor, tag=None):
+            damped = sb([P, BANK], F32, f"damped{i}_{h}", tag)
             nc.vector.tensor_tensor(damped[:], loadings(i, h, "a")[:], factor[:], ALU.mult)
             return damped
 
@@ -248,20 +254,17 @@ def tile_list_damped_trade_exposure_kernel(
 
         def scatter(i, damped):
             rows = pair_weight if i < 2 else weight[i]
-            nc.vector.tensor_tensor(page[i % 2][:].indirect(idx2[:]), damped[:], rows[:], ALU.mult)
+            nc.vector.tensor_tensor(page[i][:].indirect(idx2[:]), damped[:], rows[:], ALU.mult)
+
+        def clear_page(tag):
+            page.append(sb([P, T2], F32, f"page{len(page)}", tag))
+            nc.gpsimd.memset(page[-1][:], 0.0)
 
         grouped0 = [sb([P, BANK], BF16, f"wa_g0_{a}") for a in range(PASSES)]
         round_pair_slice(nc.scalar.copy, grouped0[0][:], 0, 0)
         round_late_slices(0, 0)
         wb_part = [deal(0)]
-        size00 = size_of(0, 0, "b", "wa_raw0_0")
-        roots00 = [sb([P, BANK // 2], F32, f"root0_0{name}") for name in ("", "b")]
-        factor00 = sb([P, BANK], F32, "factor0_0")
-        quarters = [slice(e * BANK // 2, (e + 1) * BANK // 2) for e in range(2)]
-        for e in range(2):
-            nc.scalar.activation(roots00[e][:], size00[:, quarters[e]], ACT.Abs_reciprocal_sqrt, bias=1.0)
-        for e in range(2):
-            nc.scalar.activation(factor00[:, quarters[e]], roots00[e][:], ACT.Square)
+        factor00 = factor_in_pieces(0, 0, size_of(0, 0, "b", "wa_raw0_0"))
         gather_scales(0, 1)
         quantise_wa(0, grouped0[0][:], slice(0, P))
         gather_words(1, 1)
@@ -270,38 +273,37 @@ def tile_list_damped_trade_exposure_kernel(
         quantise_wa(0, grouped0[1][:], slice(P, 2 * P))
         gather_scales(1, 1, "wa_g0_1")
         scatter_half(0, 0, damped_half(0, 0, factor00))
-        page.append(sb([P, T2], F32, "page1", "factor0_0"))
-        nc.gpsimd.memset(page[1][:], 0.0)
+        clear_page("factor0_0")
 
         factor10 = factor_of(1, 0, root_of(1, 0, size_of(1, 0, "b", "root0_0b")))
         round_late_slices(1, 0)
-        grouped1 = sb([P, PASSES * BANK], BF16, "wa_g1", "root0_0")
+        grouped1 = [sb([P, BANK], BF16, f"wa_g1_{a}", tag) for a, tag in enumerate(("root0_0a", "root0_1a"))]
+        round_pair_slice(nc.scalar.copy, grouped1[0][:], 0, 1)
+        factor01 = factor_in_pieces(0, 1, size_of(0, 1, "b", "root1_0"))
+        round_pair_slice(nc.scalar.copy, grouped1[1][:], 1, 1)
+        wa_w[1] = sb([P, PASSES * P], U32, "wa_w1", "damped0_0")
+        wa_sc[1] = sb([P, PASSES * P], U8, "wa_sc1")
         for a in range(PASSES):
-            round_pair_slice(nc.scalar.copy, grouped1[:, half_cols(a)], a, 1)
-        factor01 = factor_of(0, 1, root_of(0, 1, size_of(0, 1, "b", "root1_0")))
-        damped01 = damped_half(0, 1, factor01)
-        quantise_wa(1, grouped1[:], tag="damped0_0")
-        scatter_half(0, 1, damped01)
+            quantise_wa(1, grouped1[a][:], slice(a * P, (a + 1) * P))
+        scatter_half(0, 1, damped_half(0, 1, factor01, "root0_1a"))
+        clear_page("factor0_1")
 
         wb_part.append(deal(1, "root0_0b"))
         for a in range(PASSES):
             round_late_slices(a, 1)
-        factor11 = factor_of(1, 1, root_of(1, 1, size_of(1, 1, "b", "root0_1")))
+        factor11 = factor_of(1, 1, root_of(1, 1, size_of(1, 1, "b", "root0_1b")))
         damped1 = damped_of(1, [factor10, factor11], "a", "root1_1")
-        quantise_wa(2, grouped_late[:].rearrange("p a i s x -> p (a i s x)"), tag="factor1_0")
+        wa_w[2] = sb([P, PASSES * 2 * P], U32, "wa_w2", "factor1_0")
+        wa_sc[2] = sb([P, PASSES * 2 * P], U8, "wa_sc2")
+        quantise_wa(2, grouped_late[:].rearrange("p a i s x -> p (a i s x)"), slice(0, PASSES * 2 * P))
         scatter(1, damped1)
+        clear_page("wa_g_late")
 
-        factors2 = factors_of(2, "s", ["root0_1", "factor0_1"])
-        wr_g = sb([P, N * PACK], BF16, "wr_g", "root2_1")
-        for b in range(N // P):
-            nc.scalar.copy(
-                wr_g[:, half_cols(b)].rearrange("p (n i j) -> p n j i", i=4, j=PACK),
-                wr_raw[:, :, b * P : (b + 1) * P].rearrange("p j (n i) -> p n j i", i=4),
-            )
-        damped2 = damped_of(2, factors2, "b")
-
-        factors3 = factors_of(3, "s", ["root0_1", "factor0_1"])
-        turned_tags = ["root2_0", "root3_0", "root0_1", "factor0_1"]
+        factors2 = factors_of(2, "s", ["root0_1b", "root1_0"])
+        scatter(2, damped_of(2, factors2, "b"))
+        factors3 = factors_of(3, "s", ["root0_1b", "root1_0"])
+        scatter(3, damped_of(3, factors3, "a"))
+        turned_tags = ["root2_0", "root2_1", "root0_1b", "root1_0"]
         turned = [sb([P, BLOCKS, 2, P], BF16, f"turned{c}", turned_tags[c]) for c in range(CHUNKS)]
         pairs = [sb([P, 2, BANK], F32, f"pairs{c}", f"wa_raw{c // 2}_{c % 2}") for c in range(CHUNKS)]
 
@@ -323,7 +325,7 @@ def tile_list_damped_trade_exposure_kernel(
             return acc
 
         def add_turned(i, c, acc, identity):
-            turn_into(acc, page[i % 2], c, identity, False)
+            turn_into(acc, page[i], c, identity, False)
             if i < 2:
                 nc.scalar.copy(
                     turned[c][:, :, i, :].rearrange("t b (m c e) -> t b m c e", c=RUN, e=2),
@@ -345,14 +347,17 @@ def tile_list_damped_trade_exposure_kernel(
 
         for c in range(CHUNKS):
             add_turned(0, c, open_sum(0, c), ident)
-        scatter(2, damped2)
-        damped3 = damped_of(3, factors3, "a", "root3_1")
-        wr_w = sb([P, N], U32, "wr_w", "factor3_0")
+        wr_g = sb([P, N * PACK], BF16, "wr_g", "root3_0")
+        for b in range(N // P):
+            nc.scalar.copy(
+                wr_g[:, half_cols(b)].rearrange("p (n i j) -> p n j i", i=4, j=PACK),
+                wr_raw[:, :, b * P : (b + 1) * P].rearrange("p j (n i) -> p n j i", i=4),
+            )
+        wr_w = sb([P, N], U32, "wr_w")
         wr_sc = sb([P, N], U8, "wr_sc")
         nc.vector.quantize_mx(out=wr_w[:].bitcast(FP8X4), scales=wr_sc[:], in_=wr_g[:])
         for c in range(CHUNKS):
             add_turned(1, c, open_sum(1, c), ident)
-        scatter(3, damped3)
         sums2 = []
         for c in range(CHUNKS):
             sums2.append(open_sum(2, c))
@@ -380,7 +385,7 @@ def tile_list_damped_trade_exposure_kernel(
         def add_last(k):
             cols = slice(starts[k], starts[k] + STRIPS[k])
             halves = strip_words(k)[:, 1, :].bitcast(BF16).rearrange("p (t e) -> p t e", e=2)
-            nc.vector.tensor_tensor(halves[:, :, 1], page[1][:, cols], held[3][:, cols], ALU.add)
+            nc.vector.tensor_tensor(halves[:, :, 1], page[3][:, cols], held[3][:, cols], ALU.add)
 
         def weave(k):
             woven[k] = ring.tile([P, STRIPS[k], 2], F32, name="woven", align_bytes=64)

@@ -43,7 +43,7 @@ def tile_list_damped_trade_exposure_kernel(
             return keep.tile(shape, dtype, name=name, tag=tag or name, align_bytes=64)
 
         def bank(tag):
-            return psum.tile([P, BANK], F32, name=tag, tag=tag, bufs=4 if tag == "s" else 2)
+            return psum.tile([P, BANK], F32, name=tag, tag=tag, bufs=4 if tag == "s" else 1)
 
         def half_cols(h):
             return slice(h * BANK, (h + 1) * BANK)
@@ -142,11 +142,15 @@ def tile_list_damped_trade_exposure_kernel(
             v_sc[a, h] = sb([P, BANK], U8, f"v_sc{a}_{h}", tag)
             nc.vector.tensor_copy(v_sc[a, h][:], tab_sc[:, a * T : (a + 1) * T].indirect(half_list(idx, h)))
 
-        def deal(part, tag=None):
-            tile = sb([P, PASSES * 3 * H // 2], U8, f"wb_part{part}", tag)
-            for raw, dst, words in ((wb_raw, tile[:, : PASSES * H], 2), (wb_sc_raw, tile[:, PASSES * H :], 1)):
-                src = raw[:].bitcast(U32).rearrange("p (a m e i w) -> p e a i m w", a=PASSES, e=2, i=1 + part, w=2 * words // (1 + part))
-                nc.scalar.copy(dst.bitcast(U32).rearrange("p (a i m w) -> p a i m w", a=PASSES, i=1 + part, m=QUAD), src[:, part])
+        def deal(raw, name, words):
+            tile = sb([P, raw.shape[1]], U8, name)
+            src = raw[:].bitcast(U32).rearrange("p (a m w) -> p a m w", a=PASSES, w=PACK * words)
+            dst = tile[:].bitcast(U32).rearrange("p (a e x) -> p a e x", a=PASSES, e=2)
+            nc.scalar.copy(dst[:, :, 0, :].rearrange("p a (m w) -> p a m w", w=2 * words), src[:, :, :, : 2 * words])
+            nc.scalar.copy(
+                dst[:, :, 1, :].rearrange("p a (i m w) -> p a i m w", i=2, w=words),
+                src[:, :, :, 2 * words :].rearrange("p a m (i w) -> p a i m w", i=2),
+            )
             return tile
 
         gather_words(0, 0)
@@ -189,11 +193,10 @@ def tile_list_damped_trade_exposure_kernel(
             return acc
 
         def stress(i, h, tag):
-            words, scales = wb_part[i // 2][:, : PASSES * H], wb_part[i // 2][:, PASSES * H :]
             return product(
                 tag,
-                lambda a: words[:, 2 * (2 * a + i % 2) * P : 2 * (2 * a + i % 2 + 1) * P].bitcast(FP4X4),
-                lambda a: scales[:, (2 * a + i % 2) * P : (2 * a + i % 2 + 1) * P],
+                lambda a: wb_w[:, 2 * (a * PACK + i) * P : 2 * (a * PACK + i + 1) * P].bitcast(FP4X4),
+                lambda a: wb_sc[:, (a * PACK + i) * P : (a * PACK + i + 1) * P],
                 h,
             )
 
@@ -223,87 +226,89 @@ def tile_list_damped_trade_exposure_kernel(
             nc.scalar.activation(factor[:], root[:], ACT.Square)
             return factor
 
-        def factor_in_pieces(i, h, size):
+        def factor_in_pieces(i, h, bank_tag, tag):
             pieces = [slice(e * BANK // 2, (e + 1) * BANK // 2) for e in range(2)]
+            acc = stress(i, h, bank_tag)
+            size = sb([P, BANK], F32, f"size{i}_{h}", tag)
             roots = [sb([P, BANK // 2], F32, f"root{i}_{h}{name}") for name in "ab"]
             factor = sb([P, BANK], F32, f"factor{i}_{h}")
+            for cols in pieces:
+                nc.scalar.activation(size[:, cols], acc[:, cols], ACT.Abs)
             for root, cols in zip(roots, pieces):
                 nc.scalar.activation(root[:], size[:, cols], ACT.Abs_reciprocal_sqrt, bias=1.0)
             for root, cols in zip(roots, pieces):
                 nc.scalar.activation(factor[:, cols], root[:], ACT.Square)
             return factor
 
-        def damped_half(i, h, factor, tag=None):
+        def damped_half(i, h, factor, bank_tag, tag=None):
             damped = sb([P, BANK], F32, f"damped{i}_{h}", tag)
-            nc.vector.tensor_tensor(damped[:], loadings(i, h, "a")[:], factor[:], ALU.mult)
+            nc.vector.tensor_tensor(damped[:], loadings(i, h, bank_tag)[:], factor[:], ALU.mult)
             return damped
 
         def scatter_half(i, h, damped):
             nc.vector.tensor_tensor(page[i][:].indirect(half_list(idx2, h)), damped[:], pair_weight[:, half_cols(h)], ALU.mult)
 
-        def factors_of(i, bank_tag, tags):
-            sizes = [size_of(i, h, bank_tag, tags[h]) for h in range(HALVES)]
+        def factors_of(i, tags):
+            sizes = [size_of(i, h, f"p{h}", tags[h]) for h in range(HALVES)]
             roots = [root_of(i, h, sizes[h]) for h in range(HALVES)]
             return [factor_of(i, h, roots[h]) for h in range(HALVES)]
 
-        def damped_of(i, factors, bank_tag, tag=None):
-            damped = sb([P, S], F32, f"damped{i}", tag)
+        def damped_of(i, factors):
+            damped = sb([P, S], F32, f"damped{i}")
             for h in range(HALVES):
-                nc.vector.tensor_tensor(damped[:, half_cols(h)], loadings(i, h, bank_tag)[:], factors[h][:], ALU.mult)
+                nc.vector.tensor_tensor(damped[:, half_cols(h)], loadings(i, h, f"p{2 + h}")[:], factors[h][:], ALU.mult)
             return damped
 
         def scatter(i, damped):
-            rows = pair_weight if i < 2 else weight[i]
-            nc.vector.tensor_tensor(page[i][:].indirect(idx2[:]), damped[:], rows[:], ALU.mult)
+            nc.vector.tensor_tensor(page[i][:].indirect(idx2[:]), damped[:], weight[i][:], ALU.mult)
 
         def clear_page(tag):
             page.append(sb([P, T2], F32, f"page{len(page)}", tag))
             nc.gpsimd.memset(page[-1][:], 0.0)
 
+        wb_w = deal(wb_raw, "wb_w", 2)
+        wb_sc = deal(wb_sc_raw, "wb_sc", 1)
         grouped0 = [sb([P, BANK], BF16, f"wa_g0_{a}") for a in range(PASSES)]
         round_pair_slice(nc.scalar.copy, grouped0[0][:], 0, 0)
         round_late_slices(0, 0)
-        wb_part = [deal(0)]
-        factor00 = factor_in_pieces(0, 0, size_of(0, 0, "b", "wa_raw0_0"))
+        factor00 = factor_in_pieces(0, 0, "p0", "wa_raw0_0")
         gather_scales(0, 1)
-        quantise_wa(0, grouped0[0][:], slice(0, P))
         gather_words(1, 1)
+        quantise_wa(0, grouped0[0][:], slice(0, P))
         round_pair_slice(nc.vector.tensor_copy, grouped0[1][:], 1, 0)
         gather_words(0, 1, "wa_g0_0")
         quantise_wa(0, grouped0[1][:], slice(P, 2 * P))
         gather_scales(1, 1, "wa_g0_1")
-        scatter_half(0, 0, damped_half(0, 0, factor00))
+        scatter_half(0, 0, damped_half(0, 0, factor00, "p2"))
         clear_page("factor0_0")
 
-        factor10 = factor_of(1, 0, root_of(1, 0, size_of(1, 0, "b", "root0_0b")))
         round_late_slices(1, 0)
-        grouped1 = [sb([P, BANK], BF16, f"wa_g1_{a}", tag) for a, tag in enumerate(("root0_0a", "root0_1a"))]
-        round_pair_slice(nc.scalar.copy, grouped1[0][:], 0, 1)
-        factor01 = factor_in_pieces(0, 1, size_of(0, 1, "b", "root1_0"))
-        round_pair_slice(nc.scalar.copy, grouped1[1][:], 1, 1)
-        wa_w[1] = sb([P, PASSES * P], U32, "wa_w1", "damped0_0")
-        wa_sc[1] = sb([P, PASSES * P], U8, "wa_sc1")
+        grouped1 = sb([P, PASSES * BANK], BF16, "wa_g1", "root0_0a")
         for a in range(PASSES):
-            quantise_wa(1, grouped1[a][:], slice(a * P, (a + 1) * P))
-        scatter_half(0, 1, damped_half(0, 1, factor01, "root0_1a"))
+            round_pair_slice(nc.scalar.copy, grouped1[:, half_cols(a)], a, 1)
+        factor01 = factor_in_pieces(0, 1, "p1", "root0_0b")
+        wa_w[1] = sb([P, PASSES * P], U32, "wa_w1")
+        wa_sc[1] = sb([P, PASSES * P], U8, "wa_sc1")
+        quantise_wa(1, grouped1[:], slice(0, PASSES * P))
+        scatter_half(0, 1, damped_half(0, 1, factor01, "p0", "root0_0a"))
         clear_page("factor0_1")
 
-        wb_part.append(deal(1, "root0_0b"))
+        factor10 = factor_of(1, 0, root_of(1, 0, size_of(1, 0, "p1", "root0_1b")))
+        scatter_half(1, 0, damped_half(1, 0, factor10, "p2"))
+        factor11 = factor_of(1, 1, root_of(1, 1, size_of(1, 1, "p1", "root1_0")))
         for a in range(PASSES):
             round_late_slices(a, 1)
-        factor11 = factor_of(1, 1, root_of(1, 1, size_of(1, 1, "b", "root0_1b")))
-        damped1 = damped_of(1, [factor10, factor11], "a", "root1_1")
-        wa_w[2] = sb([P, PASSES * 2 * P], U32, "wa_w2", "factor1_0")
+        wa_w[2] = sb([P, PASSES * 2 * P], U32, "wa_w2")
         wa_sc[2] = sb([P, PASSES * 2 * P], U8, "wa_sc2")
         quantise_wa(2, grouped_late[:].rearrange("p a i s x -> p (a i s x)"), slice(0, PASSES * 2 * P))
-        scatter(1, damped1)
-        clear_page("wa_g_late")
+        scatter_half(1, 1, damped_half(1, 1, factor11, "p3", "wa_g_late"))
+        clear_page("factor1_1")
 
-        factors2 = factors_of(2, "s", ["root0_1b", "root1_0"])
-        scatter(2, damped_of(2, factors2, "b"))
-        factors3 = factors_of(3, "s", ["root0_1b", "root1_0"])
-        scatter(3, damped_of(3, factors3, "a"))
-        turned_tags = ["root2_0", "root2_1", "root0_1b", "root1_0"]
+        factors2 = factors_of(2, ["root1_1", "root0_1b"])
+        scatter(2, damped_of(2, factors2))
+        factors3 = factors_of(3, ["root1_1", "root0_1b"])
+        scatter(3, damped_of(3, factors3))
+        turned_tags = ["root2_0", "root2_1", "root1_1", "root0_1b"]
         turned = [sb([P, BLOCKS, 2, P], BF16, f"turned{c}", turned_tags[c]) for c in range(CHUNKS)]
         pairs = [sb([P, 2, BANK], F32, f"pairs{c}", f"wa_raw{c // 2}_{c % 2}") for c in range(CHUNKS)]
 
@@ -338,7 +343,7 @@ def tile_list_damped_trade_exposure_kernel(
                 )
 
         def turn_back(u, c):
-            acc = bank("b")
+            acc = bank(f"p{c % 2}")
             words = turned[c][:].rearrange("t b s x -> t (b s x)").bitcast(F32)
             for bl in range(BLOCKS):
                 cols = slice(bl * P, (bl + 1) * P)
@@ -371,7 +376,7 @@ def tile_list_damped_trade_exposure_kernel(
 
         out_rows = out.rearrange("(b p) t -> p b t", p=P)
         stage_tags = ["tab_w0", "tab_w1", "hold0", "hold1"]
-        out_banks = ["a", "a", "s", "s", "s", "s", "b", "b"]
+        out_banks = ["p2", "p3", "s", "s", "s", "s", "p0", "p1"]
         results = [sb([P, N // P * BANK], F32, f"result{c}", tag=stage_tags[c]) for c in range(CHUNKS)]
         starts = [sum(STRIPS[:k]) for k in range(len(STRIPS))]
         woven = {}

@@ -25,7 +25,7 @@ HALVES = S // BANK
 CHUNKS = T2 // BANK
 BLOCKS = BANK // P
 QUAD = 32
-RUN = 4
+RUN = 2
 GROUP = PACK * RUN
 STRIPS = (128, 128, 256, 512, 512, 512)
 
@@ -109,9 +109,9 @@ def tile_list_damped_trade_exposure_kernel(
         idx2 = keep.tile([P, S // 16], U16, name="idx2")
         nc.sync.dma_start(idx2[:], offs2)
         pair_weight = sb([P, S], F32, "pair_weight")
+        wa_raw[0, 1] = load_wa(0, 1)
         load_pair_weight(0)
-        for a in range(PASSES):
-            wa_raw[a, 1] = load_wa(a, 1)
+        wa_raw[1, 1] = load_wa(1, 1)
         load_pair_weight(1)
         held = [load_hold(0)]
         weight = {2: load_weight(2)}
@@ -142,15 +142,12 @@ def tile_list_damped_trade_exposure_kernel(
             v_sc[a, h] = sb([P, BANK], U8, f"v_sc{a}_{h}", tag)
             nc.vector.tensor_copy(v_sc[a, h][:], tab_sc[:, a * T : (a + 1) * T].indirect(half_list(idx, h)))
 
-        def deal(raw, name, words):
+        def deal(raw, name, run_dtype):
             tile = sb([P, raw.shape[1]], U8, name)
-            src = raw[:].bitcast(U32).rearrange("p (a m w) -> p a m w", a=PASSES, w=PACK * words)
-            dst = tile[:].bitcast(U32).rearrange("p (a e x) -> p a e x", a=PASSES, e=2)
-            nc.scalar.copy(dst[:, :, 0, :].rearrange("p a (m w) -> p a m w", w=2 * words), src[:, :, :, : 2 * words])
-            nc.scalar.copy(
-                dst[:, :, 1, :].rearrange("p a (i m w) -> p a i m w", i=2, w=words),
-                src[:, :, :, 2 * words :].rearrange("p a m (i w) -> p a i m w", i=2),
-            )
+            src = raw[:].bitcast(run_dtype).rearrange("p (a m e i) -> p e a m i", a=PASSES, e=2, i=2)
+            dst = tile[:].bitcast(run_dtype).rearrange("p (a e x) -> p e a x", a=PASSES, e=2)
+            nc.scalar.copy(dst[:, 0].rearrange("p a (m i) -> p a m i", i=2), src[:, 0])
+            nc.scalar.copy(dst[:, 1].rearrange("p a (i m) -> p a m i", i=2), src[:, 1])
             return tile
 
         gather_words(0, 0)
@@ -160,16 +157,16 @@ def tile_list_damped_trade_exposure_kernel(
 
         def round_pair_slice(copy, grouped, a, s):
             copy(
-                grouped.rearrange("p (m h c j) -> p m h j c", h=2, c=RUN, j=PACK),
-                wa_raw[a, s][:].rearrange("p j (m h c) -> p m h j c", h=PACK, c=RUN)[:, :, :2],
+                grouped.rearrange("p (m x j) -> p m j x", x=2 * RUN, j=PACK),
+                wa_raw[a, s][:].rearrange("p j (m e x) -> p e m j x", e=2, x=2 * RUN)[:, 0],
             )
 
         grouped_late = sb([P, PASSES, 2, 2, BANK // 2], BF16, "wa_g_late")
 
         def round_late_slices(a, s):
             nc.scalar.copy(
-                grouped_late[:, a, :, s, :].rearrange("p i (m c j) -> p i m j c", c=RUN, j=PACK),
-                wa_raw[a, s][:].rearrange("p j (m h c) -> p h m j c", h=PACK, c=RUN)[:, 2:],
+                grouped_late[:, a, :, s, :].rearrange("p i (m c j) -> p m j i c", c=RUN, j=PACK),
+                wa_raw[a, s][:].rearrange("p j (m e i c) -> p e m j i c", e=2, i=2, c=RUN)[:, 1],
             )
 
         wa_w = {0: sb([P, PASSES * P], U32, "wa_w0")}
@@ -266,8 +263,8 @@ def tile_list_damped_trade_exposure_kernel(
             page.append(sb([P, T2], F32, f"page{len(page)}", tag))
             nc.gpsimd.memset(page[-1][:], 0.0)
 
-        wb_w = deal(wb_raw, "wb_w", 2)
-        wb_sc = deal(wb_sc_raw, "wb_sc", 1)
+        wb_w = deal(wb_raw, "wb_w", U32)
+        wb_sc = deal(wb_sc_raw, "wb_sc", U16)
         grouped0 = [sb([P, BANK], BF16, f"wa_g0_{a}") for a in range(PASSES)]
         round_pair_slice(nc.scalar.copy, grouped0[0][:], 0, 0)
         round_late_slices(0, 0)

@@ -27,7 +27,7 @@ BLOCKS = BANK // P
 QUAD = 32
 RUN = 2
 GROUP = PACK * RUN
-STRIPS = (128, 128, 256, 512, 512, 512)
+STRIPS = (256, 256, 512, 512, 512)
 
 
 def tile_list_damped_trade_exposure_kernel(
@@ -403,7 +403,7 @@ def tile_list_damped_trade_exposure_kernel(
                 scales=z_sc[:],
                 in_=woven[k][:].rearrange("p t u -> p (t u)").bitcast(BF16),
             )
-            per_bank = min(BANK // width, 2 if k == 0 else N // P)
+            per_bank = BANK // width
             for first in range(0, N // P, per_bank):
                 acc = bank(out_banks[len(stored) % len(out_banks)])
                 for b in range(first, first + per_bank):
@@ -433,11 +433,13 @@ def tile_list_damped_trade_exposure_kernel(
         weave(0)
         weave(1)
         expose(0)
+        add_last(2)
+        expose(1)
         for k in range(2, len(STRIPS)):
-            add_last(k)
-            expose(k - 1)
             weave(k)
-        expose(len(STRIPS) - 1)
+            expose(k)
+            if k + 1 < len(STRIPS):
+                add_last(k + 1)
         negated = [sb([P, BANK], F32, f"negated{n}") for n in range(len(left_to_vector))]
         for (dst, result, sums), minus in zip(left_to_vector, negated):
             nc.vector.tensor_scalar(minus[:], sums, -1.0, None, ALU.mult)

@@ -250,10 +250,10 @@ def tile_list_damped_trade_exposure_kernel(
             roots = [root_of(i, h, sizes[h]) for h in range(HALVES)]
             return [factor_of(i, h, roots[h]) for h in range(HALVES)]
 
-        def damped_of(i, factors):
+        def damped_of(i, factors, banks):
             damped = sb([P, S], F32, f"damped{i}")
             for h in range(HALVES):
-                nc.vector.tensor_tensor(damped[:, half_cols(h)], loadings(i, h, f"p{2 + h}")[:], factors[h][:], ALU.mult)
+                nc.vector.tensor_tensor(damped[:, half_cols(h)], loadings(i, h, banks[h])[:], factors[h][:], ALU.mult)
             return damped
 
         def scatter(i, damped):
@@ -271,10 +271,10 @@ def tile_list_damped_trade_exposure_kernel(
         factor00 = factor_in_pieces(0, 0, "p0", "wa_raw0_0")
         gather_scales(0, 1)
         gather_words(1, 1)
-        quantise_wa(0, grouped0[0][:], slice(0, P))
+        gather_words(0, 1, "wb_sc_raw")
         round_pair_slice(nc.vector.tensor_copy, grouped0[1][:], 1, 0)
-        gather_words(0, 1, "wa_g0_0")
-        quantise_wa(0, grouped0[1][:], slice(P, 2 * P))
+        for a in range(PASSES):
+            quantise_wa(0, grouped0[a][:], slice(a * P, (a + 1) * P))
         gather_scales(1, 1, "wa_g0_1")
         scatter_half(0, 0, damped_half(0, 0, factor00, "p2"))
         clear_page("factor0_0")
@@ -302,9 +302,9 @@ def tile_list_damped_trade_exposure_kernel(
         clear_page("factor1_1")
 
         factors2 = factors_of(2, ["root1_1", "root0_1b"])
-        scatter(2, damped_of(2, factors2))
+        scatter(2, damped_of(2, factors2, ["p2", "p3"]))
         factors3 = factors_of(3, ["root1_1", "root0_1b"])
-        scatter(3, damped_of(3, factors3))
+        scatter(3, damped_of(3, factors3, ["p0", "p1"]))
         turned_tags = ["root2_0", "root2_1", "root1_1", "root0_1b"]
         turned = [sb([P, BLOCKS, 2, P], BF16, f"turned{c}", turned_tags[c]) for c in range(CHUNKS)]
         pairs = [sb([P, 2, BANK], F32, f"pairs{c}", f"wa_raw{c // 2}_{c % 2}") for c in range(CHUNKS)]
@@ -340,7 +340,7 @@ def tile_list_damped_trade_exposure_kernel(
                 )
 
         def turn_back(u, c):
-            acc = bank(f"p{c % 2}")
+            acc = bank(f"p{2 + c % 2}")
             words = turned[c][:].rearrange("t b s x -> t (b s x)").bitcast(F32)
             for bl in range(BLOCKS):
                 cols = slice(bl * P, (bl + 1) * P)
@@ -373,7 +373,7 @@ def tile_list_damped_trade_exposure_kernel(
 
         out_rows = out.rearrange("(b p) t -> p b t", p=P)
         stage_tags = ["tab_w0", "tab_w1", "hold0", "hold1"]
-        out_banks = ["p2", "p3", "s", "s", "s", "s", "p0", "p1"]
+        out_banks = ["p0", "p1", "s", "s", "s", "s", "p2", "p3"]
         results = [sb([P, N // P * BANK], F32, f"result{c}", tag=stage_tags[c]) for c in range(CHUNKS)]
         starts = [sum(STRIPS[:k]) for k in range(len(STRIPS))]
         woven = {}
@@ -403,7 +403,7 @@ def tile_list_damped_trade_exposure_kernel(
                 scales=z_sc[:],
                 in_=woven[k][:].rearrange("p t u -> p (t u)").bitcast(BF16),
             )
-            per_bank = BANK // width
+            per_bank = 1 if k == 0 else BANK // width
             for first in range(0, N // P, per_bank):
                 acc = bank(out_banks[len(stored) % len(out_banks)])
                 for b in range(first, first + per_bank):

@@ -57,8 +57,7 @@ def tile_list_damped_trade_exposure_kernel(
         def load_scales(src, name):
             width = src.shape[2]
             tile = sb([P, PASSES * width], U8, name)
-            nc.vector.memset(tile[:, :width].bitcast(I32), 0)
-            nc.gpsimd.memset(tile[:, width:].bitcast(I32), 0)
+            nc.gpsimd.memset(tile[:].bitcast(I32), 0)
             rows = src.bitcast(I32).rearrange("a (q r) c -> r q a c", r=4)
             for r in range(4):
                 nc.sync.dma_start(tile[r:P:QUAD, :].bitcast(I32).rearrange("q (a c) -> q a c", a=PASSES), rows[r])
@@ -97,17 +96,21 @@ def tile_list_damped_trade_exposure_kernel(
             return tile
 
         tab_w = [load_tab(0)]
+        idx2 = keep.tile([P, S // 16], U16, name="idx2")
+        nc.sync.dma_start(idx2[:], offs2)
+        tab_sc = sb([P, T], U8, "tab_sc")
+        nc.vector.memset(tab_sc[:].bitcast(I32), 0)
+        tab_sc_rows = tab_scales.bitcast(I32).rearrange("a (q r) c -> r q a c", r=4)
+        for r in range(4):
+            nc.sync.dma_start(tab_sc[r : P : QUAD // 2, :].bitcast(I32), tab_sc_rows[r])
+        tab_w.append(load_tab(1))
         wb_raw = sb([P, PASSES * 2 * H], U8, "wb_raw")
         nc.sync.dma_start(
             wb_raw[:].bitcast(I32).rearrange("p (a c) -> p a c", a=PASSES),
             wb_words.bitcast(I32).rearrange("a p c -> p a c"),
         )
-        tab_sc = load_scales(tab_scales, "tab_sc")
-        tab_w.append(load_tab(1))
         wb_sc_raw = load_scales(wb_scales, "wb_sc_raw")
         wa_raw = {(a, 0): load_wa(a, 0) for a in range(PASSES)}
-        idx2 = keep.tile([P, S // 16], U16, name="idx2")
-        nc.sync.dma_start(idx2[:], offs2)
         pair_weight = sb([P, S], F32, "pair_weight")
         wa_raw[0, 1] = load_wa(0, 1)
         load_pair_weight(0)
@@ -129,18 +132,21 @@ def tile_list_damped_trade_exposure_kernel(
         ident = sb([P, P], F32, "ident")
         make_identity(nc, ident[:])
 
+        lowered = sb([P, S], U8, "lowered")
+        nc.vector.memset(lowered[:].bitcast(I32), 0)
         page = [sb([P, T2], F32, "page0")]
         nc.vector.memset(page[0][:], 0.0)
 
-        v_w, v_sc = {}, {}
+        v_w = {}
+        picked = sb([P, S], U8, "picked")
+        nc.vector.tensor_copy(picked[:], tab_sc[:].indirect(idx[:]))
+        for r in range(4):
+            nc.scalar.dma_start(lowered[r:P:QUAD, :].bitcast(I32), picked[QUAD // 2 + r : P : QUAD, :].bitcast(I32))
+        v_sc = [picked, lowered]
 
         def gather_words(a, h, tag=None):
             v_w[a, h] = sb([P, BANK], U32, f"v_w{a}_{h}", tag)
             nc.vector.tensor_copy(v_w[a, h][:], tab_w[a][:].indirect(half_list(idx, h)))
-
-        def gather_scales(a, h, tag=None):
-            v_sc[a, h] = sb([P, BANK], U8, f"v_sc{a}_{h}", tag)
-            nc.vector.tensor_copy(v_sc[a, h][:], tab_sc[:, a * T : (a + 1) * T].indirect(half_list(idx, h)))
 
         def deal(raw, name, run_dtype):
             tile = sb([P, raw.shape[1]], U8, name)
@@ -151,8 +157,6 @@ def tile_list_damped_trade_exposure_kernel(
             return tile
 
         gather_words(0, 0)
-        for a in range(PASSES):
-            gather_scales(a, 0)
         gather_words(1, 0)
 
         def round_pair_slice(copy, grouped, a, s):
@@ -183,7 +187,7 @@ def tile_list_damped_trade_exposure_kernel(
                     lhsT=codes(a),
                     lhsT_scale=scales(a),
                     rhs=v_w[a, h][:].bitcast(FP8X4),
-                    rhs_scale=v_sc[a, h][:],
+                    rhs_scale=v_sc[a][:, half_cols(h)],
                     start=(a == 0),
                     stop=(a == PASSES - 1),
                 )
@@ -269,13 +273,11 @@ def tile_list_damped_trade_exposure_kernel(
         round_pair_slice(nc.scalar.copy, grouped0[0][:], 0, 0)
         round_late_slices(0, 0)
         factor00 = factor_in_pieces(0, 0, "p0", "wa_raw0_0")
-        gather_scales(0, 1)
-        gather_words(1, 1)
         gather_words(0, 1, "wb_sc_raw")
         round_pair_slice(nc.vector.tensor_copy, grouped0[1][:], 1, 0)
         for a in range(PASSES):
             quantise_wa(0, grouped0[a][:], slice(a * P, (a + 1) * P))
-        gather_scales(1, 1, "wa_g0_1")
+        gather_words(1, 1, "wa_g0_1")
         scatter_half(0, 0, damped_half(0, 0, factor00, "p2"))
         clear_page("factor0_0")
 

@@ -104,6 +104,12 @@ def tile_list_damped_trade_exposure_kernel(
         for r in range(4):
             nc.sync.dma_start(tab_sc[r : P : QUAD // 2, :].bitcast(I32), tab_sc_rows[r])
         tab_w.append(load_tab(1))
+        lowered = sb([P, S], U8, "lowered")
+        nc.vector.memset(lowered[:].bitcast(I32), 0)
+        picked = sb([P, S], U8, "picked")
+        nc.vector.tensor_copy(picked[:], tab_sc[:].indirect(idx[:]))
+        nc.scalar.dma_start(lowered[: P - QUAD // 2, :].bitcast(I32), picked[QUAD // 2 :, :].bitcast(I32))
+        v_sc = [picked, lowered]
         wb_raw = sb([P, PASSES * 2 * H], U8, "wb_raw")
         nc.sync.dma_start(
             wb_raw[:].bitcast(I32).rearrange("p (a c) -> p a c", a=PASSES),
@@ -132,17 +138,10 @@ def tile_list_damped_trade_exposure_kernel(
         ident = sb([P, P], F32, "ident")
         make_identity(nc, ident[:])
 
-        lowered = sb([P, S], U8, "lowered")
-        nc.vector.memset(lowered[:].bitcast(I32), 0)
         page = [sb([P, T2], F32, "page0")]
         nc.vector.memset(page[0][:], 0.0)
 
         v_w = {}
-        picked = sb([P, S], U8, "picked")
-        nc.vector.tensor_copy(picked[:], tab_sc[:].indirect(idx[:]))
-        for r in range(4):
-            nc.scalar.dma_start(lowered[r:P:QUAD, :].bitcast(I32), picked[QUAD // 2 + r : P : QUAD, :].bitcast(I32))
-        v_sc = [picked, lowered]
 
         def gather_words(a, h, tag=None):
             v_w[a, h] = sb([P, BANK], U32, f"v_w{a}_{h}", tag)
@@ -156,7 +155,7 @@ def tile_list_damped_trade_exposure_kernel(
             nc.scalar.copy(dst[:, 1].rearrange("p a (i m) -> p a m i", i=2), src[:, 1])
             return tile
 
-        gather_words(0, 0)
+        gather_words(0, 0, "tab_sc")
         gather_words(1, 0)
 
         def round_pair_slice(copy, grouped, a, s):

@@ -37,6 +37,7 @@ def tile_list_damped_trade_exposure_kernel(
     with ExitStack() as ctx:
         keep = ctx.enter_context(tc.tile_pool(name="keep", bufs=1))
         ring = ctx.enter_context(tc.tile_pool(name="ring", bufs=2))
+        shared = ctx.enter_context(tc.tile_pool(name="shared", bufs=1))
         psum = ctx.enter_context(tc.psum_pool(name="psum", bufs=1))
 
         def sb(shape, dtype, name, tag=None):
@@ -64,7 +65,10 @@ def tile_list_damped_trade_exposure_kernel(
             return tile
 
         def load_tab(a):
-            tile = sb([P, T], U32, f"tab_w{a}")
+            if a == 0:
+                tile = sb([P, T], U32, "tab_w0")
+            else:
+                tile = shared.tile([P, T], U32, name="tab_w1", align_bytes=64, offset=0)
             nc.sync.dma_start(tile[:].bitcast(I32), tab_words[a].rearrange("p t i -> p (t i)").bitcast(I32))
             return tile
 
@@ -95,26 +99,25 @@ def tile_list_damped_trade_exposure_kernel(
             nc.sync.dma_start(tile[:], rows)
             return tile
 
-        tab_w = [load_tab(0)]
         idx2 = keep.tile([P, S // 16], U16, name="idx2")
         nc.sync.dma_start(idx2[:], offs2)
+        wb_raw = sb([P, PASSES * 2 * H], U8, "wb_raw")
+        nc.sync.dma_start(
+            wb_raw[:].bitcast(I32).rearrange("p (a c) -> p a c", a=PASSES),
+            wb_words.bitcast(I32).rearrange("a p c -> p a c"),
+        )
         tab_sc = sb([P, T], U8, "tab_sc")
         nc.vector.memset(tab_sc[:].bitcast(I32), 0)
         tab_sc_rows = tab_scales.bitcast(I32).rearrange("a (q r) c -> r q a c", r=4)
         for r in range(4):
             nc.sync.dma_start(tab_sc[r : P : QUAD // 2, :].bitcast(I32), tab_sc_rows[r])
-        tab_w.append(load_tab(1))
+        tab_w = [load_tab(a) for a in range(PASSES)]
         lowered = sb([P, S], U8, "lowered")
         nc.vector.memset(lowered[:].bitcast(I32), 0)
         picked = sb([P, S], U8, "picked")
         nc.vector.tensor_copy(picked[:], tab_sc[:].indirect(idx[:]))
         nc.scalar.dma_start(lowered[: P - QUAD // 2, :].bitcast(I32), picked[QUAD // 2 :, :].bitcast(I32))
         v_sc = [picked, lowered]
-        wb_raw = sb([P, PASSES * 2 * H], U8, "wb_raw")
-        nc.sync.dma_start(
-            wb_raw[:].bitcast(I32).rearrange("p (a c) -> p a c", a=PASSES),
-            wb_words.bitcast(I32).rearrange("a p c -> p a c"),
-        )
         wb_sc_raw = load_scales(wb_scales, "wb_sc_raw")
         wa_raw = {(a, 0): load_wa(a, 0) for a in range(PASSES)}
         pair_weight = sb([P, S], F32, "pair_weight")
@@ -155,8 +158,9 @@ def tile_list_damped_trade_exposure_kernel(
             nc.scalar.copy(dst[:, 1].rearrange("p a (i m) -> p a m i", i=2), src[:, 1])
             return tile
 
-        gather_words(0, 0, "tab_sc")
-        gather_words(1, 0)
+        for a in range(PASSES):
+            for h in range(HALVES):
+                gather_words(a, h)
 
         def round_pair_slice(copy, grouped, a, s):
             copy(
@@ -172,7 +176,7 @@ def tile_list_damped_trade_exposure_kernel(
                 wa_raw[a, s][:].rearrange("p j (m e i c) -> p e m j i c", e=2, i=2, c=RUN)[:, 1],
             )
 
-        wa_w = {0: sb([P, PASSES * P], U32, "wa_w0")}
+        wa_w = {0: shared.tile([P, PASSES * P], U32, name="wa_w0", align_bytes=64, offset=0)}
         wa_sc = {0: sb([P, PASSES * P], U8, "wa_sc0")}
 
         def quantise_wa(g, grouped, cols):
@@ -216,8 +220,8 @@ def tile_list_damped_trade_exposure_kernel(
             nc.scalar.activation(size[:], acc[:], ACT.Abs)
             return size
 
-        def root_of(i, h, size):
-            root = sb([P, BANK], F32, f"root{i}_{h}")
+        def root_of(i, h, size, tag=None):
+            root = sb([P, BANK], F32, f"root{i}_{h}", tag)
             nc.scalar.activation(root[:], size[:], ACT.Abs_reciprocal_sqrt, bias=1.0)
             return root
 
@@ -268,32 +272,31 @@ def tile_list_damped_trade_exposure_kernel(
 
         wb_w = deal(wb_raw, "wb_w", U32)
         wb_sc = deal(wb_sc_raw, "wb_sc", U16)
-        grouped0 = [sb([P, BANK], BF16, f"wa_g0_{a}") for a in range(PASSES)]
+        grouped0 = [sb([P, BANK], BF16, "wa_g0_0"), shared.tile([P, BANK], BF16, name="wa_g0_1", align_bytes=64, offset=1024)]
         round_pair_slice(nc.scalar.copy, grouped0[0][:], 0, 0)
         round_late_slices(0, 0)
         factor00 = factor_in_pieces(0, 0, "p0", "wa_raw0_0")
-        gather_words(0, 1, "wb_sc_raw")
+        size10 = size_of(1, 0, "p1", "root0_0a")
         round_pair_slice(nc.vector.tensor_copy, grouped0[1][:], 1, 0)
         for a in range(PASSES):
             quantise_wa(0, grouped0[a][:], slice(a * P, (a + 1) * P))
-        gather_words(1, 1, "wa_g0_1")
         scatter_half(0, 0, damped_half(0, 0, factor00, "p2"))
         clear_page("factor0_0")
 
         round_late_slices(1, 0)
-        grouped1 = sb([P, PASSES * BANK], BF16, "wa_g1", "root0_0a")
+        grouped1 = sb([P, PASSES * BANK], BF16, "wa_g1", "root0_0b")
         for a in range(PASSES):
             round_pair_slice(nc.scalar.copy, grouped1[:, half_cols(a)], a, 1)
-        factor01 = factor_in_pieces(0, 1, "p1", "root0_0b")
+        factor01 = factor_in_pieces(0, 1, "p1", None)
         wa_w[1] = sb([P, PASSES * P], U32, "wa_w1")
         wa_sc[1] = sb([P, PASSES * P], U8, "wa_sc1")
         quantise_wa(1, grouped1[:], slice(0, PASSES * P))
-        scatter_half(0, 1, damped_half(0, 1, factor01, "p0", "root0_0a"))
+        scatter_half(0, 1, damped_half(0, 1, factor01, "p0", "root0_0b"))
         clear_page("factor0_1")
 
-        factor10 = factor_of(1, 0, root_of(1, 0, size_of(1, 0, "p1", "root0_1b")))
+        factor10 = factor_of(1, 0, root_of(1, 0, size10, "root0_1b"))
         scatter_half(1, 0, damped_half(1, 0, factor10, "p2"))
-        factor11 = factor_of(1, 1, root_of(1, 1, size_of(1, 1, "p1", "root1_0")))
+        factor11 = factor_of(1, 1, root_of(1, 1, size_of(1, 1, "p1", "root0_1b")))
         for a in range(PASSES):
             round_late_slices(a, 1)
         wa_w[2] = sb([P, PASSES * 2 * P], U32, "wa_w2")
@@ -373,7 +376,7 @@ def tile_list_damped_trade_exposure_kernel(
             turn_back(1, c)
 
         out_rows = out.rearrange("(b p) t -> p b t", p=P)
-        stage_tags = ["tab_w0", "tab_w1", "hold0", "hold1"]
+        stage_tags = ["tab_w0", "page0", "hold0", "hold1"]
         out_banks = ["p0", "p1", "s", "s", "s", "s", "p2", "p3"]
         results = [sb([P, N // P * BANK], F32, f"result{c}", tag=stage_tags[c]) for c in range(CHUNKS)]
         starts = [sum(STRIPS[:k]) for k in range(len(STRIPS))]

@@ -43,8 +43,11 @@ def tile_list_damped_trade_exposure_kernel(
         def sb(shape, dtype, name, tag=None):
             return keep.tile(shape, dtype, name=name, tag=tag or name, align_bytes=64)
 
+        def placed(shape, dtype, name, offset):
+            return shared.tile(shape, dtype, name=name, align_bytes=64, offset=offset)
+
         def bank(tag):
-            return psum.tile([P, BANK], F32, name=tag, tag=tag, bufs=4 if tag == "s" else 1)
+            return psum.tile([P, BANK], F32, name=tag, tag=tag)
 
         def half_cols(h):
             return slice(h * BANK, (h + 1) * BANK)
@@ -73,7 +76,10 @@ def tile_list_damped_trade_exposure_kernel(
             return tile
 
         def load_wa(a, s):
-            tile = sb([P, PACK, H // 2], F32, f"wa_raw{a}_{s}")
+            if (a, s) == (1, 1):
+                tile = placed([P, PACK, H // 2], F32, "wa_raw1_1", 20480)
+            else:
+                tile = sb([P, PACK, H // 2], F32, f"wa_raw{a}_{s}")
             rows = wa[a * P * PACK : (a + 1) * P * PACK, s * H // 2 : (s + 1) * H // 2]
             nc.sync.dma_start(tile[:], rows.rearrange("(p j) c -> p j c", j=PACK))
             return tile
@@ -214,22 +220,6 @@ def tile_list_damped_trade_exposure_kernel(
                 h,
             )
 
-        def size_of(i, h, bank_tag, tag=None):
-            acc = stress(i, h, bank_tag)
-            size = sb([P, BANK], F32, f"size{i}_{h}", tag)
-            nc.scalar.activation(size[:], acc[:], ACT.Abs)
-            return size
-
-        def root_of(i, h, size, tag=None):
-            root = sb([P, BANK], F32, f"root{i}_{h}", tag)
-            nc.scalar.activation(root[:], size[:], ACT.Abs_reciprocal_sqrt, bias=1.0)
-            return root
-
-        def factor_of(i, h, root):
-            factor = sb([P, BANK], F32, f"factor{i}_{h}")
-            nc.scalar.activation(factor[:], root[:], ACT.Square)
-            return factor
-
         def factor_in_pieces(i, h, bank_tag, tag):
             pieces = [slice(e * BANK // 2, (e + 1) * BANK // 2) for e in range(2)]
             acc = stress(i, h, bank_tag)
@@ -252,20 +242,6 @@ def tile_list_damped_trade_exposure_kernel(
         def scatter_half(i, h, damped):
             nc.vector.tensor_tensor(page[i][:].indirect(half_list(idx2, h)), damped[:], pair_weight[:, half_cols(h)], ALU.mult)
 
-        def factors_of(i, tags):
-            sizes = [size_of(i, h, f"p{h}", tags[h]) for h in range(HALVES)]
-            roots = [root_of(i, h, sizes[h]) for h in range(HALVES)]
-            return [factor_of(i, h, roots[h]) for h in range(HALVES)]
-
-        def damped_of(i, factors, banks):
-            damped = sb([P, S], F32, f"damped{i}")
-            for h in range(HALVES):
-                nc.vector.tensor_tensor(damped[:, half_cols(h)], loadings(i, h, banks[h])[:], factors[h][:], ALU.mult)
-            return damped
-
-        def scatter(i, damped):
-            nc.vector.tensor_tensor(page[i][:].indirect(idx2[:]), damped[:], weight[i][:], ALU.mult)
-
         def clear_page(tag):
             page.append(sb([P, T2], F32, f"page{len(page)}", tag))
             nc.gpsimd.memset(page[-1][:], 0.0)
@@ -276,7 +252,8 @@ def tile_list_damped_trade_exposure_kernel(
         round_pair_slice(nc.scalar.copy, grouped0[0][:], 0, 0)
         round_late_slices(0, 0)
         factor00 = factor_in_pieces(0, 0, "p0", "wa_raw0_0")
-        size10 = size_of(1, 0, "p1", "root0_0a")
+        sizes1 = sb([P, S], F32, "sizes1", "root0_0a")
+        nc.scalar.activation(sizes1[:, half_cols(0)], stress(1, 0, "p1")[:], ACT.Abs)
         round_pair_slice(nc.vector.tensor_copy, grouped0[1][:], 1, 0)
         for a in range(PASSES):
             quantise_wa(0, grouped0[a][:], slice(a * P, (a + 1) * P))
@@ -294,24 +271,46 @@ def tile_list_damped_trade_exposure_kernel(
         scatter_half(0, 1, damped_half(0, 1, factor01, "p0", "root0_0b"))
         clear_page("factor0_1")
 
-        factor10 = factor_of(1, 0, root_of(1, 0, size10, "root0_1b"))
-        scatter_half(1, 0, damped_half(1, 0, factor10, "p2"))
-        factor11 = factor_of(1, 1, root_of(1, 1, size_of(1, 1, "p1", "root0_1b")))
-        for a in range(PASSES):
-            round_late_slices(a, 1)
-        wa_w[2] = sb([P, PASSES * 2 * P], U32, "wa_w2")
+        def squares(i, roots):
+            factors = [sb([P, BANK], F32, f"factor{i}_{h}") for h in range(HALVES)]
+            for h in range(HALVES):
+                nc.scalar.activation(factors[h][:], roots[:, half_cols(h)], ACT.Square)
+            return factors
+
+        def wide_factor(i, sizes, roots, width):
+            for at in range(0, S, width):
+                nc.scalar.activation(roots[:, at : at + width], sizes[:, at : at + width], ACT.Abs_reciprocal_sqrt, bias=1.0)
+            return squares(i, roots)
+
+        def fill_sizes(i, sizes):
+            for h in range(HALVES):
+                nc.scalar.activation(sizes[:, half_cols(h)], stress(i, h, f"p{h}")[:], ACT.Abs)
+            return sizes
+
+        def damped_of(i, factor, banks, damped):
+            for h in range(HALVES):
+                nc.vector.tensor_tensor(damped[:, half_cols(h)], loadings(i, h, banks[h])[:], factor[h][:], ALU.mult)
+            return damped
+
+        def scatter(i, damped, weights):
+            nc.vector.tensor_tensor(page[i][:].indirect(idx2[:]), damped[:], weights[:], ALU.mult)
+
+        nc.scalar.activation(sizes1[:, half_cols(1)], stress(1, 1, "p1")[:], ACT.Abs)
+        round_late_slices(0, 1)
+        roots1 = placed([P, S], F32, "roots1", 12288)
+        nc.scalar.activation(roots1[:], sizes1[:], ACT.Abs_reciprocal_sqrt, bias=1.0)
+        round_late_slices(1, 1)
+        factor1 = squares(1, roots1)
+        damped1 = damped_of(1, factor1, ["p2", "p3"], placed([P, S], F32, "damped1", 12352 - 4096))
+        wa_w[2] = sb([P, PASSES * 2 * P], U32, "wa_w2", "factor1_0")
         wa_sc[2] = sb([P, PASSES * 2 * P], U8, "wa_sc2")
         quantise_wa(2, grouped_late[:].rearrange("p a i s x -> p (a i s x)"), slice(0, PASSES * 2 * P))
-        scatter_half(1, 1, damped_half(1, 1, factor11, "p3", "wa_g_late"))
+        scatter(1, damped1, pair_weight)
         clear_page("factor1_1")
 
-        factors2 = factors_of(2, ["root1_1", "root0_1b"])
-        scatter(2, damped_of(2, factors2, ["p2", "p3"]))
-        factors3 = factors_of(3, ["root1_1", "root0_1b"])
-        scatter(3, damped_of(3, factors3, ["p0", "p1"]))
-        turned_tags = ["root2_0", "root2_1", "root1_1", "root0_1b"]
-        turned = [sb([P, BLOCKS, 2, P], BF16, f"turned{c}", turned_tags[c]) for c in range(CHUNKS)]
-        pairs = [sb([P, 2, BANK], F32, f"pairs{c}", f"wa_raw{c // 2}_{c % 2}") for c in range(CHUNKS)]
+        turned_at = [12352, 16320, 20480, 22528]
+        turned = [placed([P, BLOCKS, 2, P], BF16, f"turned{c}", turned_at[c]) for c in range(CHUNKS)]
+        pairs = [sb([P, 2, BANK], F32, f"pairs{c}", ["wa_raw0_0", "wa_raw0_1", "wa_raw1_0", "wa_raw1_1"][c]) for c in range(CHUNKS)]
 
         def turn_into(acc, src, c, identity, opens):
             for bl in range(BLOCKS):
@@ -326,7 +325,7 @@ def tile_list_damped_trade_exposure_kernel(
                 )
 
         def open_sum(i, c):
-            acc = bank("s")
+            acc = bank(["p4", "p5", "p6", "p7"][c] if i == 0 else ["p6", "p7", "p2", "p4"][c])
             turn_into(acc, held[i], c, ident, True)
             return acc
 
@@ -344,7 +343,7 @@ def tile_list_damped_trade_exposure_kernel(
                 )
 
         def turn_back(u, c):
-            acc = bank(f"p{2 + c % 2}")
+            acc = bank(["p3", "p5"][c % 2])
             words = turned[c][:].rearrange("t b s x -> t (b s x)").bitcast(F32)
             for bl in range(BLOCKS):
                 cols = slice(bl * P, (bl + 1) * P)
@@ -353,17 +352,22 @@ def tile_list_damped_trade_exposure_kernel(
 
         for c in range(CHUNKS):
             add_turned(0, c, open_sum(0, c), ident)
-        wr_g = sb([P, N * PACK], BF16, "wr_g", "root3_0")
+        factor2 = wide_factor(2, fill_sizes(2, sb([P, S], F32, "sizes2", "root0_0a")), sb([P, S], F32, "roots2"), BANK)
+        scatter(2, damped_of(2, factor2, ["p4", "p5"], sb([P, S], F32, "damped2")), weight[2])
+        factor3 = wide_factor(3, fill_sizes(3, sb([P, S], F32, "sizes3", "page0")), sb([P, S], F32, "roots3"), S)
+        for c in range(CHUNKS):
+            add_turned(1, c, open_sum(1, c), ident)
+        wr_g = sb([P, N * PACK], BF16, "wr_g", "factor0_0")
         for b in range(N // P):
             nc.scalar.copy(
                 wr_g[:, half_cols(b)].rearrange("p (n i j) -> p n j i", i=4, j=PACK),
                 wr_raw[:, :, b * P : (b + 1) * P].rearrange("p j (n i) -> p n j i", i=4),
             )
-        wr_w = sb([P, N], U32, "wr_w")
+        damped3 = damped_of(3, factor3, ["p0", "p1"], sb([P, S], F32, "damped3", "wr_raw"))
+        wr_w = sb([P, N], U32, "wr_w", "factor3_0")
         wr_sc = sb([P, N], U8, "wr_sc")
         nc.vector.quantize_mx(out=wr_w[:].bitcast(FP8X4), scales=wr_sc[:], in_=wr_g[:])
-        for c in range(CHUNKS):
-            add_turned(1, c, open_sum(1, c), ident)
+        scatter(3, damped3, weight[3])
         sums2 = []
         for c in range(CHUNKS):
             sums2.append(open_sum(2, c))
@@ -377,7 +381,7 @@ def tile_list_damped_trade_exposure_kernel(
 
         out_rows = out.rearrange("(b p) t -> p b t", p=P)
         stage_tags = ["tab_w0", "page0", "hold0", "hold1"]
-        out_banks = ["p0", "p1", "s", "s", "s", "s", "p2", "p3"]
+        out_banks = ["p0", "p1", "p6", "p7", "p2", "p4", "p3", "p5"]
         results = [sb([P, N // P * BANK], F32, f"result{c}", tag=stage_tags[c]) for c in range(CHUNKS)]
         starts = [sum(STRIPS[:k]) for k in range(len(STRIPS))]
         woven = {}

@@ -174,11 +174,11 @@ def tile_list_damped_trade_exposure_kernel(
                 wa_raw[a, s][:].rearrange("p j (m e x) -> p e m j x", e=2, x=2 * RUN)[:, 0],
             )
 
-        grouped_late = sb([P, PASSES, 2, 2, BANK // 2], BF16, "wa_g_late")
+        grouped_late = [sb([P, 2, 2, BANK // 2], BF16, "wa_g_late0")]
 
-        def round_late_slices(a, s):
-            nc.scalar.copy(
-                grouped_late[:, a, :, s, :].rearrange("p i (m c j) -> p m j i c", c=RUN, j=PACK),
+        def round_late_slices(copy, a, s):
+            copy(
+                grouped_late[a][:, :, s, :].rearrange("p i (m c j) -> p m j i c", c=RUN, j=PACK),
                 wa_raw[a, s][:].rearrange("p j (m e i c) -> p e m j i c", e=2, i=2, c=RUN)[:, 1],
             )
 
@@ -250,25 +250,27 @@ def tile_list_damped_trade_exposure_kernel(
         wb_sc = deal(wb_sc_raw, "wb_sc", U16)
         grouped0 = [sb([P, BANK], BF16, "wa_g0_0"), shared.tile([P, BANK], BF16, name="wa_g0_1", align_bytes=64, offset=1024)]
         round_pair_slice(nc.scalar.copy, grouped0[0][:], 0, 0)
-        round_late_slices(0, 0)
+        round_late_slices(nc.scalar.copy, 0, 0)
         factor00 = factor_in_pieces(0, 0, "p0", "wa_raw0_0")
         sizes1 = sb([P, S], F32, "sizes1", "root0_0a")
         nc.scalar.activation(sizes1[:, half_cols(0)], stress(1, 0, "p1")[:], ACT.Abs)
         round_pair_slice(nc.vector.tensor_copy, grouped0[1][:], 1, 0)
         for a in range(PASSES):
             quantise_wa(0, grouped0[a][:], slice(a * P, (a + 1) * P))
+        grouped_late.append(placed([P, 2, 2, BANK // 2], BF16, "wa_g_late1", 1024))
+        round_late_slices(nc.vector.tensor_copy, 1, 0)
         scatter_half(0, 0, damped_half(0, 0, factor00, "p2"))
         clear_page("factor0_0")
 
-        round_late_slices(1, 0)
         grouped1 = sb([P, PASSES * BANK], BF16, "wa_g1", "root0_0b")
         for a in range(PASSES):
             round_pair_slice(nc.scalar.copy, grouped1[:, half_cols(a)], a, 1)
         factor01 = factor_in_pieces(0, 1, "p1", None)
-        wa_w[1] = sb([P, PASSES * P], U32, "wa_w1")
+        damped01 = damped_half(0, 1, factor01, "p0")
+        wa_w[1] = sb([P, PASSES * P], U32, "wa_w1", "root0_1b")
         wa_sc[1] = sb([P, PASSES * P], U8, "wa_sc1")
         quantise_wa(1, grouped1[:], slice(0, PASSES * P))
-        scatter_half(0, 1, damped_half(0, 1, factor01, "p0", "root0_0b"))
+        scatter_half(0, 1, damped01)
         clear_page("factor0_1")
 
         def squares(i, roots):
@@ -296,15 +298,16 @@ def tile_list_damped_trade_exposure_kernel(
             nc.vector.tensor_tensor(page[i][:].indirect(idx2[:]), damped[:], weights[:], ALU.mult)
 
         nc.scalar.activation(sizes1[:, half_cols(1)], stress(1, 1, "p1")[:], ACT.Abs)
-        round_late_slices(0, 1)
+        round_late_slices(nc.scalar.copy, 0, 1)
         roots1 = placed([P, S], F32, "roots1", 12288)
         nc.scalar.activation(roots1[:], sizes1[:], ACT.Abs_reciprocal_sqrt, bias=1.0)
-        round_late_slices(1, 1)
+        round_late_slices(nc.scalar.copy, 1, 1)
         factor1 = squares(1, roots1)
         damped1 = damped_of(1, factor1, ["p2", "p3"], placed([P, S], F32, "damped1", 12352 - 4096))
         wa_w[2] = sb([P, PASSES * 2 * P], U32, "wa_w2", "factor1_0")
         wa_sc[2] = sb([P, PASSES * 2 * P], U8, "wa_sc2")
-        quantise_wa(2, grouped_late[:].rearrange("p a i s x -> p (a i s x)"), slice(0, PASSES * 2 * P))
+        for a in range(PASSES):
+            quantise_wa(2, grouped_late[a][:].rearrange("p i s x -> p (i s x)"), slice(2 * a * P, 2 * (a + 1) * P))
         scatter(1, damped1, pair_weight)
         clear_page("factor1_1")
 
@@ -355,14 +358,13 @@ def tile_list_damped_trade_exposure_kernel(
         factor2 = wide_factor(2, fill_sizes(2, sb([P, S], F32, "sizes2", "root0_0a")), sb([P, S], F32, "roots2"), BANK)
         scatter(2, damped_of(2, factor2, ["p4", "p5"], sb([P, S], F32, "damped2")), weight[2])
         factor3 = wide_factor(3, fill_sizes(3, sb([P, S], F32, "sizes3", "page0")), sb([P, S], F32, "roots3"), S)
-        for c in range(CHUNKS):
-            add_turned(1, c, open_sum(1, c), ident)
-        wr_g = sb([P, N * PACK], BF16, "wr_g", "factor0_0")
+        wr_g = sb([P, N * PACK], BF16, "wr_g", "roots3")
         for b in range(N // P):
             nc.scalar.copy(
                 wr_g[:, half_cols(b)].rearrange("p (n i j) -> p n j i", i=4, j=PACK),
                 wr_raw[:, :, b * P : (b + 1) * P].rearrange("p j (n i) -> p n j i", i=4),
             )
+            add_turned(1, b, open_sum(1, b), ident)
         damped3 = damped_of(3, factor3, ["p0", "p1"], sb([P, S], F32, "damped3", "wr_raw"))
         wr_w = sb([P, N], U32, "wr_w", "factor3_0")
         wr_sc = sb([P, N], U8, "wr_sc")

@@ -84,10 +84,9 @@ def tile_list_damped_trade_exposure_kernel(
             nc.sync.dma_start(tile[:], rows.rearrange("(p j) c -> p j c", j=PACK))
             return tile
 
-        def load_pair_weight(h):
+        def load_pair_weight(h, rep):
             rows = wgs.rearrange("(m x) j -> m x j", x=GROUP)[:, : 2 * RUN, half_cols(h)]
-            for rep in range(2):
-                nc.sync.dma_start(pair_weight[rep * P // 2 : (rep + 1) * P // 2, half_cols(h)], rows)
+            nc.sync.dma_start(pair_weight[rep * P // 2 : (rep + 1) * P // 2, half_cols(h)], rows)
 
         def load_weight(i):
             tile = sb([P, S], F32, f"weight{i}")
@@ -125,12 +124,15 @@ def tile_list_damped_trade_exposure_kernel(
         nc.scalar.dma_start(lowered[: P - QUAD // 2, :].bitcast(I32), picked[QUAD // 2 :, :].bitcast(I32))
         v_sc = [picked, lowered]
         wb_sc_raw = load_scales(wb_scales, "wb_sc_raw")
-        wa_raw = {(a, 0): load_wa(a, 0) for a in range(PASSES)}
         pair_weight = sb([P, S], F32, "pair_weight")
-        wa_raw[0, 1] = load_wa(0, 1)
-        load_pair_weight(0)
-        wa_raw[1, 1] = load_wa(1, 1)
-        load_pair_weight(1)
+        wa_raw = {}
+        for a in range(PASSES):
+            wa_raw[a, 0] = load_wa(a, 0)
+            load_pair_weight(0, a)
+        for a in range(PASSES):
+            wa_raw[a, 1] = load_wa(a, 1)
+        for rep in range(2):
+            load_pair_weight(1, rep)
         held = [load_hold(0)]
         weight = {2: load_weight(2)}
         wr_raw = sb([P, PACK, N], F32, "wr_raw")
@@ -383,7 +385,7 @@ def tile_list_damped_trade_exposure_kernel(
 
         out_rows = out.rearrange("(b p) t -> p b t", p=P)
         stage_tags = ["tab_w0", "page0", "hold0", "hold1"]
-        out_banks = ["p0", "p1", "p6", "p7", "p2", "p4", "p3", "p5"]
+        out_banks = ["p5", "p3", "p0", "p1", "p6", "p7", "p2", "p4"]
         results = [sb([P, N // P * BANK], F32, f"result{c}", tag=stage_tags[c]) for c in range(CHUNKS)]
         starts = [sum(STRIPS[:k]) for k in range(len(STRIPS))]
         woven = {}
@@ -395,9 +397,10 @@ def tile_list_damped_trade_exposure_kernel(
             return pairs[c][:, :, at : at + STRIPS[k]]
 
         def add_last(k):
-            cols = slice(starts[k], starts[k] + STRIPS[k])
             halves = strip_words(k)[:, 1, :].bitcast(BF16).rearrange("p (t e) -> p t e", e=2)
-            nc.vector.tensor_tensor(halves[:, :, 1], page[3][:, cols], held[3][:, cols], ALU.add)
+            for at in range(0, STRIPS[k], STRIPS[0]):
+                cols = slice(starts[k] + at, starts[k] + at + STRIPS[0])
+                nc.vector.tensor_tensor(halves[:, at : at + STRIPS[0], 1], page[3][:, cols], held[3][:, cols], ALU.add)
 
         def weave(k):
             woven[k] = ring.tile([P, STRIPS[k], 2], F32, name="woven", align_bytes=64)

@@ -118,7 +118,7 @@ def tile_list_damped_trade_exposure_kernel(
             nc.sync.dma_start(tab_sc[r : P : QUAD // 2, :].bitcast(I32), tab_sc_rows[r])
         tab_w = [load_tab(a) for a in range(PASSES)]
         lowered = sb([P, S], U8, "lowered")
-        nc.vector.memset(lowered[:].bitcast(I32), 0)
+        nc.vector.memset(lowered[P - QUAD :, :].bitcast(I32), 0)
         picked = sb([P, S], U8, "picked")
         nc.vector.tensor_copy(picked[:], tab_sc[:].indirect(idx[:]))
         nc.scalar.dma_start(lowered[: P - QUAD // 2, :].bitcast(I32), picked[QUAD // 2 :, :].bitcast(I32))
@@ -190,15 +190,15 @@ def tile_list_damped_trade_exposure_kernel(
         def quantise_wa(g, grouped, cols):
             nc.vector.quantize_mx(out=wa_w[g][:, cols].bitcast(FP8X4), scales=wa_sc[g][:, cols], in_=grouped)
 
-        def product(tag, codes, scales, h):
-            acc = bank(tag)
+        def product(tag, codes, scales, h, cols=slice(0, BANK)):
+            acc = bank(tag)[:, : cols.stop - cols.start]
             for a in range(PASSES):
                 nc.tensor.matmul_mx(
-                    out=acc[:],
+                    out=acc,
                     lhsT=codes(a),
                     lhsT_scale=scales(a),
-                    rhs=v_w[a, h][:].bitcast(FP8X4),
-                    rhs_scale=v_sc[a][:, half_cols(h)],
+                    rhs=v_w[a, h][:, cols].bitcast(FP8X4),
+                    rhs_scale=v_sc[a][:, half_cols(h)][:, cols],
                     start=(a == 0),
                     stop=(a == PASSES - 1),
                 )
@@ -212,7 +212,7 @@ def tile_list_damped_trade_exposure_kernel(
                 h,
             )
 
-        def loadings(i, h, tag):
+        def loadings(i, h, tag, cols=slice(0, BANK)):
             g = min(i, 2)
             at = [a * P if i < 2 else (2 * a + i - 2) * P for a in range(PASSES)]
             return product(
@@ -220,9 +220,10 @@ def tile_list_damped_trade_exposure_kernel(
                 lambda a: wa_w[g][:, at[a] : at[a] + P].bitcast(FP8X4),
                 lambda a: wa_sc[g][:, at[a] : at[a] + P],
                 h,
+                cols,
             )
 
-        def factor_in_pieces(i, h, bank_tag, tag):
+        def factor_in_pieces(i, h, bank_tag, tag, between=None):
             pieces = [slice(e * BANK // 2, (e + 1) * BANK // 2) for e in range(2)]
             acc = stress(i, h, bank_tag)
             size = sb([P, BANK], F32, f"size{i}_{h}", tag)
@@ -232,8 +233,10 @@ def tile_list_damped_trade_exposure_kernel(
                 nc.scalar.activation(size[:, cols], acc[:, cols], ACT.Abs)
             for root, cols in zip(roots, pieces):
                 nc.scalar.activation(root[:], size[:, cols], ACT.Abs_reciprocal_sqrt, bias=1.0)
-            for root, cols in zip(roots, pieces):
-                nc.scalar.activation(factor[:, cols], root[:], ACT.Square)
+            nc.scalar.activation(factor[:, pieces[0]], roots[0][:], ACT.Square)
+            if between:
+                between()
+            nc.scalar.activation(factor[:, pieces[1]], roots[1][:], ACT.Square)
             return factor
 
         def damped_half(i, h, factor, bank_tag, tag=None):
@@ -261,17 +264,26 @@ def tile_list_damped_trade_exposure_kernel(
             quantise_wa(0, grouped0[a][:], slice(a * P, (a + 1) * P))
         grouped_late.append(placed([P, 2, 2, BANK // 2], BF16, "wa_g_late1", 1024))
         round_late_slices(nc.vector.tensor_copy, 1, 0)
-        scatter_half(0, 0, damped_half(0, 0, factor00, "p2"))
+        damped00 = sb([P, BANK], F32, "damped0_0")
+        for e in range(2):
+            cols = slice(e * BANK // 2, (e + 1) * BANK // 2)
+            nc.vector.tensor_tensor(damped00[:, cols], loadings(0, 0, f"p{2 + e}", cols), factor00[:, cols], ALU.mult)
+        scatter_half(0, 0, damped00)
         clear_page("factor0_0")
 
-        grouped1 = sb([P, PASSES * BANK], BF16, "wa_g1", "root0_0b")
-        for a in range(PASSES):
-            round_pair_slice(nc.scalar.copy, grouped1[:, half_cols(a)], a, 1)
-        factor01 = factor_in_pieces(0, 1, "p1", None)
+        grouped1 = [sb([P, BANK], BF16, "wa_g1_0", "root0_0b")]
+        round_pair_slice(nc.scalar.copy, grouped1[0][:], 0, 1)
+
+        def round_last_half():
+            grouped1.append(sb([P, BANK], BF16, "wa_g1_1", "root0_1a"))
+            round_pair_slice(nc.scalar.copy, grouped1[1][:], 1, 1)
+
+        factor01 = factor_in_pieces(0, 1, "p1", None, round_last_half)
         damped01 = damped_half(0, 1, factor01, "p0")
         wa_w[1] = sb([P, PASSES * P], U32, "wa_w1", "root0_1b")
         wa_sc[1] = sb([P, PASSES * P], U8, "wa_sc1")
-        quantise_wa(1, grouped1[:], slice(0, PASSES * P))
+        for a in range(PASSES):
+            quantise_wa(1, grouped1[a][:], slice(a * P, (a + 1) * P))
         scatter_half(0, 1, damped01)
         clear_page("factor0_1")
 

from contextlib import ExitStack

import concourse.mybir as mybir
from concourse.masks import make_identity

K, T, S, H, T2, N = 1024, 2048, 1024, 512, 2048, 512
FLOPS = 2 * (2 * K * H * S + H * N * T2)

F32 = mybir.dt.float32
BF16 = mybir.dt.bfloat16
I32 = mybir.dt.int32
U32 = mybir.dt.uint32
U16 = mybir.dt.uint16
U8 = mybir.dt.uint8
FP8X4 = mybir.dt.float8_e4m3fn_x4
FP4X4 = mybir.dt.float4_e2m1fn_x4
ACT = mybir.ActivationFunctionType
ALU = mybir.AluOpType

P = 128
PACK = 4
PASSES = K // (P * PACK)
BANK = 512
HALVES = S // BANK
CHUNKS = T2 // BANK
BLOCKS = BANK // P
QUAD = 32
RUN = 2
GROUP = PACK * RUN
STRIPS = (256, 256, 512, 512, 512)


def tile_list_damped_trade_exposure_kernel(
    tc, tab_words, tab_scales, offs, wa, wb_words, wb_scales, wgs, offs2, hold, wr, out
):
    nc = tc.nc
    with ExitStack() as ctx:
        keep = ctx.enter_context(tc.tile_pool(name="keep", bufs=1))
        ring = ctx.enter_context(tc.tile_pool(name="ring", bufs=2))
        shared = ctx.enter_context(tc.tile_pool(name="shared", bufs=1))
        psum = ctx.enter_context(tc.psum_pool(name="psum", bufs=1))

        def sb(shape, dtype, name, tag=None):
            return keep.tile(shape, dtype, name=name, tag=tag or name, align_bytes=64)

        def placed(shape, dtype, name, offset):
            return shared.tile(shape, dtype, name=name, align_bytes=64, offset=offset)

        def bank(tag):
            return psum.tile([P, BANK], F32, name=tag, tag=tag)

        def half_cols(h):
            return slice(h * BANK, (h + 1) * BANK)

        def half_list(lst, h):
            return lst[:, h * (BANK // 16) : (h + 1) * (BANK // 16)]

        idx = keep.tile([P, S // 16], U16, name="idx")
        nc.sync.dma_start(idx[:], offs)

        def load_scales(src, name):
            width = src.shape[2]
            tile = sb([P, PASSES * width], U8, name)
            nc.gpsimd.memset(tile[:].bitcast(I32), 0)
            rows = src.bitcast(I32).rearrange("a (q r) c -> r q a c", r=4)
            for r in range(4):
                nc.sync.dma_start(tile[r:P:QUAD, :].bitcast(I32).rearrange("q (a c) -> q a c", a=PASSES), rows[r])
            return tile

        def load_tab(a):
            if a == 0:
                tile = sb([P, T], U32, "tab_w0")
            else:
                tile = shared.tile([P, T], U32, name="tab_w1", align_bytes=64, offset=0)
            nc.sync.dma_start(tile[:].bitcast(I32), tab_words[a].rearrange("p t i -> p (t i)").bitcast(I32))
            return tile

        def load_wa(a, s):
            if (a, s) == (1, 1):
                tile = placed([P, PACK, H // 2], F32, "wa_raw1_1", 20480)
            else:
                tile = sb([P, PACK, H // 2], F32, f"wa_raw{a}_{s}")
            rows = wa[a * P * PACK : (a + 1) * P * PACK, s * H // 2 : (s + 1) * H // 2]
            nc.sync.dma_start(tile[:], rows.rearrange("(p j) c -> p j c", j=PACK))
            return tile

        def load_pair_weight(h, rep):
            rows = wgs.rearrange("(m x) j -> m x j", x=GROUP)[:, : 2 * RUN, half_cols(h)]
            nc.sync.dma_start(pair_weight[rep * P // 2 : (rep + 1) * P // 2, half_cols(h)], rows)

        def load_weight(i):
            tile = sb([P, S], F32, f"weight{i}")
            rows = wgs.rearrange("(m i c) j -> i m c j", i=PACK, c=RUN)[i]
            for q in range(4):
                nc.sync.dma_start(tile[QUAD * q : QUAD * (q + 1), :], rows)
            return tile

        def load_hold(i):
            tile = sb([P, T2], F32, f"hold{i}")
            if i < 2:
                rows = hold.rearrange("(s m x) t -> s m x t", s=2, x=GROUP)[i][:, : 2 * RUN, :]
            else:
                rows = hold.rearrange("(m i c) t -> i m c t", i=PACK, c=RUN)[i]
            nc.sync.dma_start(tile[:], rows)
            return tile

        idx2 = keep.tile([P, S // 16], U16, name="idx2")
        nc.sync.dma_start(idx2[:], offs2)
        wb_raw = sb([P, PASSES * 2 * H], U8, "wb_raw")
        nc.sync.dma_start(
            wb_raw[:].bitcast(I32).rearrange("p (a c) -> p a c", a=PASSES),
            wb_words.bitcast(I32).rearrange("a p c -> p a c"),
        )
        tab_sc = sb([P, T], U8, "tab_sc")
        nc.vector.memset(tab_sc[:].bitcast(I32), 0)
        tab_sc_rows = tab_scales.bitcast(I32).rearrange("a (q r) c -> r q a c", r=4)
        for r in range(4):
            nc.sync.dma_start(tab_sc[r : P : QUAD // 2, :].bitcast(I32), tab_sc_rows[r])
        tab_w = [load_tab(a) for a in range(PASSES)]
        lowered = sb([P, S], U8, "lowered")
        nc.vector.memset(lowered[P - QUAD :, :].bitcast(I32), 0)
        picked = sb([P, S], U8, "picked")
        nc.vector.tensor_copy(picked[:], tab_sc[:].indirect(idx[:]))
        nc.scalar.dma_start(lowered[: P - QUAD // 2, :].bitcast(I32), picked[QUAD // 2 :, :].bitcast(I32))
        v_sc = [picked, lowered]
        wb_sc_raw = load_scales(wb_scales, "wb_sc_raw")
        pair_weight = sb([P, S], F32, "pair_weight")
        wa_raw = {}
        for a in range(PASSES):
            wa_raw[a, 0] = load_wa(a, 0)
            load_pair_weight(0, a)
        for a in range(PASSES):
            wa_raw[a, 1] = load_wa(a, 1)
        for rep in range(2):
            load_pair_weight(1, rep)
        held = [load_hold(0)]
        weight = {2: load_weight(2)}
        wr_raw = sb([P, PACK, N], F32, "wr_raw")
        wr_rows = wr.rearrange("(m i c) n -> i m c n", i=PACK, c=RUN)
        for i in range(PACK):
            nc.sync.dma_start(wr_raw[:, i, :], wr_rows[i])
        held.extend(load_hold(i) for i in (1, 2))
        weight[3] = load_weight(3)
        held.append(load_hold(3))

        warm = sb([P, 2], F32, "warm")
        nc.gpsimd.memset(warm[:, 0:1], 1.0)
        nc.scalar.activation(warm[:, 1:2], warm[:, 0:1], ACT.Abs_reciprocal_sqrt)
        ident = sb([P, P], F32, "ident")
        make_identity(nc, ident[:])

        page = [sb([P, T2], F32, "page0")]
        nc.vector.memset(page[0][:], 0.0)

        v_w = {}

        def gather_words(a, h, tag=None):
            v_w[a, h] = sb([P, BANK], U32, f"v_w{a}_{h}", tag)
            nc.vector.tensor_copy(v_w[a, h][:], tab_w[a][:].indirect(half_list(idx, h)))

        def deal(raw, name, run_dtype):
            tile = sb([P, raw.shape[1]], U8, name)
            src = raw[:].bitcast(run_dtype).rearrange("p (a m e i) -> p e a m i", a=PASSES, e=2, i=2)
            dst = tile[:].bitcast(run_dtype).rearrange("p (a e x) -> p e a x", a=PASSES, e=2)
            nc.scalar.copy(dst[:, 0].rearrange("p a (m i) -> p a m i", i=2), src[:, 0])
            nc.scalar.copy(dst[:, 1].rearrange("p a (i m) -> p a m i", i=2), src[:, 1])
            return tile

        for a in range(PASSES):
            for h in range(HALVES):
                gather_words(a, h)

        def round_pair_slice(copy, grouped, a, s):
            copy(
                grouped.rearrange("p (m x j) -> p m j x", x=2 * RUN, j=PACK),
                wa_raw[a, s][:].rearrange("p j (m e x) -> p e m j x", e=2, x=2 * RUN)[:, 0],
            )

        grouped_late = [sb([P, 2, 2, BANK // 2], BF16, "wa_g_late0")]

        def round_late_slices(copy, a, s):
            copy(
                grouped_late[a][:, :, s, :].rearrange("p i (m c j) -> p m j i c", c=RUN, j=PACK),
                wa_raw[a, s][:].rearrange("p j (m e i c) -> p e m j i c", e=2, i=2, c=RUN)[:, 1],
            )

        wa_w = {0: shared.tile([P, PASSES * P], U32, name="wa_w0", align_bytes=64, offset=0)}
        wa_sc = {0: sb([P, PASSES * P], U8, "wa_sc0")}

        def quantise_wa(g, grouped, cols):
            nc.vector.quantize_mx(out=wa_w[g][:, cols].bitcast(FP8X4), scales=wa_sc[g][:, cols], in_=grouped)

        def product(tag, codes, scales, h, cols=slice(0, BANK)):
            acc = bank(tag)[:, : cols.stop - cols.start]
            for a in range(PASSES):
                nc.tensor.matmul_mx(
                    out=acc,
                    lhsT=codes(a),
                    lhsT_scale=scales(a),
                    rhs=v_w[a, h][:, cols].bitcast(FP8X4),
                    rhs_scale=v_sc[a][:, half_cols(h)][:, cols],
                    start=(a == 0),
                    stop=(a == PASSES - 1),
                )
            return acc

        def stress(i, h, tag):
            return product(
                tag,
                lambda a: wb_w[:, 2 * (a * PACK + i) * P : 2 * (a * PACK + i + 1) * P].bitcast(FP4X4),
                lambda a: wb_sc[:, (a * PACK + i) * P : (a * PACK + i + 1) * P],
                h,
            )

        def loadings(i, h, tag, cols=slice(0, BANK)):
            g = min(i, 2)
            at = [a * P if i < 2 else (2 * a + i - 2) * P for a in range(PASSES)]
            return product(
                tag,
                lambda a: wa_w[g][:, at[a] : at[a] + P].bitcast(FP8X4),
                lambda a: wa_sc[g][:, at[a] : at[a] + P],
                h,
                cols,
            )

        def factor_in_pieces(i, h, bank_tag, tag, between=None):
            pieces = [slice(e * BANK // 2, (e + 1) * BANK // 2) for e in range(2)]
            acc = stress(i, h, bank_tag)
            size = sb([P, BANK], F32, f"size{i}_{h}", tag)
            roots = [sb([P, BANK // 2], F32, f"root{i}_{h}{name}") for name in "ab"]
            factor = sb([P, BANK], F32, f"factor{i}_{h}")
            for cols in pieces:
                nc.scalar.activation(size[:, cols], acc[:, cols], ACT.Abs)
            for root, cols in zip(roots, pieces):
                nc.scalar.activation(root[:], size[:, cols], ACT.Abs_reciprocal_sqrt, bias=1.0)
            nc.scalar.activation(factor[:, pieces[0]], roots[0][:], ACT.Square)
            if between:
                between()
            nc.scalar.activation(factor[:, pieces[1]], roots[1][:], ACT.Square)
            return factor

        def damped_half(i, h, factor, bank_tag, tag=None):
            damped = sb([P, BANK], F32, f"damped{i}_{h}", tag)
            nc.vector.tensor_tensor(damped[:], loadings(i, h, bank_tag)[:], factor[:], ALU.mult)
            return damped

        def scatter_half(i, h, damped):
            nc.vector.tensor_tensor(page[i][:].indirect(half_list(idx2, h)), damped[:], pair_weight[:, half_cols(h)], ALU.mult)

        def clear_page(tag):
            page.append(sb([P, T2], F32, f"page{len(page)}", tag))
            nc.gpsimd.memset(page[-1][:], 0.0)

        wb_w = deal(wb_raw, "wb_w", U32)
        wb_sc = deal(wb_sc_raw, "wb_sc", U16)
        grouped0 = [sb([P, BANK], BF16, "wa_g0_0"), shared.tile([P, BANK], BF16, name="wa_g0_1", align_bytes=64, offset=1024)]
        round_pair_slice(nc.scalar.copy, grouped0[0][:], 0, 0)
        round_late_slices(nc.scalar.copy, 0, 0)
        factor00 = factor_in_pieces(0, 0, "p0", "wa_raw0_0")
        sizes1 = sb([P, S], F32, "sizes1", "root0_0a")
        nc.scalar.activation(sizes1[:, half_cols(0)], stress(1, 0, "p1")[:], ACT.Abs)
        round_pair_slice(nc.vector.tensor_copy, grouped0[1][:], 1, 0)
        for a in range(PASSES):
            quantise_wa(0, grouped0[a][:], slice(a * P, (a + 1) * P))
        grouped_late.append(placed([P, 2, 2, BANK // 2], BF16, "wa_g_late1", 1024))
        round_late_slices(nc.vector.tensor_copy, 1, 0)
        damped00 = sb([P, BANK], F32, "damped0_0")
        for e in range(2):
            cols = slice(e * BANK // 2, (e + 1) * BANK // 2)
            nc.vector.tensor_tensor(damped00[:, cols], loadings(0, 0, f"p{2 + e}", cols), factor00[:, cols], ALU.mult)
        scatter_half(0, 0, damped00)
        clear_page("factor0_0")

        grouped1 = [sb([P, BANK], BF16, "wa_g1_0", "root0_0b")]
        round_pair_slice(nc.scalar.copy, grouped1[0][:], 0, 1)

        def round_last_half():
            grouped1.append(sb([P, BANK], BF16, "wa_g1_1", "root0_1a"))
            round_pair_slice(nc.scalar.copy, grouped1[1][:], 1, 1)

        factor01 = factor_in_pieces(0, 1, "p1", None, round_last_half)
        damped01 = damped_half(0, 1, factor01, "p0")
        wa_w[1] = sb([P, PASSES * P], U32, "wa_w1", "root0_1b")
        wa_sc[1] = sb([P, PASSES * P], U8, "wa_sc1")
        for a in range(PASSES):
            quantise_wa(1, grouped1[a][:], slice(a * P, (a + 1) * P))
        scatter_half(0, 1, damped01)
        clear_page("factor0_1")

        def squares(i, roots):
            factors = [sb([P, BANK], F32, f"factor{i}_{h}") for h in range(HALVES)]
            for h in range(HALVES):
                nc.scalar.activation(factors[h][:], roots[:, half_cols(h)], ACT.Square)
            return factors

        def wide_factor(i, sizes, roots, width):
            for at in range(0, S, width):
                nc.scalar.activation(roots[:, at : at + width], sizes[:, at : at + width], ACT.Abs_reciprocal_sqrt, bias=1.0)
            return squares(i, roots)

        def fill_sizes(i, sizes):
            for h in range(HALVES):
                nc.scalar.activation(sizes[:, half_cols(h)], stress(i, h, f"p{h}")[:], ACT.Abs)
            return sizes

        def damped_of(i, factor, banks, damped):
            for h in range(HALVES):
                nc.vector.tensor_tensor(damped[:, half_cols(h)], loadings(i, h, banks[h])[:], factor[h][:], ALU.mult)
            return damped

        def scatter(i, damped, weights):
            nc.vector.tensor_tensor(page[i][:].indirect(idx2[:]), damped[:], weights[:], ALU.mult)

        nc.scalar.activation(sizes1[:, half_cols(1)], stress(1, 1, "p1")[:], ACT.Abs)
        round_late_slices(nc.scalar.copy, 0, 1)
        roots1 = placed([P, S], F32, "roots1", 12288)
        nc.scalar.activation(roots1[:], sizes1[:], ACT.Abs_reciprocal_sqrt, bias=1.0)
        round_late_slices(nc.scalar.copy, 1, 1)
        factor1 = squares(1, roots1)
        damped1 = damped_of(1, factor1, ["p2", "p3"], placed([P, S], F32, "damped1", 12352 - 4096))
        wa_w[2] = sb([P, PASSES * 2 * P], U32, "wa_w2", "factor1_0")
        wa_sc[2] = sb([P, PASSES * 2 * P], U8, "wa_sc2")
        for a in range(PASSES):
            quantise_wa(2, grouped_late[a][:].rearrange("p i s x -> p (i s x)"), slice(2 * a * P, 2 * (a + 1) * P))
        scatter(1, damped1, pair_weight)
        clear_page("factor1_1")

        turned_at = [12352, 16320, 20480, 22528]
        turned = [placed([P, BLOCKS, 2, P], BF16, f"turned{c}", turned_at[c]) for c in range(CHUNKS)]
        pairs = [sb([P, 2, BANK], F32, f"pairs{c}", ["wa_raw0_0", "wa_raw0_1", "wa_raw1_0", "wa_raw1_1"][c]) for c in range(CHUNKS)]

        def turn_into(acc, src, c, identity, opens):
            for bl in range(BLOCKS):
                cols = slice(c * BANK + bl * P, c * BANK + (bl + 1) * P)
                nc.tensor.matmul(
                    acc[:, bl * P : (bl + 1) * P],
                    src[:, cols],
                    identity[:],
                    start=opens and bl == 0,
                    stop=not opens and bl == BLOCKS - 1,
                    is_transpose=True,
                )

        def open_sum(i, c):
            acc = bank(["p4", "p5", "p6", "p7"][c] if i == 0 else ["p6", "p7", "p2", "p4"][c])
            turn_into(acc, held[i], c, ident, True)
            return acc

        def add_turned(i, c, acc, identity):
            turn_into(acc, page[i], c, identity, False)
            if i < 2:
                nc.scalar.copy(
                    turned[c][:, :, i, :].rearrange("t b (m c e) -> t b m c e", c=RUN, e=2),
                    acc[:].rearrange("t (b m e c) -> t b m c e", b=BLOCKS, e=2, c=RUN),
                )
            else:
                nc.scalar.copy(
                    turned[c][:].rearrange("t b s (x e) -> t b s x e", e=2)[:, :, :, :, 0],
                    acc[:].rearrange("t (b s x) -> t b s x", b=BLOCKS, s=2),
                )

        def turn_back(u, c):
            acc = bank(["p3", "p5"][c % 2])
            words = turned[c][:].rearrange("t b s x -> t (b s x)").bitcast(F32)
            for bl in range(BLOCKS):
                cols = slice(bl * P, (bl + 1) * P)
                nc.tensor.transpose(acc[:, cols], words[:, cols], ident[:])
            nc.scalar.copy(pairs[c][:, u, :], acc[:])

        for c in range(CHUNKS):
            add_turned(0, c, open_sum(0, c), ident)
        factor2 = wide_factor(2, fill_sizes(2, sb([P, S], F32, "sizes2", "root0_0a")), sb([P, S], F32, "roots2"), BANK)
        scatter(2, damped_of(2, factor2, ["p4", "p5"], sb([P, S], F32, "damped2")), weight[2])
        factor3 = wide_factor(3, fill_sizes(3, sb([P, S], F32, "sizes3", "page0")), sb([P, S], F32, "roots3"), S)
        wr_g = sb([P, N * PACK], BF16, "wr_g", "roots3")
        for b in range(N // P):
            nc.scalar.copy(
                wr_g[:, half_cols(b)].rearrange("p (n i j) -> p n j i", i=4, j=PACK),
                wr_raw[:, :, b * P : (b + 1) * P].rearrange("p j (n i) -> p n j i", i=4),
            )
            add_turned(1, b, open_sum(1, b), ident)
        damped3 = damped_of(3, factor3, ["p0", "p1"], sb([P, S], F32, "damped3", "wr_raw"))
        wr_w = sb([P, N], U32, "wr_w", "factor3_0")
        wr_sc = sb([P, N], U8, "wr_sc")
        nc.vector.quantize_mx(out=wr_w[:].bitcast(FP8X4), scales=wr_sc[:], in_=wr_g[:])
        scatter(3, damped3, weight[3])
        sums2 = []
        for c in range(CHUNKS):
            sums2.append(open_sum(2, c))
            turn_back(0, c)
        late_ident = sb([P, P], F32, "late_ident", "hold2")
        nc.scalar.copy(late_ident[:], ident[:])
        for c in range(CHUNKS):
            add_turned(2, c, sums2[c], late_ident)
        for c in range(CHUNKS):
            turn_back(1, c)

        out_rows = out.rearrange("(b p) t -> p b t", p=P)
        stage_tags = ["tab_w0", "page0", "hold0", "hold1"]
        out_banks = ["p5", "p3", "p0", "p1", "p6", "p7", "p2", "p4"]
        results = [sb([P, N // P * BANK], F32, f"result{c}", tag=stage_tags[c]) for c in range(CHUNKS)]
        starts = [sum(STRIPS[:k]) for k in range(len(STRIPS))]
        woven = {}
        stored = []
        left_to_vector = []

        def strip_words(k):
            c, at = divmod(starts[k], BANK)
            return pairs[c][:, :, at : at + STRIPS[k]]

        def add_last(k):
            halves = strip_words(k)[:, 1, :].bitcast(BF16).rearrange("p (t e) -> p t e", e=2)
            for at in range(0, STRIPS[k], STRIPS[0]):
                cols = slice(starts[k] + at, starts[k] + at + STRIPS[0])
                nc.vector.tensor_tensor(halves[:, at : at + STRIPS[0], 1], page[3][:, cols], held[3][:, cols], ALU.add)

        def weave(k):
            woven[k] = ring.tile([P, STRIPS[k], 2], F32, name="woven", align_bytes=64)
            nc.vector.tensor_copy(woven[k][:], strip_words(k).rearrange("p u t -> p t u"))

        def expose(k):
            width = STRIPS[k]
            cols = slice(starts[k], starts[k] + width)
            z_w = sb([P, width], U32, f"z_w{k}")
            z_sc = sb([P, width], U8, f"z_sc{k}")
            nc.vector.quantize_mx(
                out=z_w[:].bitcast(FP8X4),
                scales=z_sc[:],
                in_=woven[k][:].rearrange("p t u -> p (t u)").bitcast(BF16),
            )
            per_bank = 1 if k == 0 else BANK // width
            for first in range(0, N // P, per_bank):
                acc = bank(out_banks[len(stored) % len(out_banks)])
                for b in range(first, first + per_bank):
                    rows = slice(b * P, (b + 1) * P)
                    nc.tensor.matmul_mx(
                        out=acc[:, (b - first) * width : (b - first + 1) * width],
                        lhsT=wr_w[:, rows].bitcast(FP8X4),
                        lhsT_scale=wr_sc[:, rows],
                        rhs=z_w[:].bitcast(FP8X4),
                        rhs_scale=z_sc[:],
                        start=True,
                        stop=True,
                    )
                c, at = divmod(starts[k] * (N // P) + first * width, N // P * BANK)
                sums = acc[:, : per_bank * width]
                result = results[c][:, at : at + per_bank * width]
                dst = out_rows[:, first : first + per_bank, cols]
                if k == len(STRIPS) - 1 and first + per_bank == N // P:
                    left_to_vector.append((dst, result, sums))
                else:
                    nc.scalar.activation(result, sums, ACT.Abs)
                    nc.sync.dma_start(dst, result.rearrange("p (b t) -> p b t", b=per_bank))
                stored.append(result)

        add_last(0)
        add_last(1)
        weave(0)
        weave(1)
        expose(0)
        add_last(2)
        expose(1)
        for k in range(2, len(STRIPS)):
            weave(k)
            expose(k)
            if k + 1 < len(STRIPS):
                add_last(k + 1)
        negated = [sb([P, BANK], F32, f"negated{n}") for n in range(len(left_to_vector))]
        for (dst, result, sums), minus in zip(left_to_vector, negated):
            nc.vector.tensor_scalar(minus[:], sums, -1.0, None, ALU.mult)
        for (dst, result, sums), minus in zip(left_to_vector, negated):
            nc.vector.tensor_tensor(result, sums, minus[:], ALU.max)
            nc.sync.dma_start(dst, result.rearrange("p (b t) -> p b t", b=dst.shape[1]))
